import numpy as np, ml_dtypes
CORES = [35,38,43,46]
N = 4
BF = ml_dtypes.bfloat16
B, W, CAP, RO = 1024, 8192, 64, 4
L = N * CAP
def parts(rng):
    share = rng.choice(np.array([0.1, 0.2, 0.4, 0.6]), (N, 8, 1, B))
    v = np.where(rng.random((N, 8, 16, B)) < share, -rng.integers(1, 256, (N, 8, 16, B)), rng.integers(0, 256, (N, 8, 16, B)))
    a = rng.integers(0, 256, (N, 8, 16, W)) * (rng.random((N, 8, 16, W)) < rng.choice(np.array([0.3, 0.6, 0.9]), (N, 8, 1, W))); a[..., W - 1] = 0
    u = rng.integers(0, W - 1, (N, 8, 16, B))
    u = np.where(rng.random(u.shape) < rng.choice(np.array([0.0, 0.0, 0.1, 0.1, 0.4, 0.96]), (N, 8, 1, B)), W - 1, u)
    to = np.where(rng.random((N, 8, W)) < rng.choice(np.array([0.0, 0.1, 0.25]), (N, 8, 1)), rng.integers(0, N, (N, 8, 1)), rng.integers(0, N, (N, 8, W)))
    pay = to * B + rng.integers(0, B, (N, 8, W))
    wk = np.where(rng.random((N, 8, L)) < 0.04, B, rng.integers(0, B, (N, 8, L)))
    return v, a, u, pay, wk
def pack(v, a, u, pay, wk):
    return {"vp": np.ascontiguousarray(v.reshape(N, 128, B)).astype(np.float32).astype(BF), "am": np.ascontiguousarray(a.reshape(N, 128, W)).astype(np.float32).astype(BF),
            "qu": np.ascontiguousarray(u.reshape(N, 128, B)).astype(np.int32), "pay": np.ascontiguousarray(pay).astype(np.int32), "wk": np.ascontiguousarray(wk).astype(np.int32)}
def setup_inputs(rng):
    return pack(*parts(rng))
def plant(rng, v, a, u, pay, wk, q, g, to):
    m = len(to); lanes = rng.permutation(L)[:m]; banks = rng.permutation(B)[:m]; lines = rng.permutation(W - 1)[:m]
    row = rng.integers(0, 16, m); j = rng.integers(0, 16, m)
    u[q, g][:, banks] = W - 1; u[q, g][row, banks] = lines
    v[q, g][j, banks] = -rng.integers(1, 256, m); a[q, g][j, lines] = 255
    order = np.argsort(lanes); pay[q, g][lines[order]] = to
    wk[q, g] = B; wk[q, g][lanes] = banks
def setup_inputs_room(rng):
    v, a, u, pay, wk = parts(rng)
    for q in range(N):
        for g in range(8):
            cnt = [CAP, CAP + 1, CAP - 1, 0, 1, 0, 2, CAP // 2][:N]
            if (q + g) % 4 == 3: cnt = [L] + [0] * (N - 1)
            to = np.concatenate([np.full(n, (q + 1 + g + j) % N, np.int64) for j, n in enumerate(cnt)])
            plant(rng, v, a, u, pay, wk, q, g, rng.permutation(to) * B + rng.integers(0, B, len(to)))
    return pack(v, a, u, pay, wk)
def setup_inputs_ties(rng):
    v, a, u, pay, wk = parts(rng)
    v[:, ::2] = rng.integers(-3, 3, (N, 4, 16, B)); a[:, ::2] = rng.integers(0, 4, (N, 4, 16, W))
    v[:, 1::2] = rng.integers(-3, 2, (N, 4, 16, B)) * 85; a[:, 1::2] = rng.integers(0, 4, (N, 4, 16, W)) * 85
    a = a * (rng.random((N, 8, 1, W)) < 0.6); a[..., W - 1] = 0
    u[:, :, 15] = np.where(rng.random((N, 8, B)) < 0.4, W - 1, u[:, :, 15])
    return pack(v, a, u, pay, wk)
def setup_inputs_alike(rng):
    v, a, u, pay, wk = parts(rng)
    wk[:, 0] = rng.choice(np.array([0, B - 1, 5, B // 2]), (N, L))
    u[:, 2] = rng.choice(np.array([0, W - 2, 7, W // 2, W - 1]), (N, 16, B))
    pay[:, 4] = rng.integers(0, N, (N, W)) * B + rng.choice(np.array([0, B - 1]), (N, W))
    u[:, 6] = np.repeat(u[:, 6, :1], 16, axis=1)
    wk[:, 1::2, L - 1] = wk[:, 1::2, 0]
    return pack(v, a, u, pay, wk)
def setup_inputs_dry(rng):
    v, a, u, pay, wk = parts(rng); o = rng.permutation(8)
    wk[:, o[0]] = B; a[:, o[1]] = 0; u[:, o[2]] = W - 1; v[:, o[3]] = np.abs(v[:, o[3]])
    v[:, o[4]] = -255; a[:, o[4]] = 255; a[..., W - 1] = 0
    wk[rng.integers(0, N), o[5]] = B
    h = int(o[6]); wk[:, h] = B
    for q in range(N):
        b = int(rng.integers(1, B)); n, m = [int(i) for i in rng.permutation(W - 1)[:2]]
        wk[q, h, int(rng.integers(0, L))] = b
        v[q, h, :, b] = -rng.integers(1, 256, 16); u[q, h, :, b] = n; a[q, h, :, n] = 0; pay[q, h, n] = (q + 1) % N * B
        v[q, h, :, 0] = -rng.integers(1, 256, 16); u[q, h, :, 0] = m; a[q, h, :, m] = 255; pay[q, h, m] = rng.integers(0, N) * B + rng.integers(1, B)
    return pack(v, a, u, pay, wk)
def setup_inputs_spread(rng):
    v, a, u, pay, wk = parts(rng)
    v = (np.exp2(8 * rng.random((N, 8, 1, B))) * rng.random((N, 8, 16, B))).astype(np.int64) * np.where(rng.random((N, 8, 16, B)) < 0.4, -1, 1)
    a = (np.exp2(8 * rng.random((N, 8, 1, W))) * rng.random((N, 8, 16, W))).astype(np.int64); a[..., W - 1] = 0
    u = np.where(u == W - 1, u, ((W - 1) * rng.random(u.shape) ** 2).astype(np.int64))
    pay = pay // B * B + (B * rng.random(pay.shape) ** 2).astype(np.int64)
    wk = np.where(wk == B, B, (B * rng.random(wk.shape) ** 2).astype(np.int64))
    return pack(v, a, u, pay, wk)
def check_inputs(d):
    bad = []
    for k, lo, hi in (("vp", -255, 255), ("am", 0, 255)):
        x = np.asarray(d[k]).astype(np.float32)
        if not np.all((x >= lo) & (x <= hi)): bad.append("range of " + k)
        elif not np.all(x == np.rint(x)): bad.append("whole numbers in " + k)
    if not np.all(np.asarray(d["am"]).astype(np.float32)[..., W - 1] == 0): bad.append("zeros in the last column of am")
    for k, hi in (("qu", W - 1), ("pay", N * B - 1), ("wk", B)):
        if np.min(d[k]) < 0 or np.max(d[k]) > hi: bad.append("range of " + k)
    return bad
def reference(vp, am, qu, pay, wk):
    v = vp.astype(np.float32).astype(np.int64).reshape(N, 8, 16, B); a = am.astype(np.float32).astype(np.int64).reshape(N, 8, 16, W)
    u = qu.astype(np.int64).reshape(N, 8, 16, B); payee = pay.astype(np.int64)
    w = wk.astype(np.int64); c = np.zeros((N, 8, 16, L), np.int64)
    for rnd in range(RO):
        w2 = np.full((N, 8, L), B, np.int64); c2 = np.zeros((N, 8, 16, L), np.int64)
        for q in range(N):
            for g in range(8):
                vv, aa, uu = v[q, g], a[q, g], u[q, g]
                lane = np.nonzero(w[q, g] < B)[0]
                lane = lane[np.sort(np.unique(w[q, g][lane], return_index=True)[1])]
                b = w[q, g][lane]
                x = np.maximum(vv[:, b] - c[q, g][:, lane], -255); vv[:, b] = x
                keep = np.any(x < 0, axis=0); b, x = b[keep], x[:, keep]
                n = uu[:, b]
                score = np.sum(x[:, None, :] + aa[:, n] >= 0, axis=0)
                best = 15 - np.argmax(score[::-1], axis=0)
                p = n[best, np.arange(len(b))]
                keep = p != W - 1; b, x, best, p = b[keep], x[:, keep], best[keep], p[keep]
                keep = np.sort(np.unique(p, return_index=True)[1]); b, x, best, p = b[keep], x[:, keep], best[keep], p[keep]
                t = np.minimum(aa[:, p], np.maximum(-x, 0))
                vv[:, b] = x + t; aa[:, p] = aa[:, p] - t; uu[best, b] = W - 1
                to = payee[q, g][p]
                for r in range(N):
                    k = np.nonzero(to // B == r)[0][:CAP]; s = q * CAP + np.arange(len(k))
                    w2[r, g][s] = to[k] % B; c2[r, g][:, s] = t[:, k]
        w, c = w2, c2
    return {"yv": v.reshape(N, 128, B).astype(np.float32).astype(BF), "yw": w.astype(np.float32), "yc": c.reshape(N, 128, L).astype(np.float32).astype(BF)}

@@ -1,0 +1,451 @@
+from concourse.bass import DstId, RemoteDMATransfer
+from concourse.mybir import AluOpType as OP, ActivationFunctionType as AF
+
+STEPS, B, NONE = 4, 1024, 8191
+VW, AW, DUMA = 1536, 8464, 8208
+BIG = 65536.0
+SCRATCH = {}
+
+
+def _buf(dtype, n, names, parts=128):
+    for b in names.split():
+        SCRATCH[b] = ("sbuf", [parts, n], dtype)
+
+
+_buf("bfloat16", VW, "NV")
+_buf("float32", VW, "Q")
+_buf("bfloat16", B, "Vin")
+_buf("int32", B, "Qin")
+_buf("bfloat16", AW, "A")
+_buf("bfloat16", 8192, "PT")
+_buf("int32", 512, "payS payH payL")
+_buf("float32", 512, "payF payA")
+_buf("bfloat16", 3072, "payB")
+_buf("int32", 256, "wkI", 8)
+_buf("float32", 256, "wkE", 8)
+_buf("float16", 256, "wkH", 8)
+_buf("float16", 128, "sel8", 8)
+_buf("bfloat16", 128, "sel8b", 8)
+_buf("bfloat16", 256, "o8", 8)
+_buf("float32", 128, "imp qg BLKf")
+_buf("float32", 256, "tt lane gmA SC SP SS nF np qa aS")
+_buf("int32", 8, "pc pj pg pb")
+_buf("float32", 32, "cf")
+_buf("float32", 16, "l16 LC LC2 Wf wa pWf pa")
+_buf("uint16", 16, "WL wU pL sL pU")
+_buf("float32", 8, "g8")
+_buf("float32", 64, "khi klo")
+_buf("bfloat16", 64, "tmp")
+_buf("float16", 128, "I16 NI16 ONEh BLKh")
+_buf("bfloat16", 128, "Ib BLKb B512 NB512 BLK4n BLK4k DG WBm irow MONE C16 RMx HALF ZERO BIGW")
+_buf("bfloat16", 8, "SB8")
+_buf("bfloat16", 1024, "WT")
+_buf("bfloat16", 256, "gmB gmC GM GM2 ONEb thr SD y nx mm D1 D2 PG Ap t ta OA c0")
+_buf("float16", 256, "rowl KM Z")
+_buf("float16", 16, "SR")
+_buf("uint16", 256, "nU bR pR")
+_buf("bfloat16", 4096, "eq G cmp")
+for _s in range(STEPS):
+    _buf("bfloat16", 1280, "WB%d WC%d" % (_s, _s))
+    _buf("bfloat16", 256, "LB%d LD%d" % (_s + 1, _s + 1))
+PSUM = ["k%d" % s for s in range(8)]
+for _s in PSUM:
+    SCRATCH[_s] = ("psum", [128, 512], "float32")
+SEMAPHORES = ["sv", "ss", "st", "sg", "lb", "lc"] + ["rb%d" % s for s in range(STEPS)] + ["rc%d" % s for s in range(STEPS)] + ["d%d" % k for k in range(30)]
+
+
+def split_engines(topo, cores, src):
+    dst = [c for c in cores if c != src]
+    off = [c for c in dst if topo.chip(c) != topo.chip(src)]
+    on = [c for c in dst if topo.chip(c) == topo.chip(src)]
+    out, used = {}, []
+    for group in (off, on):
+        if not group:
+            continue
+        free = [e for e in topo.engines(src, group[0]) if e not in used]
+        n = 1
+        while 2 * n * len(group) <= len(free):
+            n *= 2
+        for k, c in enumerate(group):
+            out[c] = free[k * n:(k + 1) * n]
+            used = used + out[c]
+    return out
+
+
+def rank_program(g, core, T, topo):
+    q = T.rank_of(core)
+    if q is None:
+        return
+    cores = list(T.cores)
+    queue = {"v": g.vector, "s": g.scalar, "t": g.tensor, "g": g, "y": g.sync}
+    semof = {"v": "sv", "s": "ss", "t": "st", "g": "sg"}
+    cnt = {"sv": 0, "ss": 0, "st": 0, "sg": 0}
+    know = {e: {} for e in queue}
+    snap, lastw, readers, total = {}, {}, {}, {}
+    ndma = [0]
+
+    def need_wait(e, sem, val):
+        if know[e].get(sem, 0) >= val:
+            return
+        queue[e].wait_ge(T.sem[sem], val)
+        for s2, v2 in snap.get((sem, val), {}).items():
+            know[e][s2] = max(know[e].get(s2, 0), v2)
+        know[e][sem] = max(know[e].get(sem, 0), val)
+
+    def waits(e, R, W, X=()):
+        need = {}
+        for b in R:
+            if b in lastw:
+                s, v = lastw[b]
+                need[s] = max(need.get(s, 0), v)
+        for b in list(W) + list(X):
+            deps = list(readers.get(b, {}).items())
+            if b in lastw:
+                deps.append(lastw[b])
+            for s, v in deps:
+                if s != semof.get(e) or (e != "t" and b in W):
+                    need[s] = max(need.get(s, 0), v)
+        for s in sorted(need):
+            need_wait(e, s, need[s])
+
+    def note(sem, val, R, W, e):
+        sn = dict(know[e])
+        sn[sem] = val
+        snap[(sem, val)] = sn
+        total[sem] = val
+        for b in R:
+            readers.setdefault(b, {})[sem] = val
+        for b in W:
+            lastw[b] = (sem, val)
+            readers[b] = {}
+
+    def op(e, name, R, W, *a, **k):
+        waits(e, R, W, [b for b in R if b in PSUM and b not in W])
+        eng = queue[e]
+        call = {"tc": lambda: eng.tensor_copy(*a), "tt": lambda: eng.tensor_tensor(*a), "ts": lambda: eng.tensor_scalar(*a),
+                "scan": lambda: eng.tensor_tensor_scan(*a), "ms": lambda: eng.memset(*a), "act": lambda: eng.activation(*a, **k),
+                "mm": lambda: eng.matmul(*a), "iota": lambda: eng.iota(*a, **k)}[name]
+        sem = semof[e]
+        cnt[sem] += 1
+        call().then_inc(T.sem[sem], 1)
+        note(sem, cnt[sem], R, W, e)
+
+    def dma(e, R, W, out, in_):
+        waits(e, R, W)
+        sem = "d%d" % ndma[0]
+        ndma[0] += 1
+        queue[e].dma_start(out, in_).then_inc(T.sem[sem], 16)
+        note(sem, 16, R, W, e)
+
+    def v(name, R, W, *a):
+        op("v", name, R, W, *a)
+
+    def ts(R, W, out, in_, *a):
+        v("ts", R, [W], out, in_, *a)
+
+    def act(R, W, out, in_, func=AF.Copy, **k):
+        op("s", "act", R, W, out, in_, func, **k)
+
+    def mm(R, W, out, lhsT, rhs, start=True, stop=True):
+        op("t", "mm", R, W, out, lhsT, rhs, start, stop)
+
+    dma("y", [], ["wkI"], T.wkI[:], T.wk[:])
+    dma("y", [], ["payS"], T.payS[:], T.pay[:])
+    dma("y", [], ["Qin"], T.Qin[:], T.qu[:])
+    dma("y", [], ["Vin"], T.Vin[:], T.vp[:])
+    dma("y", [], ["Am"], T.A[:, 0:8192], T.am[:])
+
+    def iota(buf, out, pattern, base, cm):
+        op("g", "iota", [], [buf], out, pattern, base, cm, allow_small_or_imprecise_dtypes=True)
+    iota("pc", T.pc[:, 0:1], [[1, 1]], 0, 1)
+    iota("qg", T.qg[:], [[1, 8], [0, 16]], 0, 0)
+    iota("khi", T.khi[:], [[1, 2], [0, 32]], 32 + 2 * q, 0)
+    iota("klo", T.klo[:], [[0, 2], [1, 32]], 0, 0)
+    iota("tt", T.tt[:], [[0, 16], [1, 16]], 0, 0)
+    iota("imp", T.imp[:], [[1, 128]], 0, -1)
+    iota("g8", T.g8[:], [[1, 8]], 0, 0)
+    iota("lane", T.lane[:], [[1, 256]], 0, 0)
+    iota("l16", T.l16[:], [[16, 16]], 0, 0)
+
+    col = {}
+
+    def c(name):
+        return T.cf[:, col[name]:col[name] + 1]
+
+    def colop(name, R, call, *a):
+        col[name] = len(col)
+        v(call, R, [name], c(name), *a)
+    v("ms", [], ["ZERO"], T.ZERO[:], 0.0)
+    v("ms", [], ["NVp"], T.NV[:, B:VW], 0.0)
+    v("ms", [], ["Qp"], T.Q[:, B:VW], float(NONE))
+    v("ms", [], ["Apd"], T.A[:, 8192:AW], 0.0)
+    v("ms", [], ["c0"], T.c0[:], 0.0)
+    v("ms", [], ["ONEb"], T.ONEb[:], 1.0)
+    v("ms", [], ["MONE"], T.MONE[:], -1.0)
+    v("ms", [], ["HALF"], T.HALF[:], 0.5)
+    v("ms", [], ["C16"], T.C16[:], 16384.0)
+    ts(["pc"], "pj", T.pj[:, 0:1], T.pc[:, 0:1], 15, None, OP.bitwise_and)
+    ts(["pc"], "pg", T.pg[:, 0:1], T.pc[:, 0:1], 4, None, OP.arith_shift_right)
+    colop("jf", ["pj"], "tc", T.pj[:, 0:1])
+    colop("gf", ["pg"], "tc", T.pg[:, 0:1])
+    colop("pf", ["pc"], "tc", T.pc[:, 0:1])
+    colop("ja", ["jf"], "ts", c("jf"), 4.0, None, OP.is_equal)
+    colop("jb", ["jf"], "ts", c("jf"), 5.0, None, OP.is_equal)
+    ts(["khi", "ja"], "khi", T.khi[:], T.khi[:], c("ja"), None, OP.mult)
+    ts(["klo", "jb"], "klo", T.klo[:], T.klo[:], c("jb"), None, OP.mult)
+    v("tt", ["khi", "klo"], ["tmp"], T.tmp[:], T.khi[:], T.klo[:], OP.add)
+    pf8 = T.cf[0:8, col["pf"]:col["pf"] + 1]
+    ts(["qg", "pf"], "sel8", T.sel8[:], T.qg[0:8, :], pf8, None, OP.is_equal)
+    ts(["qg", "pf"], "sel8b", T.sel8b[:], T.qg[0:8, :], pf8, None, OP.is_equal)
+    colop("corr", ["jf"], "ts", c("jf"), 15.0, BIG, OP.is_lt, OP.mult)
+    ts(["tt", "jf"], "gmA", T.gmA[:], T.tt[:], c("jf"), None, OP.subtract)
+    ts(["gmA"], "gmB", T.gmB[:], T.gmA[:], 0.0, -4.0 * BIG, OP.is_le, OP.mult)
+    ts(["gmA"], "gmC", T.gmC[:], T.gmA[:], 1.0, BIG, OP.is_equal, OP.mult)
+    v("tt", ["gmB", "gmC"], ["GM"], T.GM[:], T.gmB[:], T.gmC[:], OP.add)
+    for s in range(STEPS):
+        for r in range(4):
+            act(["tmp"], ["WB%d" % s], T["WB%d" % s][:, r * 256:r * 256 + 64], T.tmp[:])
+            act(["ZERO"], ["WC%d" % s], T["WC%d" % s][:, r * 256:r * 256 + 64], T.ZERO[:, 0:64])
+    ts(["wkI"], "wkE", T.wkE[:], T.wkI[:], float(B), None, OP.is_ge)
+    v("tt", ["wkE", "lane"], ["wkE"], T.wkE[:], T.wkE[:], T.lane[0:8, :], OP.mult)
+    v("tt", ["wkI", "wkE"], ["wkH"], T.wkH[:], T.wkI[:], T.wkE[:], OP.add)
+    ts(["imp"], "Ib", T.Ib[:], T.imp[:], 0.0, None, OP.is_equal)
+    ts(["qg", "gf"], "BLKb", T.BLKb[:], T.qg[:], c("gf"), None, OP.is_equal)
+    colop("j4", ["jf"], "ts", c("jf"), 4.0, None, OP.is_lt)
+    colop("j15", ["jf"], "ts", c("jf"), 15.0, 16384.0, OP.is_equal, OP.mult)
+    v("tc", ["payS"], ["payF"], T.payF[:], T.payS[:])
+    v("tc", ["Qin"], ["Qm"], T.Q[:, 0:B], T.Qin[:])
+    ts(["payF", "j15"], "payF", T.payF[:, 511:512], T.payF[:, 511:512], c("j15"), None, OP.add)
+    ts(["payS"], "payH", T.payH[:], T.payS[:], 5, 31, OP.arith_shift_right, OP.bitwise_and)
+    v("tc", ["payH"], ["b4"], T.payB[:, 2048:2560], T.payH[:])
+    ts(["payS"], "payL", T.payL[:], T.payS[:], 31, None, OP.bitwise_and)
+    v("tc", ["payL"], ["b5"], T.payB[:, 2560:3072], T.payL[:])
+    act(["Vin"], ["NVm"], T.NV[:, 0:B], T.Vin[:], AF.Copy, scale=-1.0)
+    for r in range(4):
+        act(["payF"], ["payA"], T.payA[:], T.payF[:], AF.Abs, bias=-1024.0 * r - 511.5)
+        act(["payA"], ["b%d" % r], T.payB[:, 512 * r:512 * r + 512], T.payA[:], AF.Relu, bias=-512.0)
+    for j in range(16):
+        k = min(j, 5)
+        dma("y", ["b%d" % k], ["PT%d" % j], T.PT[j::16, :], T.payB[:, 512 * k:512 * k + 512])
+
+    def consts2():
+        for k in range(4):
+            ts(["pj"], "pb%d" % k, T.pb[:, k:k + 1], T.pj[:, 0:1], k, 1, OP.arith_shift_right, OP.bitwise_and)
+        for k in range(4):
+            colop("f%d" % k, ["pb%d" % k], "ts", T.pb[:, k:k + 1], 2.0 ** -(2 ** k) - 1.0, 1.0, OP.mult, OP.add)
+        colop("f01", ["f0", "f1"], "tt", c("f0"), c("f1"), OP.mult)
+        colop("f23", ["f2", "f3"], "tt", c("f2"), c("f3"), OP.mult)
+        colop("pw", ["f01", "f23"], "tt", c("f01"), c("f23"), OP.mult)
+        for h in range(2):
+            v("scan", ["HALF", "ZERO"], ["thr"], T.thr[:, 128 * h:128 * h + 128], T.HALF[:], T.ZERO[:], 5.0 * 2.0 ** 63, OP.mult, OP.add)
+        ts(["BLKb"], "BIGW", T.BIGW[:], T.BLKb[:], 2.0 ** 95, None, OP.mult)
+        for k in range(8):
+            ts(["BLKb", "pw"], "WT%d" % k, T.WT[:, 128 * k:128 * k + 128], T.BLKb[:], c("pw"), 2.0 ** (63 - 16 * k), OP.mult, OP.mult)
+        ts(["g8", "gf"], "SB8", T.SB8[:], T.g8[:], c("gf"), None, OP.is_equal)
+        ts(["tt"], "irow", T.irow[:], T.tt[:, 0:128], 1 / 16, -0.46875, OP.mult, OP.add)
+        ts(["tt"], "RMx", T.RMx[:], T.tt[:, 0:128], 0.0, -1024.0, OP.is_equal, OP.mult)
+        ts(["imp"], "I16", T.I16[:], T.imp[:], 0.0, None, OP.is_equal)
+        ts(["imp"], "NI16", T.NI16[:], T.imp[:], 0.0, -1.0, OP.is_equal, OP.mult)
+        ts(["GM"], "GM2", T.GM2[:], T.GM[:], 4.0, -8.0, OP.min, OP.max)
+        colop("jc2", ["jf"], "ts", c("jf"), 1 / 16, -0.46875, OP.mult, OP.add)
+        colop("icol", ["jf"], "ts", c("jf"), 256.0, -1024.0, OP.mult, OP.add)
+        colop("corr2", ["jf"], "ts", c("jf"), 15.0, 4.0, OP.is_lt, OP.mult)
+        colop("los", ["corr2"], "ts", c("corr2"), 1.0, None, OP.add)
+        colop("ja32", ["ja"], "ts", c("ja"), 32.0, None, OP.mult)
+        colop("jw", ["ja32", "jb"], "tt", c("ja32"), c("jb"), OP.add)
+        ts(["BLKb"], "B512", T.B512[:], T.BLKb[:], 512.0, None, OP.mult)
+        ts(["BLKb"], "NB512", T.NB512[:], T.BLKb[:], -512.0, None, OP.mult)
+        v("tc", ["BLKb"], ["BLKf"], T.BLKf[:], T.BLKb[:])
+        v("tc", ["BLKb"], ["BLKh"], T.BLKh[:], T.BLKb[:])
+        ts(["Ib", "j4"], "DG", T.DG[:], T.Ib[:], c("j4"), 2.0 ** 95, OP.mult, OP.mult)
+        ts(["qg"], "ONEh", T.ONEh[:], T.qg[:], 0.0, 1.0, OP.mult, OP.add)
+        ts(["BLKb", "j4"], "BLK4n", T.BLK4n[:], T.BLKb[:], c("j4"), -1.0, OP.mult, OP.mult)
+        ts(["BLKb", "j4"], "BLK4k", T.BLK4k[:], T.BLKb[:], c("j4"), 8192.0, OP.mult, OP.mult)
+        ts(["BLKb", "jw"], "WBm", T.WBm[:], T.BLKb[:], c("jw"), None, OP.mult)
+        ts(["lane"], "rowl", T.rowl[:], T.lane[:], 1024.0, None, OP.add)
+        ts(["l16", "jf"], "LC", T.LC[:], T.l16[:], c("jf"), 1280.0, OP.add, OP.add)
+        ts(["l16", "jf"], "LC2", T.LC2[:], T.l16[:], c("jf"), float(DUMA), OP.add, OP.add)
+
+    PTs = ["PT%d" % j for j in range(16)]
+    route = split_engines(topo, cores, core)
+    arrive = sum(len(split_engines(topo, cores, s)[core]) for s in cores if s != core)
+    nlocal = {"lb": 0, "lc": 0}
+
+    def exchange(win, land, rsem, lsem):
+        waits("g", [win], [])
+        tr = []
+        for r, d in enumerate(cores):
+            if d == core:
+                continue
+            m = 0
+            for e in route[d]:
+                m |= 1 << e
+            tr.append(RemoteDMATransfer(dst_ids=[DstId(rid=topo.addr(d)[0], pnc=topo.addr(d)[1])], dma_engine_mask=m, remote_sem=T.sem[rsem],
+                                        src=T[win][:, r * 256:r * 256 + 64], dst=T[land][:, q * 64:q * 64 + 64]))
+            nlocal[lsem] += len(route[d])
+        g.remote_dma_fused(tr, local_sem=T.sem[lsem])
+        act([win], [land + "o"], T[land][:, q * 64:q * 64 + 64], T[win][:, q * 256:q * 256 + 64])
+        lastw[land] = (rsem, arrive)
+        total[rsem] = arrive
+
+    def dd_open():
+        mm(["MONE", "thr"], ["k2"], T.k2[:, 0:256], T.MONE[0:1, :], T.thr[0:1, :], True, False)
+
+    def dd_block(h, l0, l1, Rk, Rb, Wk, Wb, stop=False):
+        e, at = "eq%d_%d" % (h, l0 // 128), 256 * h + l0
+        ts([Rk, Wk], e, T.eq[:, at:at + l1 - l0], Rb[:, l0:l1], Wb[:, h:h + 1], None, OP.is_equal)
+        k = h % 8
+        for o in (0, 128):
+            a, b = max(l0, o), min(l1, o + 128)
+            if a < b:
+                same = h // 8 == o // 128
+                mm(["WT%d" % k if same else "BIGW", e], ["k2"], T.k2[:, a:b], T.WT[:, 128 * k:128 * k + 128] if same else T.BIGW[:],
+                   T.eq[:, at + a - l0:at + b - l0], False, stop)
+
+    AA, VV, QQ = ["Am", "Apd"], ["NVm", "NVp"], ["Qm", "Qp"]
+
+    def amounts(k):
+        act(AA + ["nU"], ["g%d" % k], T.G[:, 1024 * k:1024 * k + 1024], T.A[:].indirect(T.nU[:, 64 * k:64 * k + 64]))
+
+    def compare(l0, l1):
+        h, n = l0 // 128, l1 - l0
+        kk, m0 = "k%d" % (3 + h), l0 % 128
+        mm(["ONEb", "irow"], [kk], T[kk][m0:m0 + n, 0:128], T.ONEb[0:1, 0:n], T.irow[0:1, :], True, False)
+        gk = ["g%d" % k for k in range(l0 // 64, l1 // 64)]
+        for i in range(16):
+            at, ok = 256 * i + l0, "c%d_%d" % (i, l0)
+            v("tt", gk + ["k1"], [ok], T.cmp[:, at:at + n], T.G[:, 16 * l0 + i:16 * l1:16], T.k1[:, l0:l1], OP.is_ge)
+            mm([ok, "SB8"], [kk], T[kk][m0:m0 + n, i:128:16], T.cmp[:, at:at + n], T.SB8[:], False, i == 15)
+
+    def best(h):
+        kk, o = "k%d" % (3 + h), 128 * h
+        v("scan", ["RMx", kk], ["KM%d" % h], T.KM[:, o:o + 128], T.RMx[:], T[kk][:, 0:128], 0.0, OP.add, OP.max)
+        ts(["KM%d" % h], "SR%d" % h, T.SR[:, 8 * h:8 * h + 8], T.KM[:, o + 15:o + 128:16], 12582912.0, 12582912.0, OP.add, OP.subtract)
+        mm(["KM%d" % h, "I16"], ["k7"], T.k7[0:8, o:o + 128], T.KM[:, o + 15:o + 128:16], T.I16[:], True, False)
+        mm(["SR%d" % h, "NI16"], ["k7"], T.k7[0:8, o:o + 128], T.SR[:, 8 * h:8 * h + 8], T.NI16[:], False, True)
+
+    def rows(h, e):
+        o = 128 * h
+        if e == "s":
+            act(["k7"], ["o8%d" % h], T.o8[:, o:o + 128], T.k7[0:8, o:o + 128])
+        else:
+            v("tc", ["k7"], ["o8%d" % h], T.o8[:, o:o + 128], T.k7[0:8, o:o + 128])
+        mm(["sel8b", "o8%d" % h], ["k6"], T.k6[:, o:o + 128], T.sel8b[:], T.o8[:, o:o + 128])
+
+    def pick(h):
+        o = 128 * h
+        ts(["k6", "jc2"], "k6", T.k6[:, 256 + o:384 + o], T.k6[:, o:o + 128], c("jc2"), None, OP.is_equal)
+        v("tt", ["k6", "nF"], ["np%d" % h], T.np[:, o:o + 128], T.k6[:, 256 + o:384 + o], T.nF[:, o:o + 128], OP.mult)
+        out = T.k5[:, o:o + 128]
+        mm(["ONEb", "C16"], ["k5"], out, T.ONEb[0:1, 0:128], T.C16[0:1, :], True, False)
+        mm(["B512", "D1"], ["k5"], out, T.B512[:], T.D1[:, o:o + 128], False, False)
+        mm(["NB512", "D2"], ["k5"], out, T.NB512[:], T.D2[:, o:o + 128], False, False)
+        mm(["BLKf", "np%d" % h], ["k5"], out, T.BLKf[:], T.np[:, o:o + 128], False, True)
+
+    def lines(h):
+        o, w = 128 * h, slice(8 * h, 8 * h + 8)
+        v("scan", ["GM", "k5"], ["SP%d" % h], T.SP[:, o:o + 128], T.GM[:, 0:128], T.k5[:, o:o + 128], 0.0, OP.add, OP.max)
+        sp = T.SP[:, o + 15:o + 128:16]
+        ts(["SP%d" % h, "corr"], "pL%d" % h, T.pL[:, w], sp, c("corr"), 8191.0, OP.subtract, OP.min)
+        act(PTs + ["pL%d" % h], ["PG%d" % h], T.PG[:, o:o + 128], T.PT[:].indirect(T.pL[:, w]))
+        act(AA + ["pL%d" % h], ["Ap%d" % h], T.Ap[:, o:o + 128], T.A[:].indirect(T.pL[:, w]))
+        ts(["SP%d" % h, "corr"], "pWf%d" % h, T.pWf[:, w], sp, c("corr"), 8191.0, OP.subtract, OP.min)
+        v("tc", ["k5"], ["pR%d" % h], T.pR[:, o:o + 128], T.k5[:, o:o + 128])
+
+    def write_banks():
+        v("tt", ["nx", "ta", "wU"], VV, T.NV[:].indirect(T.wU[:]), T.nx[:], T.ta[:], OP.add)
+
+    for s in range(STEPS):
+        last = s == STEPS - 1
+        if s == 0:
+            mm(["sel8", "wkH"], ["k0"], T.k0[:, 0:256], T.sel8[:], T.wkH[:])
+            carry, ck = T.c0, ["c0"]
+        else:
+            mm(["WBm", "LB%d" % s, "LB%do" % s], ["k0"], T.k0[:, 0:256], T.WBm[:], T["LB%d" % s][:])
+            carry, ck = T["LD%d" % s], ["LD%d" % s, "LD%do" % s]
+        v("scan", ["GM", "k0"], ["SC"], T.SC[:], T.GM[:], T.k0[:, 0:256], 0.0, OP.add, OP.max)
+        ts(["SC", "corr"], "WL", T.WL[:], T.SC[:, 15::16], c("corr"), None, OP.subtract)
+        v("tc", QQ + ["WL"], ["nU"], T.nU[:], T.Q[:].indirect(T.WL[:]))
+        if s:
+            write_banks()
+        v("tt", VV + ["WL"] + ck, ["y"], T.y[:], T.NV[:].indirect(T.WL[:]), carry[:], OP.add)
+        ts(["y"], "nx", T.nx[:], T.y[:], 255.0, None, OP.min)
+        mm(["Ib", "nx"], ["k1"], T.k1[:, 0:256], T.Ib[:], T.nx[:])
+        if s == 0:
+            consts2()
+        v("tc", ["k0"], ["bR"], T.bR[:], T.k0[:, 0:256])
+        ts(["SC", "corr"], "Wf", T.Wf[:], T.SC[:, 15::16], c("corr"), None, OP.subtract)
+        amounts(0)
+        act(["nx"], ["mm"], T.mm[:], T.nx[:], AF.Relu)
+        mm(["BLKb", "mm"], ["k5"], T.k5[:, 256:512], T.BLKb[:], T.mm[:])
+        dd_open()
+        for h in range(16):
+            dd_block(h, 16 * h, 256, "bR", T.bR, "Wf", T.Wf, h == 15)
+        v("tc", ["nU"], ["nF"], T.nF[:], T.nU[:])
+        amounts(1)
+        act(["k5"], ["D2"], T.D2[:], T.k5[:, 256:512], AF.Sign, bias=-0.5)
+        amounts(2)
+        act(["k2"], ["D1"], T.D1[:], T.k2[:, 0:256], AF.Sign)
+        amounts(3)
+        compare(0, 128)
+        best(0)
+        compare(128, 192)
+        rows(0, "v")
+        v("scan", ["GM2", "D1"], ["SD"], T.SD[:], T.GM2[:], T.D1[:], 0.0, OP.add, OP.max)
+        pick(0)
+        ts(["SD", "los"], "wa", T.wa[:], T.SD[:, 15::16], c("los"), None, OP.is_equal)
+        v("tt", ["wa", "LC"], ["wa"], T.wa[:], T.wa[:], T.LC[:], OP.mult)
+        v("tt", ["wa", "Wf"], ["wa"], T.wa[:], T.wa[:], T.Wf[:], OP.max)
+        v("tc", ["wa"], ["wU"], T.wU[:], T.wa[:])
+        compare(192, 256)
+        best(1)
+        rows(1, "s")
+        lines(0)
+        mm(["Ib", "mm"], ["k3"], T.k3[:, 256:512], T.Ib[:], T.mm[:])
+        dd_open()
+        pick(1)
+        for h in range(8):
+            dd_block(h, 16 * h, 128, "pR0", T.pR, "pWf0", T.pWf)
+        lines(1)
+        mm(["DG", "PG0", "PG1"], ["k2"], T.k2[:, 0:256], T.DG[:], T.PG[:], False, False)
+        for h in range(8):
+            dd_block(h, 128, 256, "pR1", T.pR, "pWf0", T.pWf)
+        for h in range(8, 16):
+            dd_block(h, 16 * h, 256, "pR1", T.pR, "pWf1", T.pWf, h == 15)
+        v("tt", ["Ap0", "Ap1", "k3"], ["t"], T.t[:], T.Ap[:], T.k3[:, 256:512], OP.min)
+        ts(["k2", "j4"], "OA", T.OA[:], T.k2[:, 0:256], 0.0, c("j4"), OP.is_lt, OP.mult)
+        mm(["BLK4n", "OA"], ["k1"], T.k1[:, 0:256], T.BLK4n[:], T.OA[:])
+        if not last:
+            mm(["BLK4k", "OA"], ["k4"], T.k4[:, 256:512], T.BLK4k[:], T.OA[:])
+            act(["k4"], ["aS"], T.aS[:], T.k4[:, 256:512])
+        mm(["ONEh", "rowl"], ["k0"], T.k0[:, 256:512], T.ONEh[0:1, :], T.rowl[0:1, :], True, False)
+        v("scan", ["OA", "ONEb", "icol"], ["k7"], T.k7[:, 0:256], T.OA[:], T.ONEb[:], c("icol"), OP.add, OP.subtract)
+        v("tt", ["k7", "OA"], ["Z"], T.Z[:], T.k7[:, 0:256], T.OA[:], OP.mult)
+        mm(["BLKh", "Z"], ["k0"], T.k0[:, 256:512], T.BLKh[:], T.Z[:], False, True)
+        v("tt", ["k1", "t"], ["ta"], T.ta[:], T.k1[:, 0:256], T.t[:], OP.mult)
+        v("scan", ["GM", "k0"], ["SS"], T.SS[:], T.GM[:], T.k0[:, 256:512], 0.0, OP.add, OP.max)
+        ts(["SS", "corr"], "sL", T.sL[:], T.SS[:, 15::16], c("corr"), None, OP.subtract)
+        wb, wc, lb, lc = "WB%d" % s, "WC%d" % s, "LB%d" % (s + 1), "LD%d" % (s + 1)
+        v("tc", ["PG0", "PG1", "sL"], [wb], T[wb][:].indirect(T.sL[:]), T.PG[:])
+        exchange(wb, lb, "rb%d" % s, "lb")
+        v("tc", ["t", "sL"], [wc], T[wc][:].indirect(T.sL[:]), T.t[:])
+        exchange(wc, lc, "rc%d" % s, "lc")
+        if last:
+            write_banks()
+        else:
+            ts(["SS", "corr"], "pa", T.pa[:], T.SS[:, 15::16], c("corr"), 1024.0, OP.subtract, OP.is_ge)
+            v("tt", ["pa", "LC2"], ["pa"], T.pa[:], T.pa[:], T.LC2[:], OP.mult)
+            v("tt", ["pa", "pWf0", "pWf1"], ["pa"], T.pa[:], T.pa[:], T.pWf[:], OP.max)
+            v("tc", ["pa"], ["pU"], T.pU[:], T.pa[:])
+            v("tt", ["Ap0", "Ap1", "ta", "pU"], AA, T.A[:].indirect(T.pU[:]), T.Ap[:], T.ta[:], OP.add)
+            v("tt", ["k6", "aS"], ["qa"], T.qa[:], T.k6[:, 256:512], T.aS[:], OP.mult)
+            v("tt", ["qa", "nF", "wU"], QQ, T.Q[:].indirect(T.wU[:]), T.qa[:], T.nF[:], OP.max)
+    ts(VV, "Vin", T.Vin[:], T.NV[:, 0:B], -1.0, None, OP.mult)
+    dma("y", ["Vin"], ["yv"], T.yv[:], T.Vin[:])
+    dma("y", ["LD4", "LD4o"], ["yc"], T.yc[:], T.LD4[:])
+    mm(["WBm", "LB4", "LB4o"], ["k0"], T.k0[:, 0:256], T.WBm[:], T.LB4[:])
+    ts(["k0"], "SC", T.SC[:], T.k0[:, 0:256], float(B), None, OP.min)
+    dma("s", ["SC"], ["yw"], T.yw[:], T.SC[0:128:16, :])
+    total["lb"], total["lc"] = nlocal["lb"], nlocal["lc"]
+    for sem in sorted(total):
+        need_wait("g", sem, total[sem])

@@ -1,9 +1,18 @@
 from concourse.bass import DstId, RemoteDMATransfer
 from concourse.mybir import AluOpType as OP, ActivationFunctionType as AF
 
-STEPS, B, NONE = 4, 1024, 8191
-VW, AW, DUMA = 1536, 8464, 8208
-BIG = 65536.0
+STEPS, B = 4, 1024
+LO = 32
+NONE = LO + 8191
+VO = 1600.0
+VW, AW, XWIN = 1536, LO + 8464, LO + 9488
+EMPTY = 512.0 * B
+LIFT = 2.0 ** 20
+KILL = 2.0 ** 70
+MAGIC = 1.5 * 2.0 ** 23
+HEAD = "bo qr up wf op"
+ORDER = """bt0 po bt1 am0 am1 cm0 cm1 bt2 bt3 dz cm2 am2 cm3 we0 lo0 nf cm4 pk0 am3 cm5 ln0 cm6 br0 cm7 lt0 py0 we1 lt1 lo1 rk0 pk1 ms0 ct0 es
+    ln1 pc0 lt2 py1 lt3 lt4 ms1 lt5 sl0 rk1 pc1 cv dr0 bl br1 ct1 pl0 sl1 pl1 wb0 nr0 ll ex dr1 nr1 wr0 wl bo wr1 qr wb1 op up wf"""
 SCRATCH = {}
 
 
@@ -12,46 +21,40 @@ def _buf(dtype, n, names, parts=128):
         SCRATCH[b] = ("sbuf", [parts, n], dtype)
 
 
-_buf("bfloat16", VW, "NV")
-_buf("float32", VW, "Q")
-_buf("bfloat16", B, "Vin")
+_buf("bfloat16", VW, "V")
+_buf("float32", VW, "Q VT")
+_buf("float32", B, "Vr")
 _buf("int32", B, "Qin")
 _buf("bfloat16", AW, "A")
-_buf("bfloat16", 8192, "PT")
-_buf("int32", 512, "payS payH payL")
+_buf("bfloat16", LO + 8192, "PT")
+_buf("float32", 1024 * (STEPS - 1) + XWIN, "XW")
+_buf("int32", 512, "payS payL")
 _buf("float32", 512, "payF payA")
-_buf("bfloat16", 3072, "payB")
+_buf("bfloat16", 2560, "payB")
+_buf("bfloat16", 1024, "WT ONE")
 _buf("int32", 256, "wkI", 8)
-_buf("float32", 256, "wkE", 8)
 _buf("float16", 256, "wkH", 8)
 _buf("float16", 128, "sel8", 8)
-_buf("bfloat16", 128, "sel8b", 8)
-_buf("bfloat16", 256, "o8", 8)
-_buf("float32", 128, "imp qg BLKf")
-_buf("float32", 256, "tt lane gmA SC SP SS nF np qa aS")
+_buf("float32", 128, "imp qg BLKf If u1 u2")
+_buf("float32", 144, "ebi")
+_buf("bfloat16", 144, "EB")
+_buf("float32", 256, "SC SP SS nF np Xs qn vn Vg yw32")
 _buf("int32", 8, "pc pj pg pb")
-_buf("float32", 32, "cf")
-_buf("float32", 16, "l16 LC LC2 Wf wa pWf pa")
+_buf("float32", 48, "cf")
+_buf("float32", 16, "l16 LC Wf wa pWf pWc pa")
 _buf("uint16", 16, "WL wU pL sL pU")
-_buf("float32", 8, "g8")
-_buf("float32", 64, "khi klo")
-_buf("bfloat16", 64, "tmp")
-_buf("float16", 128, "I16 NI16 ONEh BLKh")
-_buf("bfloat16", 128, "Ib BLKb B512 NB512 BLK4n BLK4k DG WBm irow MONE C16 RMx HALF ZERO BIGW")
-_buf("bfloat16", 8, "SB8")
-_buf("bfloat16", 1024, "WT")
-_buf("bfloat16", 256, "gmB gmC GM GM2 ONEb thr SD y nx mm D1 D2 PG Ap t ta OA c0")
-_buf("float16", 256, "rowl KM Z")
-_buf("float16", 16, "SR")
-_buf("uint16", 256, "nU bR pR")
+_buf("float16", 128, "N512 BLKh")
+_buf("bfloat16", 128, "Ib NIb BLKb B512 B4a B4q B4n I8k DG WBm HALF ZERO BIGW TRI")
+_buf("bfloat16", 256, "tt GM GM2 STEP thr thr2 SD x mm D1 D2 e Mb PG Ap r An tp OA cb")
+_buf("float16", 256, "Z bR y")
+_buf("uint16", 256, "nU pR")
 _buf("bfloat16", 4096, "eq G cmp")
-for _s in range(STEPS):
-    _buf("bfloat16", 1280, "WB%d WC%d" % (_s, _s))
-    _buf("bfloat16", 256, "LB%d LD%d" % (_s + 1, _s + 1))
+for _s in range(STEPS + 1):
+    _buf("float32", 256, "L%d" % _s)
 PSUM = ["k%d" % s for s in range(8)]
 for _s in PSUM:
     SCRATCH[_s] = ("psum", [128, 512], "float32")
-SEMAPHORES = ["sv", "ss", "st", "sg", "lb", "lc"] + ["rb%d" % s for s in range(STEPS)] + ["rc%d" % s for s in range(STEPS)] + ["d%d" % k for k in range(30)]
+SEMAPHORES = ["sv", "ss", "st", "sg", "lx"] + ["rx%d" % s for s in range(STEPS)] + ["d%d" % k for k in range(16)]
 
 
 def split_engines(topo, cores, src):
@@ -149,23 +152,25 @@ def rank_program(g, core, T, topo):
     def mm(R, W, out, lhsT, rhs, start=True, stop=True):
         op("t", "mm", R, W, out, lhsT, rhs, start, stop)
 
+    def acc(bank, out, terms):
+        for k, (R, lhsT, rhs) in enumerate(terms):
+            mm(R, [bank], out, lhsT, rhs, k == 0, k == len(terms) - 1)
+
     dma("y", [], ["wkI"], T.wkI[:], T.wk[:])
     dma("y", [], ["payS"], T.payS[:], T.pay[:])
     dma("y", [], ["Qin"], T.Qin[:], T.qu[:])
-    dma("y", [], ["Vin"], T.Vin[:], T.vp[:])
-    dma("y", [], ["Am"], T.A[:, 0:8192], T.am[:])
+    dma("y", [], ["Am"], T.A[:, LO:LO + 8192], T.am[:])
+    dma("y", [], ["Vm"], T.V[:, 0:B], T.vp[:])
 
     def iota(buf, out, pattern, base, cm):
         op("g", "iota", [], [buf], out, pattern, base, cm, allow_small_or_imprecise_dtypes=True)
     iota("pc", T.pc[:, 0:1], [[1, 1]], 0, 1)
     iota("qg", T.qg[:], [[1, 8], [0, 16]], 0, 0)
-    iota("khi", T.khi[:], [[1, 2], [0, 32]], 32 + 2 * q, 0)
-    iota("klo", T.klo[:], [[0, 2], [1, 32]], 0, 0)
-    iota("tt", T.tt[:], [[0, 16], [1, 16]], 0, 0)
     iota("imp", T.imp[:], [[1, 128]], 0, -1)
-    iota("g8", T.g8[:], [[1, 8]], 0, 0)
-    iota("lane", T.lane[:], [[1, 256]], 0, 0)
+    iota("tt", T.tt[:], [[0, 16], [1, 16]], 0, 0)
     iota("l16", T.l16[:], [[16, 16]], 0, 0)
+    iota("ebi", T.ebi[:], [[1, 144]], -15, 0)
+    iota("PTa", T.PT[:, 0:LO + 4096], [[0, LO + 4096]], 1, 0)
 
     col = {}
 
@@ -175,104 +180,121 @@ def rank_program(g, core, T, topo):
     def colop(name, R, call, *a):
         col[name] = len(col)
         v(call, R, [name], c(name), *a)
+
+    def byrow(name, parts):
+        for n, (cmp, k, val) in enumerate(parts):
+            colop("%s_%d" % (name, n), ["jf"], "ts", c("jf"), float(k), float(val), cmp, OP.mult)
+        col[name] = col[name + "_0"]
+        lastw[name] = lastw[name + "_0"]
+        for n in range(1, len(parts)):
+            act([name, "%s_%d" % (name, n)], [name], c(name), c(name), AF.Identity, bias=c("%s_%d" % (name, n)))
+
+    def fill(W, out, n, val):
+        act(["ONE"], [W], out, T.ONE[:, 0:n], AF.Copy, scale=val)
+
+    def scaled(name, src, by):
+        act([src] + ([by] if by in col else []), [name], T[name][:], T[src][:], AF.Copy, scale=c(by) if by in col else by)
+
+    v("ms", [], ["ONE"], T.ONE[:], 1.0)
+    for k in range(4):
+        fill("PTb%d" % k, T.PT[:, LO + 4096 + 1024 * k:LO + 5120 + 1024 * k], 1024, 1.0)
     v("ms", [], ["ZERO"], T.ZERO[:], 0.0)
-    v("ms", [], ["NVp"], T.NV[:, B:VW], 0.0)
-    v("ms", [], ["Qp"], T.Q[:, B:VW], float(NONE))
-    v("ms", [], ["Apd"], T.A[:, 8192:AW], 0.0)
-    v("ms", [], ["c0"], T.c0[:], 0.0)
-    v("ms", [], ["ONEb"], T.ONEb[:], 1.0)
-    v("ms", [], ["MONE"], T.MONE[:], -1.0)
     v("ms", [], ["HALF"], T.HALF[:], 0.5)
-    v("ms", [], ["C16"], T.C16[:], 16384.0)
+    v("ms", [], ["Vp"], T.V[:, B:VW], 0.0)
+    v("ms", [], ["Apd"], T.A[:, LO + 8192:AW], 0.0)
+    v("ms", [], ["Apl"], T.A[:, 0:LO], 0.0)
+    v("ms", [], ["Qp"], T.Q[:, B:VW], float(NONE))
+    for h in range(2):
+        v("scan", ["HALF", "ZERO"], ["thr"], T.thr[:, 128 * h:128 * h + 128], T.HALF[:], T.ZERO[:], 5.0 * 2.0 ** 63, OP.mult, OP.add)
     ts(["pc"], "pj", T.pj[:, 0:1], T.pc[:, 0:1], 15, None, OP.bitwise_and)
     ts(["pc"], "pg", T.pg[:, 0:1], T.pc[:, 0:1], 4, None, OP.arith_shift_right)
     colop("jf", ["pj"], "tc", T.pj[:, 0:1])
     colop("gf", ["pg"], "tc", T.pg[:, 0:1])
     colop("pf", ["pc"], "tc", T.pc[:, 0:1])
-    colop("ja", ["jf"], "ts", c("jf"), 4.0, None, OP.is_equal)
-    colop("jb", ["jf"], "ts", c("jf"), 5.0, None, OP.is_equal)
-    ts(["khi", "ja"], "khi", T.khi[:], T.khi[:], c("ja"), None, OP.mult)
-    ts(["klo", "jb"], "klo", T.klo[:], T.klo[:], c("jb"), None, OP.mult)
-    v("tt", ["khi", "klo"], ["tmp"], T.tmp[:], T.khi[:], T.klo[:], OP.add)
+    for k in range(4):
+        ts(["pj"], "pb%d" % k, T.pb[:, k:k + 1], T.pj[:, 0:1], k, 1, OP.arith_shift_right, OP.bitwise_and)
     pf8 = T.cf[0:8, col["pf"]:col["pf"] + 1]
-    ts(["qg", "pf"], "sel8", T.sel8[:], T.qg[0:8, :], pf8, None, OP.is_equal)
-    ts(["qg", "pf"], "sel8b", T.sel8b[:], T.qg[0:8, :], pf8, None, OP.is_equal)
-    colop("corr", ["jf"], "ts", c("jf"), 15.0, BIG, OP.is_lt, OP.mult)
-    ts(["tt", "jf"], "gmA", T.gmA[:], T.tt[:], c("jf"), None, OP.subtract)
-    ts(["gmA"], "gmB", T.gmB[:], T.gmA[:], 0.0, -4.0 * BIG, OP.is_le, OP.mult)
-    ts(["gmA"], "gmC", T.gmC[:], T.gmA[:], 1.0, BIG, OP.is_equal, OP.mult)
-    v("tt", ["gmB", "gmC"], ["GM"], T.GM[:], T.gmB[:], T.gmC[:], OP.add)
-    for s in range(STEPS):
-        for r in range(4):
-            act(["tmp"], ["WB%d" % s], T["WB%d" % s][:, r * 256:r * 256 + 64], T.tmp[:])
-            act(["ZERO"], ["WC%d" % s], T["WC%d" % s][:, r * 256:r * 256 + 64], T.ZERO[:, 0:64])
-    ts(["wkI"], "wkE", T.wkE[:], T.wkI[:], float(B), None, OP.is_ge)
-    v("tt", ["wkE", "lane"], ["wkE"], T.wkE[:], T.wkE[:], T.lane[0:8, :], OP.mult)
-    v("tt", ["wkI", "wkE"], ["wkH"], T.wkH[:], T.wkI[:], T.wkE[:], OP.add)
-    ts(["imp"], "Ib", T.Ib[:], T.imp[:], 0.0, None, OP.is_equal)
+    ts(["qg", "pf"], "sel8", T.sel8[:], T.qg[0:8, :], pf8, 512.0, OP.is_equal, OP.mult)
+    v("tc", ["wkI"], ["wkH"], T.wkH[:], T.wkI[:])
+    mm(["sel8", "wkH"], ["k0"], T.k0[:, 0:256], T.sel8[:], T.wkH[:])
     ts(["qg", "gf"], "BLKb", T.BLKb[:], T.qg[:], c("gf"), None, OP.is_equal)
-    colop("j4", ["jf"], "ts", c("jf"), 4.0, None, OP.is_lt)
-    colop("j15", ["jf"], "ts", c("jf"), 15.0, 16384.0, OP.is_equal, OP.mult)
+    ts(["imp"], "Ib", T.Ib[:], T.imp[:], 0.0, None, OP.is_equal)
+    ts(["Ib"], "N512", T.N512[:], T.Ib[:], -512.0, None, OP.mult)
+    for k in range(4):
+        colop("f%d" % k, ["pb%d" % k], "ts", T.pb[:, k:k + 1], 2.0 ** -(2 ** k) - 1.0, 1.0, OP.mult, OP.add)
+    colop("f01", ["f0", "f1"], "tt", c("f0"), c("f1"), OP.mult)
+    colop("f23", ["f2", "f3"], "tt", c("f2"), c("f3"), OP.mult)
+    colop("pw", ["f01", "f23"], "tt", c("f01"), c("f23"), OP.mult)
+    colop("jh", ["jf"], "ts", c("jf"), 0.5, None, OP.add)
+    colop("corr", ["jf"], "ts", c("jf"), -LIFT, 15 * LIFT, OP.mult, OP.add)
+    colop("n15", ["jf"], "ts", c("jf"), 15.0, None, OP.is_lt)
+    ts(["tt", "jh"], "GM", T.GM[:], T.tt[:], c("jh"), 64 * LIFT, OP.subtract, OP.mult)
+    ts(["GM"], "GM", T.GM[:], T.GM[:], LIFT, None, OP.min)
     v("tc", ["payS"], ["payF"], T.payF[:], T.payS[:])
-    v("tc", ["Qin"], ["Qm"], T.Q[:, 0:B], T.Qin[:])
-    ts(["payF", "j15"], "payF", T.payF[:, 511:512], T.payF[:, 511:512], c("j15"), None, OP.add)
-    ts(["payS"], "payH", T.payH[:], T.payS[:], 5, 31, OP.arith_shift_right, OP.bitwise_and)
-    v("tc", ["payH"], ["b4"], T.payB[:, 2048:2560], T.payH[:])
+    v("tc", ["k0"], ["L0"], T.L0[:], T.k0[:, 0:256])
+    for k in range(3):
+        act(["payF"], ["b%d" % k], T.payB[:, 512 * k:512 * k + 512], T.payF[:], AF.Sign, bias=0.5 - 1024 * (k + 1))
+    act(["payF"], ["payA"], T.payA[:], T.payF[:], AF.Identity, bias=-15.5 / 32, scale=1 / 32)
     ts(["payS"], "payL", T.payL[:], T.payS[:], 31, None, OP.bitwise_and)
-    v("tc", ["payL"], ["b5"], T.payB[:, 2560:3072], T.payL[:])
-    act(["Vin"], ["NVm"], T.NV[:, 0:B], T.Vin[:], AF.Copy, scale=-1.0)
-    for r in range(4):
-        act(["payF"], ["payA"], T.payA[:], T.payF[:], AF.Abs, bias=-1024.0 * r - 511.5)
-        act(["payA"], ["b%d" % r], T.payB[:, 512 * r:512 * r + 512], T.payA[:], AF.Relu, bias=-512.0)
-    for j in range(16):
-        k = min(j, 5)
-        dma("y", ["b%d" % k], ["PT%d" % j], T.PT[j::16, :], T.payB[:, 512 * k:512 * k + 512])
+    v("tc", ["payL"], ["b4"], T.payB[:, 2048:2560], T.payL[:])
+    for k in range(8):
+        ts(["BLKb", "pw"], "WT%d" % k, T.WT[:, 128 * k:128 * k + 128], T.BLKb[:], c("pw"), 2.0 ** (63 - 16 * k), OP.mult, OP.mult)
+    ts(["payA"], "b3", T.payB[:, 1536:2048], T.payA[:], MAGIC, MAGIC, OP.add, OP.subtract)
+    for k in range(3):
+        end = T.payB[:, 512 * k + 511:512 * k + 512]
+        ts(["b%d" % k, "n15"], "b%d" % k, end, end, c("n15"), None, OP.mult)
+    ts(["Qin"], "Qm", T.Q[:, 0:B], T.Qin[:], float(LO), None, OP.add)
+    PTf = ["PTa"] + ["PTb%d" % k for k in range(4)]
+    for j in range(5):
+        dma("y", ["b%d" % j, "Am"] + PTf, ["PT%d" % j], T.PT[j::16, LO:LO + 8192], T.payB[:, 512 * j:512 * j + 512])
+    scaled("If", "Ib", 1.0)
+    scaled("NIb", "Ib", -1.0)
+    scaled("BIGW", "BLKb", KILL)
+    colop("g16", ["gf"], "ts", c("gf"), 16.0, None, OP.mult)
+    ts(["ebi", "g16"], "EB", T.EB[:], T.ebi[:], c("g16"), None, OP.is_equal)
+    colop("j4", ["jf"], "ts", c("jf"), 4.0, None, OP.is_lt)
+    colop("los", ["jf"], "ts", c("jf"), -2.0, 31.0, OP.mult, OP.add)
+    colop("pco", ["corr"], "ts", c("corr"), 1024.0, None, OP.add)
+    colop("n4", ["jf"], "ts", c("jf"), 4.0, None, OP.not_equal)
+    colop("j256", ["jf", "j4"], "ts", c("jf"), 256.0, c("j4"), OP.mult, OP.mult)
+    byrow("icol", [(OP.is_lt, 4, -1040 - LO), (OP.is_equal, 4, 1039 + LO), (OP.is_equal, 5, 8192)])
+    act(["icol", "j256"], ["icol"], c("icol"), c("icol"), AF.Identity, bias=c("j256"))
+    byrow("jw", [(OP.is_lt, 3, -512 * 512), (OP.is_equal, 3, 512 * 32), (OP.is_equal, 4, 512), (OP.is_equal, 5, -512 * 1536)])
+    byrow("jq", [(OP.is_lt, 4, 8192), (OP.is_equal, 4, LO - 8192)])
+    byrow("ja", [(OP.is_lt, 4, 512)])
+    byrow("jn", [(OP.is_lt, 4, -8192)])
+    byrow("jt", [(OP.is_ge, 4, 2.0 ** 90), (OP.is_ge, 6, -2.0 ** 91)])
+    byrow("dm", [(OP.is_lt, 3, -2 * KILL)])
+    byrow("da", [(OP.is_lt, 3, KILL), (OP.is_equal, 5, 3 * KILL)])
+    ts(["imp"], "u1", T.u1[:], T.imp[:], 0.0, 1.96875, OP.is_lt, OP.mult)
+    ts(["Ib"], "u2", T.u2[:], T.Ib[:], -1.03125, 0.03125, OP.mult, OP.add)
+    v("tt", ["u1", "u2"], ["u1"], T.u1[:], T.u1[:], T.u2[:], OP.add)
+    v("tt", ["u1", "BLKb"], ["TRI"], T.TRI[:], T.u1[:], T.BLKb[:], OP.mult)
+    ts(["tt", "jf"], "u2", T.u2[:], T.tt[:, 0:128], c("jf"), None, OP.is_gt)
+    ts(["u2", "dm", "da"], "u2", T.u2[:], T.u2[:], c("dm"), c("da"), OP.mult, OP.add)
+    v("tt", ["u2", "BLKb"], ["DG"], T.DG[:], T.u2[:], T.BLKb[:], OP.mult)
+    ts(["GM"], "GM2", T.GM2[:], T.GM[:], 2 / LIFT, -64.0, OP.mult, OP.max)
+    v("tc", ["BLKb"], ["BLKh"], T.BLKh[:], T.BLKb[:])
+    ts(["l16", "jf"], "LC", T.LC[:], T.l16[:], c("jf"), 1280.0 + B, OP.add, OP.add)
+    for name, by in (("B512", 512.0), ("BLKf", 1.0), ("WBm", "jw"), ("B4n", "jn"), ("B4a", "ja"), ("B4q", "jq")):
+        scaled(name, "BLKb", by)
+    scaled("I8k", "Ib", 8192.0)
+    act(["thr", "j4", "jt"], ["thr2"], T.thr2[:], T.thr[:], AF.Identity, bias=c("jt"), scale=c("j4"))
+    act(["ONE", "n4"], ["STEP"], T.STEP[:], T.ONE[:, 0:256], AF.Copy, scale=c("n4"))
 
-    def consts2():
-        for k in range(4):
-            ts(["pj"], "pb%d" % k, T.pb[:, k:k + 1], T.pj[:, 0:1], k, 1, OP.arith_shift_right, OP.bitwise_and)
-        for k in range(4):
-            colop("f%d" % k, ["pb%d" % k], "ts", T.pb[:, k:k + 1], 2.0 ** -(2 ** k) - 1.0, 1.0, OP.mult, OP.add)
-        colop("f01", ["f0", "f1"], "tt", c("f0"), c("f1"), OP.mult)
-        colop("f23", ["f2", "f3"], "tt", c("f2"), c("f3"), OP.mult)
-        colop("pw", ["f01", "f23"], "tt", c("f01"), c("f23"), OP.mult)
-        for h in range(2):
-            v("scan", ["HALF", "ZERO"], ["thr"], T.thr[:, 128 * h:128 * h + 128], T.HALF[:], T.ZERO[:], 5.0 * 2.0 ** 63, OP.mult, OP.add)
-        ts(["BLKb"], "BIGW", T.BIGW[:], T.BLKb[:], 2.0 ** 95, None, OP.mult)
-        for k in range(8):
-            ts(["BLKb", "pw"], "WT%d" % k, T.WT[:, 128 * k:128 * k + 128], T.BLKb[:], c("pw"), 2.0 ** (63 - 16 * k), OP.mult, OP.mult)
-        ts(["g8", "gf"], "SB8", T.SB8[:], T.g8[:], c("gf"), None, OP.is_equal)
-        ts(["tt"], "irow", T.irow[:], T.tt[:, 0:128], 1 / 16, -0.46875, OP.mult, OP.add)
-        ts(["tt"], "RMx", T.RMx[:], T.tt[:, 0:128], 0.0, -1024.0, OP.is_equal, OP.mult)
-        ts(["imp"], "I16", T.I16[:], T.imp[:], 0.0, None, OP.is_equal)
-        ts(["imp"], "NI16", T.NI16[:], T.imp[:], 0.0, -1.0, OP.is_equal, OP.mult)
-        ts(["GM"], "GM2", T.GM2[:], T.GM[:], 4.0, -8.0, OP.min, OP.max)
-        colop("jc2", ["jf"], "ts", c("jf"), 1 / 16, -0.46875, OP.mult, OP.add)
-        colop("icol", ["jf"], "ts", c("jf"), 256.0, -1024.0, OP.mult, OP.add)
-        colop("corr2", ["jf"], "ts", c("jf"), 15.0, 4.0, OP.is_lt, OP.mult)
-        colop("los", ["corr2"], "ts", c("corr2"), 1.0, None, OP.add)
-        colop("ja32", ["ja"], "ts", c("ja"), 32.0, None, OP.mult)
-        colop("jw", ["ja32", "jb"], "tt", c("ja32"), c("jb"), OP.add)
-        ts(["BLKb"], "B512", T.B512[:], T.BLKb[:], 512.0, None, OP.mult)
-        ts(["BLKb"], "NB512", T.NB512[:], T.BLKb[:], -512.0, None, OP.mult)
-        v("tc", ["BLKb"], ["BLKf"], T.BLKf[:], T.BLKb[:])
-        v("tc", ["BLKb"], ["BLKh"], T.BLKh[:], T.BLKb[:])
-        ts(["Ib", "j4"], "DG", T.DG[:], T.Ib[:], c("j4"), 2.0 ** 95, OP.mult, OP.mult)
-        ts(["qg"], "ONEh", T.ONEh[:], T.qg[:], 0.0, 1.0, OP.mult, OP.add)
-        ts(["BLKb", "j4"], "BLK4n", T.BLK4n[:], T.BLKb[:], c("j4"), -1.0, OP.mult, OP.mult)
-        ts(["BLKb", "j4"], "BLK4k", T.BLK4k[:], T.BLKb[:], c("j4"), 8192.0, OP.mult, OP.mult)
-        ts(["BLKb", "jw"], "WBm", T.WBm[:], T.BLKb[:], c("jw"), None, OP.mult)
-        ts(["lane"], "rowl", T.rowl[:], T.lane[:], 1024.0, None, OP.add)
-        ts(["l16", "jf"], "LC", T.LC[:], T.l16[:], c("jf"), 1280.0, OP.add, OP.add)
-        ts(["l16", "jf"], "LC2", T.LC2[:], T.l16[:], c("jf"), float(DUMA), OP.add, OP.add)
+    def empty_slots(s):
+        for r in range(4):
+            at = 1024 * s + 256 * r
+            fill("XW", T.XW[:, at:at + 64], 64, EMPTY)
 
-    PTs = ["PT%d" % j for j in range(16)]
+    PTs = PTf + ["PT%d" % j for j in range(5)]
     route = split_engines(topo, cores, core)
     arrive = sum(len(split_engines(topo, cores, s)[core]) for s in cores if s != core)
-    nlocal = {"lb": 0, "lc": 0}
+    sent = [0]
 
-    def exchange(win, land, rsem, lsem):
-        waits("g", [win], [])
+    def exchange(s):
+        land, at = "L%d" % (s + 1), 1024 * s
+        waits("g", ["XW"], [])
         tr = []
         for r, d in enumerate(cores):
             if d == core:
@@ -280,172 +302,296 @@ def rank_program(g, core, T, topo):
             m = 0
             for e in route[d]:
                 m |= 1 << e
-            tr.append(RemoteDMATransfer(dst_ids=[DstId(rid=topo.addr(d)[0], pnc=topo.addr(d)[1])], dma_engine_mask=m, remote_sem=T.sem[rsem],
-                                        src=T[win][:, r * 256:r * 256 + 64], dst=T[land][:, q * 64:q * 64 + 64]))
-            nlocal[lsem] += len(route[d])
-        g.remote_dma_fused(tr, local_sem=T.sem[lsem])
-        act([win], [land + "o"], T[land][:, q * 64:q * 64 + 64], T[win][:, q * 256:q * 256 + 64])
-        lastw[land] = (rsem, arrive)
-        total[rsem] = arrive
+            tr.append(RemoteDMATransfer(dst_ids=[DstId(rid=topo.addr(d)[0], pnc=topo.addr(d)[1])], dma_engine_mask=m, remote_sem=T.sem["rx%d" % s],
+                                        src=T.XW[:, at + r * 256:at + r * 256 + 64], dst=T[land][:, q * 64:q * 64 + 64]))
+            sent[0] += len(route[d])
+        g.remote_dma_fused(tr, local_sem=T.sem.lx)
+        readers["XW"]["lx"] = total["lx"] = sent[0]
+        v("tc", ["XW"], [land + "o"], T[land][:, q * 64:q * 64 + 64], T.XW[:, at + q * 256:at + q * 256 + 64])
+        lastw[land] = ("rx%d" % s, arrive)
+        total["rx%d" % s] = arrive
 
-    def dd_open():
-        mm(["MONE", "thr"], ["k2"], T.k2[:, 0:256], T.MONE[0:1, :], T.thr[0:1, :], True, False)
+    AA, VV, QQ, VT = ["Am", "Apd", "Apl"], ["Vm", "Vp"], ["Qm", "Qp"], ["VTm", "VTp"]
+    ddk = ["k2", "k6"]
+    drk = ["k0", "k1"]
 
-    def dd_block(h, l0, l1, Rk, Rb, Wk, Wb, stop=False):
+    def half(h):
+        return "k%d" % (3 + h), slice(128 * h, 128 * h + 128), slice(8 * h, 8 * h + 8)
+
+    def twins(h, l0, l1, Rk, Rb, Wk, Wb, stop=()):
         e, at = "eq%d_%d" % (h, l0 // 128), 256 * h + l0
         ts([Rk, Wk], e, T.eq[:, at:at + l1 - l0], Rb[:, l0:l1], Wb[:, h:h + 1], None, OP.is_equal)
         k = h % 8
-        for o in (0, 128):
-            a, b = max(l0, o), min(l1, o + 128)
+        for o in (0, 1):
+            a, b = max(l0, 128 * o), min(l1, 128 * o + 128)
             if a < b:
-                same = h // 8 == o // 128
-                mm(["WT%d" % k if same else "BIGW", e], ["k2"], T.k2[:, a:b], T.WT[:, 128 * k:128 * k + 128] if same else T.BIGW[:],
-                   T.eq[:, at + a - l0:at + b - l0], False, stop)
+                same = h // 8 == o
+                mm(["WT%d" % k if same else "BIGW", e], [ddk[o]], T[ddk[o]][:, a:b], T.WT[:, 128 * k:128 * k + 128] if same else T.BIGW[:],
+                   T.eq[:, at + a - l0:at + b - l0], h == 0, o in stop)
 
-    AA, VV, QQ = ["Am", "Apd"], ["NVm", "NVp"], ["Qm", "Qp"]
+    def unpack(s):
+        L, Lk = T["L%d" % s], ["L%d" % s, "L%do" % s]
+        ts(Lk, "bR", T.bR[:], L[:], 1 / 512, float(B), OP.mult, OP.add)
+        acc("k0", T.k0[:, 0:256], [(Lk + ["If"], T.If[:], L[:]), (["N512", "bR"], T.N512[:], T.bR[:])])
+
+    def positions():
+        v("tt", ["Vg", "k0"], ["y"], T.y[:], T.Vg[:], T.k0[:, 0:256], OP.subtract)
+        ts(["y"], "x", T.x[:], T.y[:], VO, -255.0, OP.subtract, OP.max)
+        ts(["x"], "mm", T.mm[:], T.x[:], -1.0, 0.0, OP.mult, OP.max)
+        mm(["NIb", "x"], ["k1"], T.k1[:, 0:256], T.NIb[:], T.x[:])
+        mm(["BLKb", "mm"], ["k5"], T.k5[:, 256:512], T.BLKb[:], T.mm[:])
 
     def amounts(k):
         act(AA + ["nU"], ["g%d" % k], T.G[:, 1024 * k:1024 * k + 1024], T.A[:].indirect(T.nU[:, 64 * k:64 * k + 64]))
 
-    def compare(l0, l1):
-        h, n = l0 // 128, l1 - l0
-        kk, m0 = "k%d" % (3 + h), l0 % 128
-        mm(["ONEb", "irow"], [kk], T[kk][m0:m0 + n, 0:128], T.ONEb[0:1, 0:n], T.irow[0:1, :], True, False)
-        gk = ["g%d" % k for k in range(l0 // 64, l1 // 64)]
-        for i in range(16):
-            at, ok = 256 * i + l0, "c%d_%d" % (i, l0)
-            v("tt", gk + ["k1"], [ok], T.cmp[:, at:at + n], T.G[:, 16 * l0 + i:16 * l1:16], T.k1[:, l0:l1], OP.is_ge)
-            mm([ok, "SB8"], [kk], T[kk][m0:m0 + n, i:128:16], T.cmp[:, at:at + n], T.SB8[:], False, i == 15)
+    def compare(k, part):
+        l0, kk, m0 = 64 * k, "k%d" % (3 + k // 2), 64 * (k % 2)
+        for i in range(8 * part, 8 * part + 8):
+            at, ok = 256 * i + l0, "c%d_%d" % (i, k)
+            v("tt", ["g%d" % k, "k1"], [ok], T.cmp[:, at:at + 64], T.G[:, 16 * l0 + i:16 * l0 + 1024:16], T.k1[:, l0:l0 + 64], OP.is_ge)
+            mm([ok, "EB"], [kk], T[kk][:, m0:m0 + 64], T.EB[:, 15 - i:143 - i], T.cmp[:, at:at + 64], i == 0, i == 15)
 
-    def best(h):
-        kk, o = "k%d" % (3 + h), 128 * h
-        v("scan", ["RMx", kk], ["KM%d" % h], T.KM[:, o:o + 128], T.RMx[:], T[kk][:, 0:128], 0.0, OP.add, OP.max)
-        ts(["KM%d" % h], "SR%d" % h, T.SR[:, 8 * h:8 * h + 8], T.KM[:, o + 15:o + 128:16], 12582912.0, 12582912.0, OP.add, OP.subtract)
-        mm(["KM%d" % h, "I16"], ["k7"], T.k7[0:8, o:o + 128], T.KM[:, o + 15:o + 128:16], T.I16[:], True, False)
-        mm(["SR%d" % h, "NI16"], ["k7"], T.k7[0:8, o:o + 128], T.SR[:, 8 * h:8 * h + 8], T.NI16[:], False, True)
+    def weigh(h):
+        kk, o, w = half(h)
+        act([kk], ["e%d" % h], T.e[:, o], T[kk][:, 0:128], AF.Silu, bias=-85.6, scale=4.6)
+        mm(["TRI", "e%d" % h], [kk], T[kk][:, 128:256], T.TRI[:], T.e[:, o])
 
-    def rows(h, e):
-        o = 128 * h
-        if e == "s":
-            act(["k7"], ["o8%d" % h], T.o8[:, o:o + 128], T.k7[0:8, o:o + 128])
-        else:
-            v("tc", ["k7"], ["o8%d" % h], T.o8[:, o:o + 128], T.k7[0:8, o:o + 128])
-        mm(["sel8b", "o8%d" % h], ["k6"], T.k6[:, o:o + 128], T.sel8b[:], T.o8[:, o:o + 128])
+    def losers(h):
+        kk, o, w = half(h)
+        v("tt", [ddk[h], "thr"], ["D1%d" % h], T.D1[:, o], T[ddk[h]][:, o], T.thr[:, o], OP.is_ge)
 
     def pick(h):
-        o = 128 * h
-        ts(["k6", "jc2"], "k6", T.k6[:, 256 + o:384 + o], T.k6[:, o:o + 128], c("jc2"), None, OP.is_equal)
-        v("tt", ["k6", "nF"], ["np%d" % h], T.np[:, o:o + 128], T.k6[:, 256 + o:384 + o], T.nF[:, o:o + 128], OP.mult)
-        out = T.k5[:, o:o + 128]
-        mm(["ONEb", "C16"], ["k5"], out, T.ONEb[0:1, 0:128], T.C16[0:1, :], True, False)
-        mm(["B512", "D1"], ["k5"], out, T.B512[:], T.D1[:, o:o + 128], False, False)
-        mm(["NB512", "D2"], ["k5"], out, T.NB512[:], T.D2[:, o:o + 128], False, False)
-        mm(["BLKf", "np%d" % h], ["k5"], out, T.BLKf[:], T.np[:, o:o + 128], False, True)
+        kk, o, w = half(h)
+        ts([kk], kk, T[kk][:, 256:384], T[kk][:, 128:256], 0.0, None, OP.is_gt)
+        v("tt", [kk, "nF"], ["np%d" % h], T.np[:, o], T[kk][:, 256:384], T.nF[:, o], OP.mult)
+        acc("k5", T.k5[:, o], [(["B512", "D1%d" % h], T.B512[:], T.D1[:, o]), (["B512", "D2"], T.B512[:], T.D2[:, o]), (["BLKf", "np%d" % h], T.BLKf[:], T.np[:, o])])
 
     def lines(h):
-        o, w = 128 * h, slice(8 * h, 8 * h + 8)
-        v("scan", ["GM", "k5"], ["SP%d" % h], T.SP[:, o:o + 128], T.GM[:, 0:128], T.k5[:, o:o + 128], 0.0, OP.add, OP.max)
-        sp = T.SP[:, o + 15:o + 128:16]
-        ts(["SP%d" % h, "corr"], "pL%d" % h, T.pL[:, w], sp, c("corr"), 8191.0, OP.subtract, OP.min)
-        act(PTs + ["pL%d" % h], ["PG%d" % h], T.PG[:, o:o + 128], T.PT[:].indirect(T.pL[:, w]))
-        act(AA + ["pL%d" % h], ["Ap%d" % h], T.Ap[:, o:o + 128], T.A[:].indirect(T.pL[:, w]))
-        ts(["SP%d" % h, "corr"], "pWf%d" % h, T.pWf[:, w], sp, c("corr"), 8191.0, OP.subtract, OP.min)
-        v("tc", ["k5"], ["pR%d" % h], T.pR[:, o:o + 128], T.k5[:, o:o + 128])
+        kk, o, w = half(h)
+        v("scan", ["GM", "k5"], ["SP%d" % h], T.SP[:, o], T.GM[:, 0:128], T.k5[:, o], 0.0, OP.add, OP.max)
+        sp = T.SP[:, 128 * h + 15:128 * h + 128:16]
+        ts(["SP%d" % h, "corr"], "pL%d" % h, T.pL[:, w], sp, c("corr"), float(NONE), OP.subtract, OP.min)
+        v("tc", ["k5"], ["pR%d" % h], T.pR[:, o], T.k5[:, o])
+        ts(["SP%d" % h, "corr"], "pWf%d" % h, T.pWf[:, w], sp, c("corr"), float(NONE), OP.subtract, OP.min)
 
-    def write_banks():
-        v("tt", ["nx", "ta", "wU"], VV, T.NV[:].indirect(T.wU[:]), T.nx[:], T.ta[:], OP.add)
+    def payees(h):
+        kk, o, w = half(h)
+        act(AA + ["pL%d" % h], ["Ap%d" % h], T.Ap[:, o], T.A[:].indirect(T.pL[:, w]))
+        act(PTs + ["pL%d" % h], ["PG%d" % h], T.PG[:, o], T.PT[:].indirect(T.pL[:, w]))
 
-    for s in range(STEPS):
-        last = s == STEPS - 1
-        if s == 0:
-            mm(["sel8", "wkH"], ["k0"], T.k0[:, 0:256], T.sel8[:], T.wkH[:])
-            carry, ck = T.c0, ["c0"]
-        else:
-            mm(["WBm", "LB%d" % s, "LB%do" % s], ["k0"], T.k0[:, 0:256], T.WBm[:], T["LB%d" % s][:])
-            carry, ck = T["LD%d" % s], ["LD%d" % s, "LD%do" % s]
-        v("scan", ["GM", "k0"], ["SC"], T.SC[:], T.GM[:], T.k0[:, 0:256], 0.0, OP.add, OP.max)
-        ts(["SC", "corr"], "WL", T.WL[:], T.SC[:, 15::16], c("corr"), None, OP.subtract)
-        v("tc", QQ + ["WL"], ["nU"], T.nU[:], T.Q[:].indirect(T.WL[:]))
-        if s:
-            write_banks()
-        v("tt", VV + ["WL"] + ck, ["y"], T.y[:], T.NV[:].indirect(T.WL[:]), carry[:], OP.add)
-        ts(["y"], "nx", T.nx[:], T.y[:], 255.0, None, OP.min)
-        mm(["Ib", "nx"], ["k1"], T.k1[:, 0:256], T.Ib[:], T.nx[:])
-        if s == 0:
-            consts2()
-        v("tc", ["k0"], ["bR"], T.bR[:], T.k0[:, 0:256])
-        ts(["SC", "corr"], "Wf", T.Wf[:], T.SC[:, 15::16], c("corr"), None, OP.subtract)
-        amounts(0)
-        act(["nx"], ["mm"], T.mm[:], T.nx[:], AF.Relu)
-        mm(["BLKb", "mm"], ["k5"], T.k5[:, 256:512], T.BLKb[:], T.mm[:])
-        dd_open()
-        for h in range(16):
-            dd_block(h, 16 * h, 256, "bR", T.bR, "Wf", T.Wf, h == 15)
-        v("tc", ["nU"], ["nF"], T.nF[:], T.nU[:])
-        amounts(1)
-        act(["k5"], ["D2"], T.D2[:], T.k5[:, 256:512], AF.Sign, bias=-0.5)
-        amounts(2)
-        act(["k2"], ["D1"], T.D1[:], T.k2[:, 0:256], AF.Sign)
-        amounts(3)
-        compare(0, 128)
-        best(0)
-        compare(128, 192)
-        rows(0, "v")
-        v("scan", ["GM2", "D1"], ["SD"], T.SD[:], T.GM2[:], T.D1[:], 0.0, OP.add, OP.max)
-        pick(0)
+    def missing(h):
+        kk, o, w = half(h)
+        d = drk[h]
+        acc(d, T[d][:, 0:128], [(["Ib", "mm"], T.Ib[:], T.mm[:, o]), (["NIb", "Ap%d" % h], T.NIb[:], T.Ap[:, o])])
+        act([d], ["r%d" % h], T.r[:, o], T[d][:, 0:128], AF.Relu)
+
+    def packed(h, last):
+        kk, o, w = half(h)
+        d = drk[h]
+        acc(d, T[d][:, 128:256], [(["Ib", "mm"], T.Ib[:], T.mm[:, o]), (["WBm", "PG%d" % h], T.WBm[:], T.PG[:, o]), (["NIb", "r%d" % h], T.NIb[:], T.r[:, o])])
+        act([d], ["Xs%d" % h], T.Xs[:, o], T[d][:, 128:256])
+        if not last:
+            act([d], ["An%d" % h], T.An[:, o], T[d][:, 0:128], AF.Relu, scale=-1.0)
+
+    def ranks(h):
+        kk, o, w = half(h)
+        mm(["DG", "PG%d" % h], [ddk[h]], T[ddk[h]][:, o], T.DG[:], T.PG[:, o], False, True)
+
+    def counts(h):
+        kk, o, w = half(h)
+        u = slice(256 + 128 * h, 384 + 128 * h)
+        v("tt", [ddk[h], "thr2"], ["OA%d" % h], T.OA[:, o], T[ddk[h]][:, o], T.thr2[:, o], OP.is_lt)
+        v("scan", ["OA%d" % h, "STEP", "icol", "k7"], ["k7"], T.k7[:, o], T.OA[:, o], T.STEP[:, 0:128], T.k7[:, 127:128] if h else c("icol"), OP.add, OP.subtract)
+        v("tt", ["k7", "OA%d" % h], ["Z%d" % h], T.Z[:, o], T.k7[:, o], T.OA[:, o], OP.mult)
+        acc(ddk[h], T[ddk[h]][:, u], [(["B4n", "OA%d" % h], T.B4n[:], T.OA[:, o]), (["BLKh", "Z%d" % h], T.BLKh[:], T.Z[:, o])])
+
+    def slots(h):
+        kk, o, w = half(h)
+        v("scan", ["GM", ddk[h]], ["SS%d" % h], T.SS[:, o], T.GM[:, 0:128], T[ddk[h]][:, 256 + 128 * h:384 + 128 * h], 0.0, OP.add, OP.max)
+        ts(["SS%d" % h, "corr"], "sL%d" % h, T.sL[:, w], T.SS[:, 128 * h + 15:128 * h + 128:16], c("corr"), None, OP.subtract)
+
+    def place(s, h):
+        kk, o, w = half(h)
+        v("tc", ["Xs%d" % h, "sL%d" % h], ["XW"], T.XW[:, 1024 * s:1024 * s + XWIN].indirect(T.sL[:, w]), T.Xs[:, o])
+
+    def bank_list():
+        v("scan", ["GM2", "D10", "D11"], ["SD"], T.SD[:], T.GM2[:], T.D1[:], 0.0, OP.add, OP.max)
         ts(["SD", "los"], "wa", T.wa[:], T.SD[:, 15::16], c("los"), None, OP.is_equal)
         v("tt", ["wa", "LC"], ["wa"], T.wa[:], T.wa[:], T.LC[:], OP.mult)
         v("tt", ["wa", "Wf"], ["wa"], T.wa[:], T.wa[:], T.Wf[:], OP.max)
-        v("tc", ["wa"], ["wU"], T.wU[:], T.wa[:])
-        compare(192, 256)
-        best(1)
-        rows(1, "s")
-        lines(0)
-        mm(["Ib", "mm"], ["k3"], T.k3[:, 256:512], T.Ib[:], T.mm[:])
-        dd_open()
-        pick(1)
-        for h in range(8):
-            dd_block(h, 16 * h, 128, "pR0", T.pR, "pWf0", T.pWf)
-        lines(1)
-        mm(["DG", "PG0", "PG1"], ["k2"], T.k2[:, 0:256], T.DG[:], T.PG[:], False, False)
-        for h in range(8):
-            dd_block(h, 128, 256, "pR1", T.pR, "pWf0", T.pWf)
-        for h in range(8, 16):
-            dd_block(h, 16 * h, 256, "pR1", T.pR, "pWf1", T.pWf, h == 15)
-        v("tt", ["Ap0", "Ap1", "k3"], ["t"], T.t[:], T.Ap[:], T.k3[:, 256:512], OP.min)
-        ts(["k2", "j4"], "OA", T.OA[:], T.k2[:, 0:256], 0.0, c("j4"), OP.is_lt, OP.mult)
-        mm(["BLK4n", "OA"], ["k1"], T.k1[:, 0:256], T.BLK4n[:], T.OA[:])
+        ts(["wa"], "wU", T.wU[:], T.wa[:], float(B), None, OP.subtract)
+
+    def best_row(h):
+        kk, o, w = half(h)
+        act([kk], ["Mb%d" % h], T.Mb[:, o], T[kk][:, 256:384])
+
+    def drawn(h, last):
+        kk, o, w = half(h)
         if not last:
-            mm(["BLK4k", "OA"], ["k4"], T.k4[:, 256:512], T.BLK4k[:], T.OA[:])
-            act(["k4"], ["aS"], T.aS[:], T.k4[:, 256:512])
-        mm(["ONEh", "rowl"], ["k0"], T.k0[:, 256:512], T.ONEh[0:1, :], T.rowl[0:1, :], True, False)
-        v("scan", ["OA", "ONEb", "icol"], ["k7"], T.k7[:, 0:256], T.OA[:], T.ONEb[:], c("icol"), OP.add, OP.subtract)
-        v("tt", ["k7", "OA"], ["Z"], T.Z[:], T.k7[:, 0:256], T.OA[:], OP.mult)
-        mm(["BLKh", "Z"], ["k0"], T.k0[:, 256:512], T.BLKh[:], T.Z[:], False, True)
-        v("tt", ["k1", "t"], ["ta"], T.ta[:], T.k1[:, 0:256], T.t[:], OP.mult)
-        v("scan", ["GM", "k0"], ["SS"], T.SS[:], T.GM[:], T.k0[:, 256:512], 0.0, OP.add, OP.max)
-        ts(["SS", "corr"], "sL", T.sL[:], T.SS[:, 15::16], c("corr"), None, OP.subtract)
-        wb, wc, lb, lc = "WB%d" % s, "WC%d" % s, "LB%d" % (s + 1), "LD%d" % (s + 1)
-        v("tc", ["PG0", "PG1", "sL"], [wb], T[wb][:].indirect(T.sL[:]), T.PG[:])
-        exchange(wb, lb, "rb%d" % s, "lb")
-        v("tc", ["t", "sL"], [wc], T[wc][:].indirect(T.sL[:]), T.t[:])
-        exchange(wc, lc, "rc%d" % s, "lc")
-        if last:
-            write_banks()
+            acc(kk, T[kk][:, 384:512], [(["I8k", "Mb%d" % h], T.I8k[:], T.Mb[:, o]), (["B4q", "OA%d" % h], T.B4q[:], T.OA[:, o])])
+        acc(kk, T[kk][:, 128:256], [(["Ib", "mm"], T.Ib[:], T.mm[:, o]), (["NIb", "r%d" % h], T.NIb[:], T.r[:, o]), (["B4a", "OA%d" % h], T.B4a[:], T.OA[:, o])])
+        act([kk], ["tp%d" % h], T.tp[:, o], T[kk][:, 128:256], AF.Relu, bias=-512.0)
+
+    def new_rows(h):
+        kk, o, w = half(h)
+        v("tt", [kk, "nF"], ["qn%d" % h], T.qn[:, o], T[kk][:, 384:512], T.nF[:, o], OP.max)
+
+    def write_rows(h):
+        kk, o, w = half(h)
+        act(["qn%d" % h, "wU"], QQ, T.Q[:].indirect(T.wU[:, w]), T.qn[:, o], AF.Silu)
+
+    def write_banks(h):
+        kk, o, w = half(h)
+        acc(kk, T[kk][:, 0:128], [(["Ib", "x"], T.Ib[:], T.x[:, o]), (["Ib", "tp%d" % h], T.Ib[:], T.tp[:, o])])
+        act([kk], ["vn%d" % h], T.vn[:, o], T[kk][:, 0:128], AF.Identity, bias=VO)
+        act(["vn%d" % h, "wU"], VT, T.VT[:].indirect(T.wU[:, w]), T.vn[:, o], AF.Silu)
+
+    def bank_offsets(s):
+        v("scan", ["GM", "L%d" % s, "L%do" % s], ["SC"], T.SC[:], T.GM[:], T["L%d" % s][:], 0.0, OP.add, OP.max)
+        ts(["SC", "corr"], "WL", T.WL[:], T.SC[:, 15::16], c("corr"), 1 / 512, OP.subtract, OP.mult)
+
+    def queue_rows():
+        ts(QQ + ["WL"], "nU", T.nU[:], T.Q[:].indirect(T.WL[:]), 0.25, None, OP.add)
+
+    def old_positions(s):
+        if s:
+            act(VT + ["WL"], ["Vg"], T.Vg[:], T.VT[:].indirect(T.WL[:]), AF.Identity, bias=-EMPTY)
         else:
-            ts(["SS", "corr"], "pa", T.pa[:], T.SS[:, 15::16], c("corr"), 1024.0, OP.subtract, OP.is_ge)
-            v("tt", ["pa", "LC2"], ["pa"], T.pa[:], T.pa[:], T.LC2[:], OP.mult)
-            v("tt", ["pa", "pWf0", "pWf1"], ["pa"], T.pa[:], T.pa[:], T.pWf[:], OP.max)
-            v("tc", ["pa"], ["pU"], T.pU[:], T.pa[:])
-            v("tt", ["Ap0", "Ap1", "ta", "pU"], AA, T.A[:].indirect(T.pU[:]), T.Ap[:], T.ta[:], OP.add)
-            v("tt", ["k6", "aS"], ["qa"], T.qa[:], T.k6[:, 256:512], T.aS[:], OP.mult)
-            v("tt", ["qa", "nF", "wU"], QQ, T.Q[:].indirect(T.wU[:]), T.qa[:], T.nF[:], OP.max)
-    ts(VV, "Vin", T.Vin[:], T.NV[:, 0:B], -1.0, None, OP.mult)
-    dma("y", ["Vin"], ["yv"], T.yv[:], T.Vin[:])
-    dma("y", ["LD4", "LD4o"], ["yc"], T.yc[:], T.LD4[:])
-    mm(["WBm", "LB4", "LB4o"], ["k0"], T.k0[:, 0:256], T.WBm[:], T.LB4[:])
-    ts(["k0"], "SC", T.SC[:], T.k0[:, 0:256], float(B), None, OP.min)
-    dma("s", ["SC"], ["yw"], T.yw[:], T.SC[0:128:16, :])
-    total["lb"], total["lc"] = nlocal["lb"], nlocal["lc"]
+            ts(VV + ["WL"], "Vg", T.Vg[:], T.V[:].indirect(T.WL[:]), VO - EMPTY, None, OP.add)
+
+    def bank_twins(h0, h1):
+        for h in range(h0, h1):
+            twins(h, 16 * h, 256, "bR", T.bR, "Wf", T.Wf, {7: [0], 15: [1]}.get(h, []))
+
+    def line_twins(half_, h0, h1):
+        for h in range(h0, h1):
+            twins(h, max(128 * half_, 16 * h), 128 * half_ + 128, "pR%d" % half_, T.pR, "pWf%d" % (h // 8), T.pWf)
+
+    def convert(s):
+        if s == 0:
+            fill("VTp", T.VT[:, B:VW], VW - B, VO)
+            act(["Vm"], ["VTm"], T.VT[:, 0:B], T.V[:, 0:B], AF.Identity, bias=VO)
+        if s == STEPS - 1:
+            act(VT, ["Vr"], T.Vr[:], T.VT[:, 0:B], AF.Identity, bias=MAGIC)
+            act(["Vr"], ["Vm"], T.V[:, 0:B], T.Vr[:], AF.Identity, bias=-MAGIC - VO)
+
+    def line_list():
+        ts(["pWf0", "pWf1", "pco"], "pWc", T.pWc[:], T.pWf[:], c("pco"), None, OP.add)
+        v("tt", ["SS0", "SS1", "pWc"], ["pa"], T.pa[:], T.SS[:, 15::16], T.pWc[:], OP.max)
+        ts(["pa", "pco"], "pU", T.pU[:], T.pa[:], c("pco"), None, OP.subtract)
+
+    def write_lines(last):
+        if last:
+            v("tt", ["x", "tp0", "tp1", "wU"], VV, T.V[:].indirect(T.wU[:]), T.x[:], T.tp[:], OP.add)
+        else:
+            v("tc", ["An0", "An1", "pU"], AA, T.A[:].indirect(T.pU[:]), T.An[:])
+
+    def stage(name, s):
+        last = s == STEPS - 1
+        kind, n = name[:2], int(name[2:] or 0)
+        if last and kind in ("br", "nr", "wr", "wb", "ll", "bo", "qr", "op", "up", "wf"):
+            return
+        {"bo": lambda: bank_offsets(s + 1), "qr": queue_rows, "op": lambda: old_positions(s + 1), "up": lambda: unpack(s + 1),
+         "wf": lambda: ts(["WL"], "Wf", T.Wf[:], T.WL[:], float(B), None, OP.add),
+         "am": lambda: amounts(n), "bt": lambda: bank_twins(4 * n, 4 * n + 4), "po": positions, "cm": lambda: compare(n // 2, n % 2),
+         "nf": lambda: v("tc", ["nU"], ["nF"], T.nF[:], T.nU[:]),
+         "dz": lambda: ts(["k5"], "D2", T.D2[:], T.k5[:, 256:512], 0.5, None, OP.is_lt),
+         "lo": lambda: losers(n), "bl": bank_list, "we": lambda: weigh(n), "pk": lambda: pick(n), "ln": lambda: lines(n),
+         "py": lambda: payees(n), "ms": lambda: missing(n), "lt": lambda: line_twins(min(n // 2, 1), 4 * n - 8 * (n > 1), 4 * n - 8 * (n > 1) + 4),
+         "rk": lambda: ranks(n), "pc": lambda: packed(n, last), "es": lambda: empty_slots(s), "br": lambda: best_row(n),
+         "ct": lambda: counts(n), "sl": lambda: slots(n), "dr": lambda: drawn(n, last), "pl": lambda: place(s, n),
+         "nr": lambda: new_rows(n), "wr": lambda: write_rows(n), "wb": lambda: write_banks(n), "cv": lambda: convert(s),
+         "ex": lambda: exchange(s), "ll": line_list, "wl": lambda: write_lines(last)}[kind]()
+
+    for name in HEAD.split():
+        stage(name, -1)
+    for s in range(STEPS):
+        for name in ORDER.split():
+            stage(name, s)
+
+    for s in []:
+        last = s == STEPS - 1
+        L, Lk = T["L%d" % s], ["L%d" % s, "L%do" % s]
+        v("scan", ["GM"] + Lk, ["SC"], T.SC[:], T.GM[:], L[:], 0.0, OP.add, OP.max)
+        ts(["SC", "corr"], "WL", T.WL[:], T.SC[:, 15::16], c("corr"), 1 / 512, OP.subtract, OP.mult)
+        ts(QQ + ["WL"], "nU", T.nU[:], T.Q[:].indirect(T.WL[:]), 0.25, None, OP.add)
+        if s:
+            act(VT + ["WL"], ["Vg"], T.Vg[:], T.VT[:].indirect(T.WL[:]), AF.Identity, bias=-EMPTY)
+        else:
+            act(VV + ["WL"], ["Vg"], T.Vg[:], T.V[:].indirect(T.WL[:]), AF.Identity, bias=VO - EMPTY)
+        unpack(s)
+        ts(["WL"], "Wf", T.Wf[:], T.WL[:], float(B), None, OP.add)
+        for k in range(3):
+            amounts(k)
+        for h in range(16):
+            twins(h, 16 * h, 256, "bR", T.bR, "Wf", T.Wf, {7: [0], 15: [1]}.get(h, []))
+            if h == 3:
+                positions()
+        compare(0)
+        v("tc", ["nU"], ["nF"], T.nF[:], T.nU[:])
+        ts(["k5"], "D2", T.D2[:], T.k5[:, 256:512], 0.5, None, OP.is_lt)
+        compare(1)
+        weigh(0)
+        amounts(3)
+        losers(0)
+        losers(1)
+        compare(2)
+        pick(0)
+        lines(0)
+        payees(0)
+        compare(3)
+        missing(0)
+        weigh(1)
+        for h in range(8):
+            twins(h, 16 * h, 128, "pR0", T.pR, "pWf0", T.pWf)
+        ranks(0)
+        pick(1)
+        packed(0, last)
+        counts(0)
+        lines(1)
+        payees(1)
+        empty_slots(s)
+        for h in range(16):
+            twins(h, max(128, 16 * h), 256, "pR1", T.pR, "pWf%d" % (h // 8), T.pWf)
+            if h == 7:
+                missing(1)
+        ranks(1)
+        packed(1, last)
+        bank_list()
+        if s == 0:
+            fill("VTp", T.VT[:, B:VW], VW - B, VO)
+            act(["Vm"], ["VTm"], T.VT[:, 0:B], T.V[:, 0:B], AF.Identity, bias=VO)
+        if last:
+            act(VT, ["Vr"], T.Vr[:], T.VT[:, 0:B], AF.Identity, bias=MAGIC)
+            act(["Vr"], ["Vm"], T.V[:, 0:B], T.Vr[:], AF.Identity, bias=-MAGIC - VO)
+        else:
+            best_row(0)
+            best_row(1)
+        counts(1)
+        slots(0)
+        drawn(0, last)
+        place(s, 0)
+        slots(1)
+        place(s, 1)
+        drawn(1, last)
+        exchange(s)
+        if last:
+            v("tt", ["x", "tp0", "tp1", "wU"], VV, T.V[:].indirect(T.wU[:]), T.x[:], T.tp[:], OP.add)
+        else:
+            for h in range(2):
+                new_rows(h)
+                write_rows(h)
+            ts(["pWf0", "pWf1", "pco"], "pWc", T.pWc[:], T.pWf[:], c("pco"), None, OP.add)
+            v("tt", ["SS0", "SS1", "pWc"], ["pa"], T.pa[:], T.SS[:, 15::16], T.pWc[:], OP.max)
+            ts(["pa", "pco"], "pU", T.pU[:], T.pa[:], c("pco"), None, OP.subtract)
+            v("tc", ["An0", "An1", "pU"], AA, T.A[:].indirect(T.pU[:]), T.An[:])
+            for h in range(2):
+                write_banks(h)
+    dma("y", VV, ["yv"], T.yv[:], T.V[:, 0:B])
+    unpack(STEPS)
+    ts(["bR"], "yw32", T.yw32[:], T.bR[:], float(B), None, OP.subtract)
+    dma("y", ["yw32"], ["yw"], T.yw[:], T.yw32[0:128:16, :])
+    act(["k0"], ["cb"], T.cb[:], T.k0[:, 0:256], AF.Identity, bias=EMPTY)
+    dma("s", ["cb"], ["yc"], T.yc[:], T.cb[:])
     for sem in sorted(total):
         need_wait("g", sem, total[sem])

@@ -8,11 +8,19 @@ VO = 1600.0
 VW, AW, XWIN = 1536, LO + 8464, LO + 9488
 EMPTY = 512.0 * B
 LIFT = 2.0 ** 20
-KILL = 2.0 ** 70
+RHO, TOP = 1.75, 2.0 ** 88
+KILL = 2.0 ** 90
 MAGIC = 1.5 * 2.0 ** 23
-HEAD = "bo qr up wf op"
-ORDER = """bt0 po bt1 am0 am1 cm0 cm1 bt2 bt3 dz cm2 am2 cm3 we0 lo0 nf cm4 pk0 am3 cm5 ln0 cm6 br0 cm7 lt0 py0 we1 lt1 lo1 rk0 pk1 ms0 ct0 es
-    ln1 pc0 lt2 py1 lt3 lt4 ms1 lt5 sl0 rk1 pc1 cv dr0 bl br1 ct1 pl0 sl1 pl1 wb0 nr0 ll ex dr1 nr1 wr0 wl bo wr1 qr wb1 op up wf"""
+ONS = "d2".split()
+SHARED = ()
+HEAD = "bo0a bo0b qr up wf lc op"
+FIRST = "bo0a bo0b qr up wf lc bt0 bt1 bt2 bt3 nf lo bl0a bl0b bl0c bl0d bl0e am0 am4 op"
+HELP = [0, 0, 0, 0]
+BATCH = 2
+WIDE = (0, 1, 2, 3)
+ORDER = """am0 bt0 po0a bt1 po0b bt2 nf am1 bt3 po0c cb3 lo am2 cb2 am3 cb0 cb1 ca6 ca5 we0 ca7 dz cb7 cv0 cb5 pk0a cb6 pk0b ca4 cb4 we1 bl0a ln0a ln0b ln0c
+    ln0d lt0 lt1 pk1a bl0b py0 rk0 pk1b ct0a ct0b cv1 ln1a br2 ln1b bk0 ct0c lt2 bl0c ln1c ln1d lt3 lt4 py1 lt5 bl0d rk1 sl0a tm1 tm0 sl0b ct1a ct1b bk1 ct1c pl0
+    sl1a sl1b pl1 dr ll0a nr an bl0e ll0b ex wr wb ll0c wl bo0a bo0b qr up wf op"""
 SCRATCH = {}
 
 
@@ -28,24 +36,25 @@ _buf("int32", B, "Qin")
 _buf("bfloat16", AW, "A")
 _buf("bfloat16", LO + 8192, "PT")
 _buf("float32", 1024 * (STEPS - 1) + XWIN, "XW")
-_buf("int32", 512, "payS payL")
+_buf("int32", 512, "payS")
 _buf("float32", 512, "payF payA")
 _buf("bfloat16", 2560, "payB")
-_buf("bfloat16", 1024, "WT ONE")
+_buf("bfloat16", 1024, "ONE cS")
 _buf("int32", 256, "wkI", 8)
 _buf("float16", 256, "wkH", 8)
 _buf("float16", 128, "sel8", 8)
-_buf("float32", 128, "imp qg BLKf If u1 u2")
+_buf("float32", 128, "imp qg BLKf BLKg If")
+_buf("bfloat16", 128, "u1 u2 u3 B256 MONE H8")
 _buf("float32", 144, "ebi")
-_buf("bfloat16", 144, "EB")
-_buf("float32", 256, "SC SP SS nF np Xs qn vn Vg yw32")
+_buf("bfloat16", 144, "EB EBh")
+_buf("float32", 256, "SC SP SS nF np Xb t qn vn Vg yw32 FALL")
 _buf("int32", 8, "pc pj pg pb")
-_buf("float32", 48, "cf")
-_buf("float32", 16, "l16 LC Wf wa pWf pWc pa")
+_buf("float32", 64, "cf")
+_buf("float32", 16, "l16 LC Wf wa pWf pa")
 _buf("uint16", 16, "WL wU pL sL pU")
 _buf("float16", 128, "N512 BLKh")
-_buf("bfloat16", 128, "Ib NIb BLKb B512 B4a B4q B4n I8k DG WBm HALF ZERO BIGW TRI")
-_buf("bfloat16", 256, "tt GM GM2 STEP thr thr2 SD x mm D1 D2 e Mb PG Ap r An tp OA cb")
+_buf("bfloat16", 128, "Ib NIb N32 BLKb B512 B4a B4q B4n I8k DG WBm WT TRI")
+_buf("bfloat16", 256, "tt GM GM2 STEP ZERO thr thr2 SD x mm D1 D2 e Mb PG Ap An tp OA cb")
 _buf("float16", 256, "Z bR y")
 _buf("uint16", 256, "nU pR")
 _buf("bfloat16", 4096, "eq G cmp")
@@ -153,8 +162,8 @@ def rank_program(g, core, T, topo):
         op("t", "mm", R, W, out, lhsT, rhs, start, stop)
 
     def acc(bank, out, terms):
-        for k, (R, lhsT, rhs) in enumerate(terms):
-            mm(R, [bank], out, lhsT, rhs, k == 0, k == len(terms) - 1)
+        for k, (m, R, rhs) in enumerate(terms):
+            mm([m] + R, [bank], out, T[m][:], rhs, k == 0, k == len(terms) - 1)
 
     dma("y", [], ["wkI"], T.wkI[:], T.wk[:])
     dma("y", [], ["payS"], T.payS[:], T.pay[:])
@@ -171,6 +180,8 @@ def rank_program(g, core, T, topo):
     iota("l16", T.l16[:], [[16, 16]], 0, 0)
     iota("ebi", T.ebi[:], [[1, 144]], -15, 0)
     iota("PTa", T.PT[:, 0:LO + 4096], [[0, LO + 4096]], 1, 0)
+    for s in range(STEPS):
+        iota("XE%d" % s, T.XW[:, 1024 * s:1024 * s + 832], [[0, 832]], int(EMPTY), 0)
 
     col = {}
 
@@ -181,31 +192,31 @@ def rank_program(g, core, T, topo):
         col[name] = len(col)
         v(call, R, [name], c(name), *a)
 
-    def byrow(name, parts):
-        for n, (cmp, k, val) in enumerate(parts):
-            colop("%s_%d" % (name, n), ["jf"], "ts", c("jf"), float(k), float(val), cmp, OP.mult)
-        col[name] = col[name + "_0"]
-        lastw[name] = lastw[name + "_0"]
-        for n in range(1, len(parts)):
-            act([name, "%s_%d" % (name, n)], [name], c(name), c(name), AF.Identity, bias=c("%s_%d" % (name, n)))
+    def byrow(table):
+        for is_ in sorted({t[:2] for name, start, terms in table for t in terms}):
+            colop("%s%d" % is_, ["jf"], "ts", c("jf"), float(is_[1]), None, {"lt": OP.is_lt, "eq": OP.is_equal, "ge": OP.is_ge}[is_[0]])
+        for n in range(max(len(terms) for name, start, terms in table)):
+            for name, start, terms in table:
+                if n < len(terms):
+                    is_, plus = "%s%d" % terms[n][:2], "%s_%d" % (name, n - 1) if n else start
+                    colop(name if n == len(terms) - 1 else "%s_%d" % (name, n), [is_, plus], "ts", c(is_), float(terms[n][2]),
+                          c(plus) if plus in col else plus, OP.mult, OP.add)
 
     def fill(W, out, n, val):
         act(["ONE"], [W], out, T.ONE[:, 0:n], AF.Copy, scale=val)
 
     def scaled(name, src, by):
-        act([src] + ([by] if by in col else []), [name], T[name][:], T[src][:], AF.Copy, scale=c(by) if by in col else by)
+        ts([src, by], name, T[name][:], T[src][:], c(by) if by in col else by, None, OP.mult)
 
     v("ms", [], ["ONE"], T.ONE[:], 1.0)
     for k in range(4):
         fill("PTb%d" % k, T.PT[:, LO + 4096 + 1024 * k:LO + 5120 + 1024 * k], 1024, 1.0)
     v("ms", [], ["ZERO"], T.ZERO[:], 0.0)
-    v("ms", [], ["HALF"], T.HALF[:], 0.5)
+    v("ms", [], ["FALL"], T.FALL[:], 1 / RHO)
     v("ms", [], ["Vp"], T.V[:, B:VW], 0.0)
     v("ms", [], ["Apd"], T.A[:, LO + 8192:AW], 0.0)
     v("ms", [], ["Apl"], T.A[:, 0:LO], 0.0)
-    v("ms", [], ["Qp"], T.Q[:, B:VW], float(NONE))
-    for h in range(2):
-        v("scan", ["HALF", "ZERO"], ["thr"], T.thr[:, 128 * h:128 * h + 128], T.HALF[:], T.ZERO[:], 5.0 * 2.0 ** 63, OP.mult, OP.add)
+    v("scan", ["FALL", "ZERO"], ["thr"], T.thr[:], T.FALL[:], T.ZERO[:], 2.54 * RHO * TOP, OP.mult, OP.add)
     ts(["pc"], "pj", T.pj[:, 0:1], T.pc[:, 0:1], 15, None, OP.bitwise_and)
     ts(["pc"], "pg", T.pg[:, 0:1], T.pc[:, 0:1], 4, None, OP.arith_shift_right)
     colop("jf", ["pj"], "tc", T.pj[:, 0:1])
@@ -217,75 +228,77 @@ def rank_program(g, core, T, topo):
     ts(["qg", "pf"], "sel8", T.sel8[:], T.qg[0:8, :], pf8, 512.0, OP.is_equal, OP.mult)
     v("tc", ["wkI"], ["wkH"], T.wkH[:], T.wkI[:])
     mm(["sel8", "wkH"], ["k0"], T.k0[:, 0:256], T.sel8[:], T.wkH[:])
-    ts(["qg", "gf"], "BLKb", T.BLKb[:], T.qg[:], c("gf"), None, OP.is_equal)
-    ts(["imp"], "Ib", T.Ib[:], T.imp[:], 0.0, None, OP.is_equal)
-    ts(["Ib"], "N512", T.N512[:], T.Ib[:], -512.0, None, OP.mult)
-    for k in range(4):
-        colop("f%d" % k, ["pb%d" % k], "ts", T.pb[:, k:k + 1], 2.0 ** -(2 ** k) - 1.0, 1.0, OP.mult, OP.add)
-    colop("f01", ["f0", "f1"], "tt", c("f0"), c("f1"), OP.mult)
-    colop("f23", ["f2", "f3"], "tt", c("f2"), c("f3"), OP.mult)
-    colop("pw", ["f01", "f23"], "tt", c("f01"), c("f23"), OP.mult)
-    colop("jh", ["jf"], "ts", c("jf"), 0.5, None, OP.add)
-    colop("corr", ["jf"], "ts", c("jf"), -LIFT, 15 * LIFT, OP.mult, OP.add)
-    colop("n15", ["jf"], "ts", c("jf"), 15.0, None, OP.is_lt)
-    ts(["tt", "jh"], "GM", T.GM[:], T.tt[:], c("jh"), 64 * LIFT, OP.subtract, OP.mult)
-    ts(["GM"], "GM", T.GM[:], T.GM[:], LIFT, None, OP.min)
     v("tc", ["payS"], ["payF"], T.payF[:], T.payS[:])
-    v("tc", ["k0"], ["L0"], T.L0[:], T.k0[:, 0:256])
     for k in range(3):
         act(["payF"], ["b%d" % k], T.payB[:, 512 * k:512 * k + 512], T.payF[:], AF.Sign, bias=0.5 - 1024 * (k + 1))
     act(["payF"], ["payA"], T.payA[:], T.payF[:], AF.Identity, bias=-15.5 / 32, scale=1 / 32)
-    ts(["payS"], "payL", T.payL[:], T.payS[:], 31, None, OP.bitwise_and)
-    v("tc", ["payL"], ["b4"], T.payB[:, 2048:2560], T.payL[:])
-    for k in range(8):
-        ts(["BLKb", "pw"], "WT%d" % k, T.WT[:, 128 * k:128 * k + 128], T.BLKb[:], c("pw"), 2.0 ** (63 - 16 * k), OP.mult, OP.mult)
-    ts(["payA"], "b3", T.payB[:, 1536:2048], T.payA[:], MAGIC, MAGIC, OP.add, OP.subtract)
+    fill("Qp", T.Q[:, B:VW], VW - B, float(NONE))
+    fill("VTp", T.VT[:, B:VW], VW - B, VO)
+    ts(["qg", "gf"], "BLKb", T.BLKb[:], T.qg[:], c("gf"), None, OP.is_equal)
+    ts(["imp"], "Ib", T.Ib[:], T.imp[:], 0.0, None, OP.is_equal)
+    for k in range(4):
+        colop("f%d" % k, ["pb%d" % k], "ts", T.pb[:, k:k + 1], RHO ** -(2 ** k) - 1.0, 1.0, OP.mult, OP.add)
+    colop("jh", ["jf"], "ts", c("jf"), 0.5, None, OP.add)
+    colop("corr", ["jf"], "ts", c("jf"), -LIFT, 15 * LIFT, OP.mult, OP.add)
+    colop("f01", ["f0", "f1", "f2"], "ts", c("f0"), c("f1"), c("f2"), OP.mult, OP.mult)
+    ts(["tt", "jh"], "GM", T.GM[:], T.tt[:], c("jh"), 64 * LIFT, OP.subtract, OP.mult)
+    v("tc", ["k0"], ["L0"], T.L0[:], T.k0[:, 0:256])
+    ts(["GM"], "GM", T.GM[:], T.GM[:], LIFT, None, OP.min)
+    ts(["BLKb", "f01", "f3"], "WT", T.WT[:], T.BLKb[:], c("f01"), c("f3"), OP.mult, OP.mult)
+    for name, by in (("N512", -512.0), ("If", 1.0), ("NIb", -1.0), ("N32", -32.0)):
+        scaled(name, "Ib", by)
+    ts(["Qin"], "Qm", T.Q[:, 0:B], T.Qin[:], float(LO), None, OP.add)
+    act(["payA"], ["payA"], T.payA[:], T.payA[:], AF.Identity, bias=MAGIC)
+    act(["payA"], ["b3"], T.payB[:, 1536:2048], T.payA[:], AF.Identity, bias=-MAGIC)
+    acc("k3", T.k3[:], [("If", ["payF"], T.payF[:]), ("N32", ["b3"], T.payB[:, 1536:2048])])
+    act(["k3"], ["b4"], T.payB[:, 2048:2560], T.k3[:])
+    colop("n15", ["jf"], "ts", c("jf"), 15.0, None, OP.is_lt)
     for k in range(3):
         end = T.payB[:, 512 * k + 511:512 * k + 512]
         ts(["b%d" % k, "n15"], "b%d" % k, end, end, c("n15"), None, OP.mult)
-    ts(["Qin"], "Qm", T.Q[:, 0:B], T.Qin[:], float(LO), None, OP.add)
     PTf = ["PTa"] + ["PTb%d" % k for k in range(4)]
     for j in range(5):
         dma("y", ["b%d" % j, "Am"] + PTf, ["PT%d" % j], T.PT[j::16, LO:LO + 8192], T.payB[:, 512 * j:512 * j + 512])
-    scaled("If", "Ib", 1.0)
-    scaled("NIb", "Ib", -1.0)
-    scaled("BIGW", "BLKb", KILL)
-    colop("g16", ["gf"], "ts", c("gf"), 16.0, None, OP.mult)
-    ts(["ebi", "g16"], "EB", T.EB[:], T.ebi[:], c("g16"), None, OP.is_equal)
-    colop("j4", ["jf"], "ts", c("jf"), 4.0, None, OP.is_lt)
-    colop("los", ["jf"], "ts", c("jf"), -2.0, 31.0, OP.mult, OP.add)
-    colop("pco", ["corr"], "ts", c("corr"), 1024.0, None, OP.add)
-    colop("n4", ["jf"], "ts", c("jf"), 4.0, None, OP.not_equal)
-    colop("j256", ["jf", "j4"], "ts", c("jf"), 256.0, c("j4"), OP.mult, OP.mult)
-    byrow("icol", [(OP.is_lt, 4, -1040 - LO), (OP.is_equal, 4, 1039 + LO), (OP.is_equal, 5, 8192)])
-    act(["icol", "j256"], ["icol"], c("icol"), c("icol"), AF.Identity, bias=c("j256"))
-    byrow("jw", [(OP.is_lt, 3, -512 * 512), (OP.is_equal, 3, 512 * 32), (OP.is_equal, 4, 512), (OP.is_equal, 5, -512 * 1536)])
-    byrow("jq", [(OP.is_lt, 4, 8192), (OP.is_equal, 4, LO - 8192)])
-    byrow("ja", [(OP.is_lt, 4, 512)])
-    byrow("jn", [(OP.is_lt, 4, -8192)])
-    byrow("jt", [(OP.is_ge, 4, 2.0 ** 90), (OP.is_ge, 6, -2.0 ** 91)])
-    byrow("dm", [(OP.is_lt, 3, -2 * KILL)])
-    byrow("da", [(OP.is_lt, 3, KILL), (OP.is_equal, 5, 3 * KILL)])
-    ts(["imp"], "u1", T.u1[:], T.imp[:], 0.0, 1.96875, OP.is_lt, OP.mult)
-    ts(["Ib"], "u2", T.u2[:], T.Ib[:], -1.03125, 0.03125, OP.mult, OP.add)
-    v("tt", ["u1", "u2"], ["u1"], T.u1[:], T.u1[:], T.u2[:], OP.add)
-    v("tt", ["u1", "BLKb"], ["TRI"], T.TRI[:], T.u1[:], T.BLKb[:], OP.mult)
-    ts(["tt", "jf"], "u2", T.u2[:], T.tt[:, 0:128], c("jf"), None, OP.is_gt)
-    ts(["u2", "dm", "da"], "u2", T.u2[:], T.u2[:], c("dm"), c("da"), OP.mult, OP.add)
-    v("tt", ["u2", "BLKb"], ["DG"], T.DG[:], T.u2[:], T.BLKb[:], OP.mult)
-    ts(["GM"], "GM2", T.GM2[:], T.GM[:], 2 / LIFT, -64.0, OP.mult, OP.max)
-    v("tc", ["BLKb"], ["BLKh"], T.BLKh[:], T.BLKb[:])
-    ts(["l16", "jf"], "LC", T.LC[:], T.l16[:], c("jf"), 1280.0 + B, OP.add, OP.add)
-    for name, by in (("B512", 512.0), ("BLKf", 1.0), ("WBm", "jw"), ("B4n", "jn"), ("B4a", "ja"), ("B4q", "jq")):
-        scaled(name, "BLKb", by)
-    scaled("I8k", "Ib", 8192.0)
-    act(["thr", "j4", "jt"], ["thr2"], T.thr2[:], T.thr[:], AF.Identity, bias=c("jt"), scale=c("j4"))
-    act(["ONE", "n4"], ["STEP"], T.STEP[:], T.ONE[:, 0:256], AF.Copy, scale=c("n4"))
 
-    def empty_slots(s):
-        for r in range(4):
-            at = 1024 * s + 256 * r
-            fill("XW", T.XW[:, at:at + 64], 64, EMPTY)
+    def later_constants():
+        colop("g16", ["gf"], "ts", c("gf"), 16.0, None, OP.mult)
+        if "d1" in ONS:
+            colop("los", ["jf"], "ts", c("jf"), 2.0 * 2048, -29.0 * 2048, OP.mult, OP.add)
+            scaled("B256", "BLKb", 256.0)
+            v("ms", [], ["MONE"], T.MONE[:], -1.0)
+        else:
+            colop("los", ["jf"], "ts", c("jf"), 2.0 * 4096, -30.0 * 4096, OP.mult, OP.add)
+        if "m0" in ONS or "m1" in ONS:
+            scaled("BLKg", "BLKb", 0.5)
+        colop("n4", ["jf"], "ts", c("jf"), 4.0, None, OP.not_equal)
+        colop("j256", ["jf"], "ts", c("jf"), 256.0, -1040.0 - LO, OP.mult, OP.add)
+        byrow([("icol", "j256", [("eq", 4, 2 * (1040 + LO) - 1025), ("eq", 5, 8192 + 1040 + LO - 1280)]),
+               ("jw", 0.0, [("lt", 3, -512 * 512), ("eq", 3, 512 * 32), ("eq", 4, 512), ("eq", 5, -512 * 1536)]),
+               ("jq", 0.0, [("lt", 4, 8192), ("eq", 4, LO - 8192)]),
+               ("jt", 0.0, [("ge", 4, 64 * KILL), ("ge", 6, -128 * KILL)]),
+               ("dm", 0.0, [("lt", 3, -2 * KILL)]), ("da", 0.0, [("lt", 3, KILL), ("eq", 5, 3 * KILL)])])
+        if SHARED:
+            ts(["tt"], "H8", T.H8[:], T.tt[:, 0:128], 4.0 * (min(SHARED) - 4), 0.5, OP.is_ge, OP.mult)
+        ts(["ebi", "g16"], "EB", T.EB[:], T.ebi[:], c("g16"), None, OP.is_equal)
+        ts(["ebi", "g16"], "EBh", T.EBh[:], T.ebi[:], c("g16"), 0.5, OP.is_equal, OP.mult)
+        ts(["imp"], "u1", T.u1[:], T.imp[:], 0.0, 1.96875, OP.is_lt, OP.mult)
+        ts(["Ib"], "u2", T.u2[:], T.Ib[:], -1.03125, 0.03125, OP.mult, OP.add)
+        ts(["tt", "jf"], "u3", T.u3[:], T.tt[:, 0:128], c("jf"), None, OP.is_gt)
+        ts(["GM"], "GM2", T.GM2[:], T.GM[:], 2 / LIFT, -64.0, OP.mult, OP.max)
+        ts(["l16", "jf"], "LC", T.LC[:], T.l16[:], c("jf"), 1280.0 + B, OP.add, OP.add)
+        for name, by in (("B512", 512.0), ("BLKf", 1.0), ("BLKh", 1.0), ("WBm", "jw"), ("B4q", "jq")):
+            scaled(name, "BLKb", by)
+        for name, by in (("B4n", -8192.0), ("B4a", 512.0)):
+            ts(["BLKb", "lt4"], name, T[name][:], T.BLKb[:], c("lt4"), by, OP.mult, OP.mult)
+        scaled("I8k", "Ib", 8192.0)
+        v("tt", ["u1", "u2"], ["u1"], T.u1[:], T.u1[:], T.u2[:], OP.add)
+        ts(["u3", "dm", "da"], "u3", T.u3[:], T.u3[:], c("dm"), c("da"), OP.mult, OP.add)
+        ts(["thr", "lt4", "jt"], "thr2", T.thr2[:], T.thr[:], c("lt4"), c("jt"), OP.mult, OP.add)
+        ts(["ONE", "n4"], "STEP", T.STEP[:], T.ONE[:, 0:256], c("n4"), None, OP.mult)
+        if SHARED:
+            v("tt", ["H8", "BLKb"], ["H8"], T.H8[:], T.H8[:], T.BLKb[:], OP.mult)
+        v("tt", ["u1", "BLKb"], ["TRI"], T.TRI[:], T.u1[:], T.BLKb[:], OP.mult)
+        v("tt", ["u3", "BLKb"], ["DG"], T.DG[:], T.u3[:], T.BLKb[:], OP.mult)
 
     PTs = PTf + ["PT%d" % j for j in range(5)]
     route = split_engines(topo, cores, core)
@@ -313,141 +326,16 @@ def rank_program(g, core, T, topo):
 
     AA, VV, QQ, VT = ["Am", "Apd", "Apl"], ["Vm", "Vp"], ["Qm", "Qp"], ["VTm", "VTp"]
     ddk = ["k2", "k6"]
-    drk = ["k0", "k1"]
 
     def half(h):
-        return "k%d" % (3 + h), slice(128 * h, 128 * h + 128), slice(8 * h, 8 * h + 8)
+        return (slice(128 * h, 128 * h + 128), slice(8 * h, 8 * h + 8)) if h < 2 else (slice(0, 256), slice(0, 16))
 
-    def twins(h, l0, l1, Rk, Rb, Wk, Wb, stop=()):
-        e, at = "eq%d_%d" % (h, l0 // 128), 256 * h + l0
-        ts([Rk, Wk], e, T.eq[:, at:at + l1 - l0], Rb[:, l0:l1], Wb[:, h:h + 1], None, OP.is_equal)
-        k = h % 8
-        for o in (0, 1):
-            a, b = max(l0, 128 * o), min(l1, 128 * o + 128)
-            if a < b:
-                same = h // 8 == o
-                mm(["WT%d" % k if same else "BIGW", e], [ddk[o]], T[ddk[o]][:, a:b], T.WT[:, 128 * k:128 * k + 128] if same else T.BIGW[:],
-                   T.eq[:, at + a - l0:at + b - l0], h == 0, o in stop)
-
-    def unpack(s):
-        L, Lk = T["L%d" % s], ["L%d" % s, "L%do" % s]
-        ts(Lk, "bR", T.bR[:], L[:], 1 / 512, float(B), OP.mult, OP.add)
-        acc("k0", T.k0[:, 0:256], [(Lk + ["If"], T.If[:], L[:]), (["N512", "bR"], T.N512[:], T.bR[:])])
-
-    def positions():
-        v("tt", ["Vg", "k0"], ["y"], T.y[:], T.Vg[:], T.k0[:, 0:256], OP.subtract)
-        ts(["y"], "x", T.x[:], T.y[:], VO, -255.0, OP.subtract, OP.max)
-        ts(["x"], "mm", T.mm[:], T.x[:], -1.0, 0.0, OP.mult, OP.max)
-        mm(["NIb", "x"], ["k1"], T.k1[:, 0:256], T.NIb[:], T.x[:])
-        mm(["BLKb", "mm"], ["k5"], T.k5[:, 256:512], T.BLKb[:], T.mm[:])
-
-    def amounts(k):
-        act(AA + ["nU"], ["g%d" % k], T.G[:, 1024 * k:1024 * k + 1024], T.A[:].indirect(T.nU[:, 64 * k:64 * k + 64]))
-
-    def compare(k, part):
-        l0, kk, m0 = 64 * k, "k%d" % (3 + k // 2), 64 * (k % 2)
-        for i in range(8 * part, 8 * part + 8):
-            at, ok = 256 * i + l0, "c%d_%d" % (i, k)
-            v("tt", ["g%d" % k, "k1"], [ok], T.cmp[:, at:at + 64], T.G[:, 16 * l0 + i:16 * l0 + 1024:16], T.k1[:, l0:l0 + 64], OP.is_ge)
-            mm([ok, "EB"], [kk], T[kk][:, m0:m0 + 64], T.EB[:, 15 - i:143 - i], T.cmp[:, at:at + 64], i == 0, i == 15)
-
-    def weigh(h):
-        kk, o, w = half(h)
-        act([kk], ["e%d" % h], T.e[:, o], T[kk][:, 0:128], AF.Silu, bias=-85.6, scale=4.6)
-        mm(["TRI", "e%d" % h], [kk], T[kk][:, 128:256], T.TRI[:], T.e[:, o])
-
-    def losers(h):
-        kk, o, w = half(h)
-        v("tt", [ddk[h], "thr"], ["D1%d" % h], T.D1[:, o], T[ddk[h]][:, o], T.thr[:, o], OP.is_ge)
-
-    def pick(h):
-        kk, o, w = half(h)
-        ts([kk], kk, T[kk][:, 256:384], T[kk][:, 128:256], 0.0, None, OP.is_gt)
-        v("tt", [kk, "nF"], ["np%d" % h], T.np[:, o], T[kk][:, 256:384], T.nF[:, o], OP.mult)
-        acc("k5", T.k5[:, o], [(["B512", "D1%d" % h], T.B512[:], T.D1[:, o]), (["B512", "D2"], T.B512[:], T.D2[:, o]), (["BLKf", "np%d" % h], T.BLKf[:], T.np[:, o])])
-
-    def lines(h):
-        kk, o, w = half(h)
-        v("scan", ["GM", "k5"], ["SP%d" % h], T.SP[:, o], T.GM[:, 0:128], T.k5[:, o], 0.0, OP.add, OP.max)
-        sp = T.SP[:, 128 * h + 15:128 * h + 128:16]
-        ts(["SP%d" % h, "corr"], "pL%d" % h, T.pL[:, w], sp, c("corr"), float(NONE), OP.subtract, OP.min)
-        v("tc", ["k5"], ["pR%d" % h], T.pR[:, o], T.k5[:, o])
-        ts(["SP%d" % h, "corr"], "pWf%d" % h, T.pWf[:, w], sp, c("corr"), float(NONE), OP.subtract, OP.min)
-
-    def payees(h):
-        kk, o, w = half(h)
-        act(AA + ["pL%d" % h], ["Ap%d" % h], T.Ap[:, o], T.A[:].indirect(T.pL[:, w]))
-        act(PTs + ["pL%d" % h], ["PG%d" % h], T.PG[:, o], T.PT[:].indirect(T.pL[:, w]))
-
-    def missing(h):
-        kk, o, w = half(h)
-        d = drk[h]
-        acc(d, T[d][:, 0:128], [(["Ib", "mm"], T.Ib[:], T.mm[:, o]), (["NIb", "Ap%d" % h], T.NIb[:], T.Ap[:, o])])
-        act([d], ["r%d" % h], T.r[:, o], T[d][:, 0:128], AF.Relu)
-
-    def packed(h, last):
-        kk, o, w = half(h)
-        d = drk[h]
-        acc(d, T[d][:, 128:256], [(["Ib", "mm"], T.Ib[:], T.mm[:, o]), (["WBm", "PG%d" % h], T.WBm[:], T.PG[:, o]), (["NIb", "r%d" % h], T.NIb[:], T.r[:, o])])
-        act([d], ["Xs%d" % h], T.Xs[:, o], T[d][:, 128:256])
-        if not last:
-            act([d], ["An%d" % h], T.An[:, o], T[d][:, 0:128], AF.Relu, scale=-1.0)
-
-    def ranks(h):
-        kk, o, w = half(h)
-        mm(["DG", "PG%d" % h], [ddk[h]], T[ddk[h]][:, o], T.DG[:], T.PG[:, o], False, True)
-
-    def counts(h):
-        kk, o, w = half(h)
-        u = slice(256 + 128 * h, 384 + 128 * h)
-        v("tt", [ddk[h], "thr2"], ["OA%d" % h], T.OA[:, o], T[ddk[h]][:, o], T.thr2[:, o], OP.is_lt)
-        v("scan", ["OA%d" % h, "STEP", "icol", "k7"], ["k7"], T.k7[:, o], T.OA[:, o], T.STEP[:, 0:128], T.k7[:, 127:128] if h else c("icol"), OP.add, OP.subtract)
-        v("tt", ["k7", "OA%d" % h], ["Z%d" % h], T.Z[:, o], T.k7[:, o], T.OA[:, o], OP.mult)
-        acc(ddk[h], T[ddk[h]][:, u], [(["B4n", "OA%d" % h], T.B4n[:], T.OA[:, o]), (["BLKh", "Z%d" % h], T.BLKh[:], T.Z[:, o])])
-
-    def slots(h):
-        kk, o, w = half(h)
-        v("scan", ["GM", ddk[h]], ["SS%d" % h], T.SS[:, o], T.GM[:, 0:128], T[ddk[h]][:, 256 + 128 * h:384 + 128 * h], 0.0, OP.add, OP.max)
-        ts(["SS%d" % h, "corr"], "sL%d" % h, T.sL[:, w], T.SS[:, 128 * h + 15:128 * h + 128:16], c("corr"), None, OP.subtract)
-
-    def place(s, h):
-        kk, o, w = half(h)
-        v("tc", ["Xs%d" % h, "sL%d" % h], ["XW"], T.XW[:, 1024 * s:1024 * s + XWIN].indirect(T.sL[:, w]), T.Xs[:, o])
-
-    def bank_list():
-        v("scan", ["GM2", "D10", "D11"], ["SD"], T.SD[:], T.GM2[:], T.D1[:], 0.0, OP.add, OP.max)
-        ts(["SD", "los"], "wa", T.wa[:], T.SD[:, 15::16], c("los"), None, OP.is_equal)
-        v("tt", ["wa", "LC"], ["wa"], T.wa[:], T.wa[:], T.LC[:], OP.mult)
-        v("tt", ["wa", "Wf"], ["wa"], T.wa[:], T.wa[:], T.Wf[:], OP.max)
-        ts(["wa"], "wU", T.wU[:], T.wa[:], float(B), None, OP.subtract)
-
-    def best_row(h):
-        kk, o, w = half(h)
-        act([kk], ["Mb%d" % h], T.Mb[:, o], T[kk][:, 256:384])
-
-    def drawn(h, last):
-        kk, o, w = half(h)
-        if not last:
-            acc(kk, T[kk][:, 384:512], [(["I8k", "Mb%d" % h], T.I8k[:], T.Mb[:, o]), (["B4q", "OA%d" % h], T.B4q[:], T.OA[:, o])])
-        acc(kk, T[kk][:, 128:256], [(["Ib", "mm"], T.Ib[:], T.mm[:, o]), (["NIb", "r%d" % h], T.NIb[:], T.r[:, o]), (["B4a", "OA%d" % h], T.B4a[:], T.OA[:, o])])
-        act([kk], ["tp%d" % h], T.tp[:, o], T[kk][:, 128:256], AF.Relu, bias=-512.0)
-
-    def new_rows(h):
-        kk, o, w = half(h)
-        v("tt", [kk, "nF"], ["qn%d" % h], T.qn[:, o], T[kk][:, 384:512], T.nF[:, o], OP.max)
-
-    def write_rows(h):
-        kk, o, w = half(h)
-        act(["qn%d" % h, "wU"], QQ, T.Q[:].indirect(T.wU[:, w]), T.qn[:, o], AF.Silu)
-
-    def write_banks(h):
-        kk, o, w = half(h)
-        acc(kk, T[kk][:, 0:128], [(["Ib", "x"], T.Ib[:], T.x[:, o]), (["Ib", "tp%d" % h], T.Ib[:], T.tp[:, o])])
-        act([kk], ["vn%d" % h], T.vn[:, o], T[kk][:, 0:128], AF.Identity, bias=VO)
-        act(["vn%d" % h, "wU"], VT, T.VT[:].indirect(T.wU[:, w]), T.vn[:, o], AF.Silu)
+    def of(name, h):
+        return [name + "0", name + "1"] if h == 2 else ["%s%d" % (name, h)]
 
     def bank_offsets(s):
         v("scan", ["GM", "L%d" % s, "L%do" % s], ["SC"], T.SC[:], T.GM[:], T["L%d" % s][:], 0.0, OP.add, OP.max)
+        yield
         ts(["SC", "corr"], "WL", T.WL[:], T.SC[:, 15::16], c("corr"), 1 / 512, OP.subtract, OP.mult)
 
     def queue_rows():
@@ -459,139 +347,248 @@ def rank_program(g, core, T, topo):
         else:
             ts(VV + ["WL"], "Vg", T.Vg[:], T.V[:].indirect(T.WL[:]), VO - EMPTY, None, OP.add)
 
-    def bank_twins(h0, h1):
-        for h in range(h0, h1):
-            twins(h, 16 * h, 256, "bR", T.bR, "Wf", T.Wf, {7: [0], 15: [1]}.get(h, []))
+    def unpack(s):
+        L, Lk = T["L%d" % s], ["L%d" % s, "L%do" % s]
+        ts(Lk, "bR", T.bR[:], L[:], 1 / 512, float(B), OP.mult, OP.add)
+        acc("k0", T.k0[:, 0:256], [("If", Lk, L[:]), ("N512", ["bR"], T.bR[:])])
 
-    def line_twins(half_, h0, h1):
-        for h in range(h0, h1):
-            twins(h, max(128 * half_, 16 * h), 128 * half_ + 128, "pR%d" % half_, T.pR, "pWf%d" % (h // 8), T.pWf)
+    def positions():
+        v("tt", ["Vg", "k0"], ["y"], T.y[:], T.Vg[:], T.k0[:, 0:256], OP.subtract)
+        yield
+        ts(["y"], "x", T.x[:], T.y[:], VO, -255.0, OP.subtract, OP.max)
+        acc("k1", T.k1[:, 0:256], [("NIb", ["x"], T.x[:])])
+        yield
+        ts(["x"], "mm", T.mm[:], T.x[:], -1.0, 0.0, OP.mult, OP.max)
+        acc("k5", T.k5[:, 256:512], [("BLKb", ["mm"], T.mm[:])])
+        acc("k7", T.k7[:, 256:512], [("Ib", ["mm"], T.mm[:])])
 
-    def convert(s):
-        if s == 0:
-            fill("VTp", T.VT[:, B:VW], VW - B, VO)
+    def twins(h0, lo, hi, Rk, Rb, Wk, Wb, stop=False):
+        for b in range(h0, h0 + 4, BATCH):
+            es = ["eq%d_%d" % (h, max(lo, 16 * h) // 128) for h in range(b, b + BATCH)]
+            for h in range(b, b + BATCH):
+                l0 = max(lo, 16 * h)
+                ts(Rk + [Wk], es[h - b], T.eq[:, 256 * h + l0:256 * h + hi], Rb[:, l0:hi], Wb[:, h:h + 1], TOP * RHO ** (-16 * h), OP.is_equal, OP.mult)
+            for h in range(b, b + BATCH):
+                l0 = max(lo, 16 * h)
+                mm(["WT"] + es, ["k2"], T.k2[:, l0:hi], T.WT[:], T.eq[:, 256 * h + l0:256 * h + hi], h == 0, stop and h == 15)
+
+    def bank_twins(n):
+        twins(4 * n, 0, 256, ["bR"], T.bR, "Wf", T.Wf, "d1" not in ONS)
+
+    def line_twins(n):
+        o, h0 = min(n // 2, 1), 4 * n - 8 * (n > 1)
+        twins(h0, 128 * o, 128 * o + 128, ["pR%d" % o], T.pR, "pWf%d" % (h0 // 8), T.pWf)
+
+    def all_line_twins(n):
+        twins(4 * n, 0, 256, of("pR", 2), T.pR, "pWf%d" % (n // 2), T.pWf)
+
+    def amounts(k, s):
+        a, b = (64 * k, min(64 * k + 64, 256 - HELP[s])) if k < 4 else (256 - HELP[s], 256)
+        if k < 4:
+            act(AA + ["nU"], ["g%d" % k], T.G[:, 16 * a:16 * b], T.A[:].indirect(T.nU[:, a:b]))
+        elif HELP[s]:
+            v("tc", AA + ["nU"], ["g4"], T.G[:, 16 * a:16 * b], T.A[:].indirect(T.nU[:, a:b]))
+
+    scored = [0, 0]
+
+    def compare(n, second):
+        h, wide = n // 4, n in WIDE
+        l0, w = (128 * h, 128) if wide else (128 * h + 64 * second, 64)
+        out = T.k3[:, half(h)[0]]
+        for i in range(4 * (n % 4), 4 * (n % 4) + 4):
+            if i % BATCH == 0 and n not in SHARED and (second or not wide):
+                for k in range(i, i + BATCH):
+                    v("tt", ["g%d" % (l0 // 64), "g%d" % (2 * h + second), "k1"] + ["g4"] * (h * second), ["c%d_%d" % (k, 2 * h + second)],
+                      T.cmp[:, 256 * k + l0:256 * k + l0 + w], T.G[:, 16 * l0 + k:16 * (l0 + w):16], T.k1[:, l0:l0 + w], OP.is_ge)
+            ck = ["c%d_%d" % (k, 2 * h + u) for k in range(i - i % BATCH, i - i % BATCH + BATCH) for u in range(2)]
+            if second:
+                scored[h] = scored[h] % 16 + 1
+                if scored[h] == 1 and h and SHARED:
+                    mm(["H8", "ONE"], ["k3"], out, T.H8[:], T.ONE[:, 0:128], True, False)
+                first = scored[h] == 1 and not (h and SHARED)
+                if n in SHARED:
+                    at = 512 * (n % 2) + 128 * (i % 4)
+                    mm(["cS%d" % (n % 2), "EBh"], ["k3"], out, T.EBh[:, 15 - i:143 - i], T.cS[:, at:at + 128], first, scored[h] == 16)
+                else:
+                    mm(ck + ["EB"], ["k3"], out, T.EB[:, 15 - i:143 - i], T.cmp[:, 256 * i + 128 * h:256 * i + 128 * h + 128], first, scored[h] == 16)
+
+    def signs(n):
+        if n in SHARED:
+            h, d = n // 4, ("k6", "k0")[n % 2]
+            for i in range(4):
+                acc(d, T[d][:, 128 * i:128 * i + 128], [("Ib", ["x"], T.x[:, half(h)[0]]),
+                                                        ("Ib", ["g%d" % (2 * h), "g%d" % (2 * h + 1), "g4"], T.G[:, 2048 * h + 4 * (n % 4) + i:2048 * h + 2048:16])])
+            act([d], ["cS%d" % (n % 2)], T.cS[:, 512 * (n % 2):512 * (n % 2) + 512], T[d][:], AF.Sign, bias=0.5)
+
+    def weigh(h):
+        o = half(h)[0]
+        act(["k3"], of("e", h), T.e[:, o], T.k3[:, o], AF.Silu, bias=-85.6, scale=4.6)
+        acc("k4", T.k4[:, o], [("TRI", of("e", h), T.e[:, o])])
+
+    def covered():
+        if "d2" in ONS:
+            act(["k5"], ["D2"], T.D2[:], T.k5[:, 256:512], AF.Relu, bias=1.0, scale=-1.0)
+        else:
+            ts(["k5"], "D2", T.D2[:], T.k5[:, 256:512], 0.5, None, OP.is_lt)
+
+    def pick(h):
+        o = half(h)[0]
+        M = T.k4[:, 256 + o.start:256 + o.stop]
+        terms = [("B512", ["D2"], T.D2[:, o])]
+        terms += [("B256", ["ONE"], T.ONE[:, o]), ("B256", ["D1"], T.D1[:, o])] if "d1" in ONS else [("B512", ["D1"], T.D1[:, o])]
+        if "m%d" % h in ONS:
+            act(["k4"], ["k4"], M, T.k4[:, o], AF.Sign)
+            terms += [("BLKg", ["nF"], T.nF[:, o]), ("BLKg", of("np", h), T.np[:, o])]
+        else:
+            ts(["k4"], "k4", M, T.k4[:, o], 0.0, None, OP.is_gt)
+            terms += [("BLKf", of("np", h), T.np[:, o])]
+        yield
+        v("tt", ["k4", "nF"], of("np", h), T.np[:, o], M, T.nF[:, o], OP.mult)
+        acc("k5", T.k5[:, o], terms)
+
+    def losers():
+        if "d1" in ONS:
+            mm(["MONE", "thr"], ["k2"], T.k2[:, 0:256], T.MONE[0:1, :], T.thr[0:1, :], False, True)
+            act(["k2"], ["D1"], T.D1[:], T.k2[:, 0:256], AF.Sign)
+        else:
+            v("tt", ["k2", "thr"], ["D1"], T.D1[:], T.k2[:, 0:256], T.thr[:], OP.is_ge)
+
+    def lines(h):
+        o, w = half(h)
+        v("scan", ["GM", "k5"], of("SP", h), T.SP[:, o], T.GM[:, o], T.k5[:, o], 0.0, OP.add, OP.max)
+        yield
+        v("tc", ["k5"], of("pR", h), T.pR[:, o], T.k5[:, o])
+        yield
+        sp = T.SP[:, o.start + 15:o.stop:16]
+        v("ts", of("SP", h) + ["corr"], of("pL", h), T.pL[:, w], sp, c("corr"), float(NONE), OP.subtract, OP.min)
+        yield
+        v("ts", of("SP", h) + ["corr"], of("pWf", h), T.pWf[:, w], sp, c("corr"), float(NONE), OP.subtract, OP.min)
+
+    def payees(h):
+        o, w = half(h)
+        act(PTs + of("pL", h), of("PG", h), T.PG[:, o], T.PT[:].indirect(T.pL[:, w]))
+        act(AA + of("pL", h), of("Ap", h), T.Ap[:, o], T.A[:].indirect(T.pL[:, w]))
+
+    def payee_banks(h):
+        o, d = half(h)[0], ("k0", "k1", "k1")[h]
+        acc(d, T[d][:, o], [("WBm", of("PG", h), T.PG[:, o])])
+        act([d], of("Xb", h), T.Xb[:, o], T[d][:, o])
+
+    def draws(h):
+        o = half(h)[0]
+        v("tt", of("Ap", h) + ["k7"], of("t", h), T.t[:, o], T.Ap[:, o], T.k7[:, 256 + o.start:256 + o.stop], OP.min)
+
+    def kept():
+        acc("k1", T.k1[:, 256:512], [("NIb", ["mm"], T.mm[:]), ("Ib", of("Ap", 2), T.Ap[:])])
+        act(["k1"], ["An"], T.An[:], T.k1[:, 256:512], AF.Relu)
+
+    def ranks(h):
+        o = half(h)[0]
+        mm(["DG"] + of("PG", h), ["k2"], T.k2[:, o], T.DG[:], T.PG[:, o], False, True)
+
+    def counts(h):
+        o = half(h)[0]
+        v("tt", ["k2", "thr2"], of("OA", h), T.OA[:, o], T.k2[:, o], T.thr2[:, o], OP.is_lt)
+        yield
+        v("scan", of("OA", h) + ["STEP", "icol", "k7"], ["k7"], T.k7[:, o], T.OA[:, o], T.STEP[:, o], T.k7[:, 127:128] if h == 1 else c("icol"), OP.add, OP.subtract)
+        yield
+        v("tt", ["k7"] + of("OA", h), of("Z", h), T.Z[:, o], T.k7[:, o], T.OA[:, o], OP.mult)
+        acc("k6", T.k6[:, o], [("B4n", of("OA", h), T.OA[:, o]), ("BLKh", of("Z", h), T.Z[:, o])])
+
+    def slots(h):
+        o, w = half(h)
+        v("scan", ["GM", "k6"], of("SS", h), T.SS[:, o], T.GM[:, o], T.k6[:, o], 0.0, OP.add, OP.max)
+        yield
+        v("ts", of("SS", h) + ["corr"], of("sL", h), T.sL[:, w], T.SS[:, o.start + 15:o.stop:16], c("corr"), None, OP.subtract)
+
+    def place(s, h):
+        o, w = half(h)
+        v("tt", of("Xb", h) + of("t", h) + of("sL", h) + ["XE%d" % k for k in range(s, STEPS)], ["XW"],
+          T.XW[:, 1024 * s:1024 * s + XWIN].indirect(T.sL[:, w]), T.Xb[:, o], T.t[:, o], OP.add)
+
+    def bank_list():
+        v("scan", ["GM2", "D1"], ["SD"], T.SD[:], T.GM2[:], T.D1[:], 0.0, OP.add, OP.max)
+        yield
+        ts(["SD", "los"], "wa", T.wa[:], T.SD[:, 15::16], 2048.0 if "d1" in ONS else 4096.0, c("los"), OP.mult, OP.add)
+        yield
+        v("tt", ["wa", "Wf"], ["wa"], T.wa[:], T.wa[:], T.Wf[:], OP.add)
+        yield
+        v("tt", ["wa", "LC"], ["wa"], T.wa[:], T.wa[:], T.LC[:], OP.min)
+        yield
+        ts(["wa"], "wU", T.wU[:], T.wa[:], float(B), None, OP.subtract)
+
+    def best_rows(h):
+        o = half(h)[0]
+        act(["k4"], of("Mb", h), T.Mb[:, o], T.k4[:, 256 + o.start:256 + o.stop], AF.Relu)
+
+    def drawn(last):
+        if not last:
+            acc("k4", T.k4[:, 0:256], [("I8k", of("Mb", 2), T.Mb[:]), ("B4q", of("OA", 2), T.OA[:])])
+        acc("k3", T.k3[:, 0:256], [("If", of("t", 2), T.t[:]), ("B4a", of("OA", 2), T.OA[:])])
+        act(["k3"], ["tp"], T.tp[:], T.k3[:, 0:256], AF.Relu, bias=-512.0)
+
+    def write_rows():
+        act(["qn", "wU"], QQ, T.Q[:].indirect(T.wU[:]), T.qn[:], AF.Silu)
+
+    def write_banks():
+        acc("k3", T.k3[:, 256:512], [("Ib", ["x"], T.x[:]), ("Ib", ["tp"], T.tp[:])])
+        act(["k3"], ["vn"], T.vn[:], T.k3[:, 256:512], AF.Identity, bias=VO)
+        act(["vn", "wU"], VT, T.VT[:].indirect(T.wU[:]), T.vn[:], AF.Silu)
+
+    def convert(s, n):
+        if s == 0 and n == 0:
             act(["Vm"], ["VTm"], T.VT[:, 0:B], T.V[:, 0:B], AF.Identity, bias=VO)
-        if s == STEPS - 1:
+        if s == STEPS - 1 and n == 0:
             act(VT, ["Vr"], T.Vr[:], T.VT[:, 0:B], AF.Identity, bias=MAGIC)
+        if s == STEPS - 1 and n == 1:
             act(["Vr"], ["Vm"], T.V[:, 0:B], T.Vr[:], AF.Identity, bias=-MAGIC - VO)
 
     def line_list():
-        ts(["pWf0", "pWf1", "pco"], "pWc", T.pWc[:], T.pWf[:], c("pco"), None, OP.add)
-        v("tt", ["SS0", "SS1", "pWc"], ["pa"], T.pa[:], T.SS[:, 15::16], T.pWc[:], OP.max)
-        ts(["pa", "pco"], "pU", T.pU[:], T.pa[:], c("pco"), None, OP.subtract)
+        ts(["sL0", "sL1"], "pa", T.pa[:], T.sL[:], 1024.0, None, OP.subtract)
+        yield
+        v("tt", ["pa", "pWf0", "pWf1"], ["pa"], T.pa[:], T.pa[:], T.pWf[:], OP.max)
+        yield
+        v("tc", ["pa"], ["pU"], T.pU[:], T.pa[:])
 
     def write_lines(last):
         if last:
-            v("tt", ["x", "tp0", "tp1", "wU"], VV, T.V[:].indirect(T.wU[:]), T.x[:], T.tp[:], OP.add)
+            v("tt", ["x", "tp", "wU"], VV, T.V[:].indirect(T.wU[:]), T.x[:], T.tp[:], OP.add)
         else:
-            v("tc", ["An0", "An1", "pU"], AA, T.A[:].indirect(T.pU[:]), T.An[:])
+            v("tc", ["An", "pU"], AA, T.A[:].indirect(T.pU[:]), T.An[:])
 
     def stage(name, s):
         last = s == STEPS - 1
-        kind, n = name[:2], int(name[2:] or 0)
-        if last and kind in ("br", "nr", "wr", "wb", "ll", "bo", "qr", "op", "up", "wf"):
+        kind, n = name[:2], int(name[2:3] or 0)
+        if last and (kind in ("br", "nr", "wr", "wb", "ll", "an") or name in HEAD.split()):
             return
-        {"bo": lambda: bank_offsets(s + 1), "qr": queue_rows, "op": lambda: old_positions(s + 1), "up": lambda: unpack(s + 1),
+        if name[3:] > "a":
+            return next(begun[name[:3]], None)
+        begun[name[:3]] = {"bo": lambda: bank_offsets(s + 1), "qr": queue_rows, "op": lambda: old_positions(s + 1), "up": lambda: unpack(s + 1),
          "wf": lambda: ts(["WL"], "Wf", T.Wf[:], T.WL[:], float(B), None, OP.add),
-         "am": lambda: amounts(n), "bt": lambda: bank_twins(4 * n, 4 * n + 4), "po": positions, "cm": lambda: compare(n // 2, n % 2),
-         "nf": lambda: v("tc", ["nU"], ["nF"], T.nF[:], T.nU[:]),
-         "dz": lambda: ts(["k5"], "D2", T.D2[:], T.k5[:, 256:512], 0.5, None, OP.is_lt),
-         "lo": lambda: losers(n), "bl": bank_list, "we": lambda: weigh(n), "pk": lambda: pick(n), "ln": lambda: lines(n),
-         "py": lambda: payees(n), "ms": lambda: missing(n), "lt": lambda: line_twins(min(n // 2, 1), 4 * n - 8 * (n > 1), 4 * n - 8 * (n > 1) + 4),
-         "rk": lambda: ranks(n), "pc": lambda: packed(n, last), "es": lambda: empty_slots(s), "br": lambda: best_row(n),
-         "ct": lambda: counts(n), "sl": lambda: slots(n), "dr": lambda: drawn(n, last), "pl": lambda: place(s, n),
-         "nr": lambda: new_rows(n), "wr": lambda: write_rows(n), "wb": lambda: write_banks(n), "cv": lambda: convert(s),
+         "am": lambda: amounts(n, s), "bt": lambda: bank_twins(n), "po": positions, "ca": lambda: compare(n, 0), "cb": lambda: compare(n, 1),
+         "sg": lambda: signs(n), "nf": lambda: v("tc", ["nU"], ["nF"], T.nF[:], T.nU[:]), "dz": covered,
+         "lo": losers, "bl": bank_list, "we": lambda: weigh(n), "pk": lambda: pick(n), "ln": lambda: lines(n),
+         "py": lambda: payees(n), "lt": lambda: line_twins(n), "lu": lambda: all_line_twins(n), "rk": lambda: ranks(n), "bk": lambda: payee_banks(n), "tm": lambda: draws(n),
+         "an": kept, "br": lambda: best_rows(n), "ct": lambda: counts(n), "sl": lambda: slots(n), "dr": lambda: drawn(last), "pl": lambda: place(s, n),
+         "nr": lambda: v("tt", ["k4", "nF"], ["qn"], T.qn[:], T.k4[:, 0:256], T.nF[:], OP.max),
+         "lc": later_constants, "wr": write_rows, "wb": write_banks, "cv": lambda: convert(s, n),
          "ex": lambda: exchange(s), "ll": line_list, "wl": lambda: write_lines(last)}[kind]()
+        if name[3:]:
+            next(begun[name[:3]])
 
-    for name in HEAD.split():
-        stage(name, -1)
+    begun = {}
+    for name in FIRST.split():
+        stage(name, -1 if name in HEAD.split() else 0)
     for s in range(STEPS):
         for name in ORDER.split():
-            stage(name, s)
-
-    for s in []:
-        last = s == STEPS - 1
-        L, Lk = T["L%d" % s], ["L%d" % s, "L%do" % s]
-        v("scan", ["GM"] + Lk, ["SC"], T.SC[:], T.GM[:], L[:], 0.0, OP.add, OP.max)
-        ts(["SC", "corr"], "WL", T.WL[:], T.SC[:, 15::16], c("corr"), 1 / 512, OP.subtract, OP.mult)
-        ts(QQ + ["WL"], "nU", T.nU[:], T.Q[:].indirect(T.WL[:]), 0.25, None, OP.add)
-        if s:
-            act(VT + ["WL"], ["Vg"], T.Vg[:], T.VT[:].indirect(T.WL[:]), AF.Identity, bias=-EMPTY)
-        else:
-            act(VV + ["WL"], ["Vg"], T.Vg[:], T.V[:].indirect(T.WL[:]), AF.Identity, bias=VO - EMPTY)
-        unpack(s)
-        ts(["WL"], "Wf", T.Wf[:], T.WL[:], float(B), None, OP.add)
-        for k in range(3):
-            amounts(k)
-        for h in range(16):
-            twins(h, 16 * h, 256, "bR", T.bR, "Wf", T.Wf, {7: [0], 15: [1]}.get(h, []))
-            if h == 3:
-                positions()
-        compare(0)
-        v("tc", ["nU"], ["nF"], T.nF[:], T.nU[:])
-        ts(["k5"], "D2", T.D2[:], T.k5[:, 256:512], 0.5, None, OP.is_lt)
-        compare(1)
-        weigh(0)
-        amounts(3)
-        losers(0)
-        losers(1)
-        compare(2)
-        pick(0)
-        lines(0)
-        payees(0)
-        compare(3)
-        missing(0)
-        weigh(1)
-        for h in range(8):
-            twins(h, 16 * h, 128, "pR0", T.pR, "pWf0", T.pWf)
-        ranks(0)
-        pick(1)
-        packed(0, last)
-        counts(0)
-        lines(1)
-        payees(1)
-        empty_slots(s)
-        for h in range(16):
-            twins(h, max(128, 16 * h), 256, "pR1", T.pR, "pWf%d" % (h // 8), T.pWf)
-            if h == 7:
-                missing(1)
-        ranks(1)
-        packed(1, last)
-        bank_list()
-        if s == 0:
-            fill("VTp", T.VT[:, B:VW], VW - B, VO)
-            act(["Vm"], ["VTm"], T.VT[:, 0:B], T.V[:, 0:B], AF.Identity, bias=VO)
-        if last:
-            act(VT, ["Vr"], T.Vr[:], T.VT[:, 0:B], AF.Identity, bias=MAGIC)
-            act(["Vr"], ["Vm"], T.V[:, 0:B], T.Vr[:], AF.Identity, bias=-MAGIC - VO)
-        else:
-            best_row(0)
-            best_row(1)
-        counts(1)
-        slots(0)
-        drawn(0, last)
-        place(s, 0)
-        slots(1)
-        place(s, 1)
-        drawn(1, last)
-        exchange(s)
-        if last:
-            v("tt", ["x", "tp0", "tp1", "wU"], VV, T.V[:].indirect(T.wU[:]), T.x[:], T.tp[:], OP.add)
-        else:
-            for h in range(2):
-                new_rows(h)
-                write_rows(h)
-            ts(["pWf0", "pWf1", "pco"], "pWc", T.pWc[:], T.pWf[:], c("pco"), None, OP.add)
-            v("tt", ["SS0", "SS1", "pWc"], ["pa"], T.pa[:], T.SS[:, 15::16], T.pWc[:], OP.max)
-            ts(["pa", "pco"], "pU", T.pU[:], T.pa[:], c("pco"), None, OP.subtract)
-            v("tc", ["An0", "An1", "pU"], AA, T.A[:].indirect(T.pU[:]), T.An[:])
-            for h in range(2):
-                write_banks(h)
+            if s or name in HEAD.split() or name not in FIRST.split():
+                stage(name, s)
     dma("y", VV, ["yv"], T.yv[:], T.V[:, 0:B])
-    unpack(STEPS)
-    ts(["bR"], "yw32", T.yw32[:], T.bR[:], float(B), None, OP.subtract)
-    dma("y", ["yw32"], ["yw"], T.yw[:], T.yw32[0:128:16, :])
-    act(["k0"], ["cb"], T.cb[:], T.k0[:, 0:256], AF.Identity, bias=EMPTY)
-    dma("s", ["cb"], ["yc"], T.yc[:], T.cb[:])
+    L, Lk = T["L%d" % STEPS], ["L%d" % STEPS, "L%do" % STEPS]
+    ts(Lk, "k0", T.k0[:, 0:256], L[:], 512 * MAGIC, 512 * MAGIC, OP.add, OP.subtract)
+    v("tt", Lk + ["k0"], ["cb"], T.cb[:], L[:], T.k0[:, 0:256], OP.subtract)
+    dma("y", ["cb"], ["yc"], T.yc[:], T.cb[:])
+    act(["k0"], ["yw32"], T.yw32[:], T.k0[:, 0:256], AF.Copy, scale=1 / 512)
+    dma("s", ["yw32"], ["yw"], T.yw[:], T.yw32[0:128:16, :])
     for sem in sorted(total):
         need_wait("g", sem, total[sem])

@@ -13,14 +13,15 @@ KILL = 2.0 ** 90
 MAGIC = 1.5 * 2.0 ** 23
 ONS = "d2".split()
 SHARED = ()
-HEAD = "bo0a bo0b qr up wf lc op"
-FIRST = "bo0a bo0b qr up wf lc bt0 bt1 bt2 bt3 nf lo bl0a bl0b bl0c bl0d bl0e am0 am4 op"
+HEAD = "bo0a bo0b qr up wf op"
+FIRST = "up lc0a bo0a pt bo0b wf qr bt0 bt1 bt2 bt3 nf am0 lc0b op po0a po0b po0c lo"
+LATE = "ld bl0a qc bl0b bl0c bl0d"
 HELP = [0, 0, 0, 0]
 BATCH = 2
 WIDE = (0, 1, 2, 3)
-ORDER = """am0 bt0 po0a bt1 po0b bt2 nf am1 bt3 po0c cb3 lo am2 cb2 am3 cb0 cb1 ca6 ca5 we0 ca7 dz cb7 cv0 cb5 pk0a cb6 pk0b ca4 cb4 we1 bl0a ln0a ln0b ln0c
-    ln0d lt0 lt1 pk1a bl0b py0 rk0 pk1b ct0a ct0b cv1 ln1a br2 ln1b bk0 ct0c lt2 bl0c ln1c ln1d lt3 lt4 py1 lt5 bl0d rk1 sl0a tm1 tm0 sl0b ct1a ct1b bk1 ct1c pl0
-    sl1a sl1b pl1 dr ll0a nr an bl0e ll0b ex wr wb ll0c wl bo0a bo0b qr up wf op"""
+ORDER = """am0 bt0 am1 bt1 bt2 po0a bt3 po0b po0c nf am2 lo am3 cb3 cb0 cb2 cb1 bl0a ca7 ca4 we0 cb4 cb7 pk0a ca5 dz cv0 pk0b cb5 ca6 cb6 ln0a we1 ln0b ln0c py0 ln0d lt0
+    lt1 pk1a bl0b cv1 rk0 pk1b ct0a bk0 ct0b ln1a ln1b ct0c lt2 ln1c ln1d lt3 lt4 br2 pw py1 lt5 rk1 sl0a tm1 tm0 ct1a bl0c bk1 ct1b sl0b dr ct1c pl0 sl1a bl0d
+    sl1b ll0a pl1 an ll0b ex nr wl bo0a wb bo0b wr up op qr wf"""
 SCRATCH = {}
 
 
@@ -32,7 +33,7 @@ def _buf(dtype, n, names, parts=128):
 _buf("bfloat16", VW, "V")
 _buf("float32", VW, "Q VT")
 _buf("float32", B, "Vr")
-_buf("int32", B, "Qin")
+_buf("int32", B + 16, "Qin")
 _buf("bfloat16", AW, "A")
 _buf("bfloat16", LO + 8192, "PT")
 _buf("float32", 1024 * (STEPS - 1) + XWIN, "XW")
@@ -47,14 +48,16 @@ _buf("float32", 128, "imp qg BLKf BLKg If")
 _buf("bfloat16", 128, "u1 u2 u3 B256 MONE H8")
 _buf("float32", 144, "ebi")
 _buf("bfloat16", 144, "EB EBh")
-_buf("float32", 256, "SC SP SS nF np Xb t qn vn Vg yw32 FALL")
+_buf("float32", 256, "SC SD SP SS nF np qn vn Vg yw32 FALL")
+_buf("float32", 256, "Xb t")
+_buf("float32", 128, "NIf")
 _buf("int32", 8, "pc pj pg pb")
 _buf("float32", 64, "cf")
-_buf("float32", 16, "l16 LC Wf wa pWf pa")
+_buf("float32", 16, "l16 LC Wf wa pWf pWc pa")
 _buf("uint16", 16, "WL wU pL sL pU")
-_buf("float16", 128, "N512 BLKh")
+_buf("float16", 128, "N512 BLKh Ih")
 _buf("bfloat16", 128, "Ib NIb N32 BLKb B512 B4a B4q B4n I8k DG WBm WT TRI")
-_buf("bfloat16", 256, "tt GM GM2 STEP ZERO thr thr2 SD x mm D1 D2 e Mb PG Ap An tp OA cb")
+_buf("bfloat16", 256, "tt GM STEP ZERO thr thr2 x mm D1 D2 e Mb PG Ap An tp OA cb")
 _buf("float16", 256, "Z bR y")
 _buf("uint16", 256, "nU pR")
 _buf("bfloat16", 4096, "eq G cmp")
@@ -64,6 +67,14 @@ PSUM = ["k%d" % s for s in range(8)]
 for _s in PSUM:
     SCRATCH[_s] = ("psum", [128, 512], "float32")
 SEMAPHORES = ["sv", "ss", "st", "sg", "lx"] + ["rx%d" % s for s in range(STEPS)] + ["d%d" % k for k in range(16)]
+
+
+def step_order(s, order):
+    if s:
+        return order
+    order = [n for n in order if (n in HEAD.split() or n not in FIRST.split()) and n not in LATE.split()]
+    at = order.index("ex") + 1
+    return order[:at] + LATE.split() + order[at:]
 
 
 def split_engines(topo, cores, src):
@@ -95,11 +106,12 @@ def rank_program(g, core, T, topo):
     know = {e: {} for e in queue}
     snap, lastw, readers, total = {}, {}, {}, {}
     ndma = [0]
+    calls = []
 
     def need_wait(e, sem, val):
         if know[e].get(sem, 0) >= val:
             return
-        queue[e].wait_ge(T.sem[sem], val)
+        calls.append((e, None, sem, val))
         for s2, v2 in snap.get((sem, val), {}).items():
             know[e][s2] = max(know[e].get(s2, 0), v2)
         know[e][sem] = max(know[e].get(sem, 0), val)
@@ -136,17 +148,17 @@ def rank_program(g, core, T, topo):
         eng = queue[e]
         call = {"tc": lambda: eng.tensor_copy(*a), "tt": lambda: eng.tensor_tensor(*a), "ts": lambda: eng.tensor_scalar(*a),
                 "scan": lambda: eng.tensor_tensor_scan(*a), "ms": lambda: eng.memset(*a), "act": lambda: eng.activation(*a, **k),
-                "mm": lambda: eng.matmul(*a), "iota": lambda: eng.iota(*a, **k)}[name]
+                "mm": lambda: eng.matmul(*a), "iota": lambda: eng.iota(*a, **k), "sel": lambda: eng.affine_select(*a)}[name]
         sem = semof[e]
         cnt[sem] += 1
-        call().then_inc(T.sem[sem], 1)
+        calls.append((e, call, sem, cnt[sem]))
         note(sem, cnt[sem], R, W, e)
 
     def dma(e, R, W, out, in_):
         waits(e, R, W)
         sem = "d%d" % ndma[0]
         ndma[0] += 1
-        queue[e].dma_start(out, in_).then_inc(T.sem[sem], 16)
+        calls.append((e, lambda: queue[e].dma_start(out, in_).then_inc(T.sem[sem], 16), None, 0))
         note(sem, 16, R, W, e)
 
     def v(name, R, W, *a):
@@ -167,7 +179,7 @@ def rank_program(g, core, T, topo):
 
     dma("y", [], ["wkI"], T.wkI[:], T.wk[:])
     dma("y", [], ["payS"], T.payS[:], T.pay[:])
-    dma("y", [], ["Qin"], T.Qin[:], T.qu[:])
+    dma("y", [], ["Qin"], T.Qin[:, 0:B], T.qu[:])
     dma("y", [], ["Am"], T.A[:, LO:LO + 8192], T.am[:])
     dma("y", [], ["Vm"], T.V[:, 0:B], T.vp[:])
 
@@ -177,11 +189,22 @@ def rank_program(g, core, T, topo):
     iota("qg", T.qg[:], [[1, 8], [0, 16]], 0, 0)
     iota("imp", T.imp[:], [[1, 128]], 0, -1)
     iota("tt", T.tt[:], [[0, 16], [1, 16]], 0, 0)
-    iota("l16", T.l16[:], [[16, 16]], 0, 0)
+    iota("l16", T.l16[:], [[16, 16]], 1280, 0)
     iota("ebi", T.ebi[:], [[1, 144]], -15, 0)
-    iota("PTa", T.PT[:, 0:LO + 4096], [[0, LO + 4096]], 1, 0)
-    for s in range(STEPS):
-        iota("XE%d" % s, T.XW[:, 1024 * s:1024 * s + 832], [[0, 832]], int(EMPTY), 0)
+    iota("Apd", T.A[:, LO + 8192:AW], [[0, AW - LO - 8192]], 0, 0)
+    iota("Vp", T.V[:, B:VW], [[0, VW - B]], 0, 0)
+
+    def empty_slots(s):
+        for r in range(4):
+            at = 1024 * s + 256 * r
+            iota("XE%d_%d" % (s, r), T.XW[:, at:at + 64], [[0, 64]], -int(EMPTY), 0)
+
+    def select(out, src, *a):
+        op("g", "sel", [src], [out], T[out][:], T[src][:], *a)
+
+    def own_group(out, src):
+        select(src, src, [[-16, 8], [0, 16]], OP.is_ge, 0.0, 0, 1)
+        select(out, src, [[16, 8], [0, 16]], OP.is_ge, 0.0, 15, -1)
 
     col = {}
 
@@ -195,6 +218,7 @@ def rank_program(g, core, T, topo):
     def byrow(table):
         for is_ in sorted({t[:2] for name, start, terms in table for t in terms}):
             colop("%s%d" % is_, ["jf"], "ts", c("jf"), float(is_[1]), None, {"lt": OP.is_lt, "eq": OP.is_equal, "ge": OP.is_ge}[is_[0]])
+        yield
         for n in range(max(len(terms) for name, start, terms in table)):
             for name, start, terms in table:
                 if n < len(terms):
@@ -209,13 +233,17 @@ def rank_program(g, core, T, topo):
         ts([src, by], name, T[name][:], T[src][:], c(by) if by in col else by, None, OP.mult)
 
     v("ms", [], ["ONE"], T.ONE[:], 1.0)
-    for k in range(4):
-        fill("PTb%d" % k, T.PT[:, LO + 4096 + 1024 * k:LO + 5120 + 1024 * k], 1024, 1.0)
+    v("ms", [], ["u1"], T.u1[:], 1 / 32)
+    select("u1", "u1", [[1, 128]], OP.is_ge, 2.0, 0, -1)
+    select("u1", "u1", [[1, 128]], OP.not_equal, -1.0, 0, -1)
+    own_group("TRI", "u1")
+    iota("PTa", T.PT[:, 0:LO + 3072], [[0, LO + 3072]], 1, 0)
+    for k in range(2):
+        fill("PTb%d" % k, T.PT[:, LO + 3072 + 1024 * k:LO + 4096 + 1024 * k], 1024, 1.0)
     v("ms", [], ["ZERO"], T.ZERO[:], 0.0)
     v("ms", [], ["FALL"], T.FALL[:], 1 / RHO)
-    v("ms", [], ["Vp"], T.V[:, B:VW], 0.0)
-    v("ms", [], ["Apd"], T.A[:, LO + 8192:AW], 0.0)
     v("ms", [], ["Apl"], T.A[:, 0:LO], 0.0)
+    v("ms", [], ["Qip"], T.Qin[:, B:B + 16], 8191)
     v("scan", ["FALL", "ZERO"], ["thr"], T.thr[:], T.FALL[:], T.ZERO[:], 2.54 * RHO * TOP, OP.mult, OP.add)
     ts(["pc"], "pj", T.pj[:, 0:1], T.pc[:, 0:1], 15, None, OP.bitwise_and)
     ts(["pc"], "pg", T.pg[:, 0:1], T.pc[:, 0:1], 4, None, OP.arith_shift_right)
@@ -225,15 +253,13 @@ def rank_program(g, core, T, topo):
     for k in range(4):
         ts(["pj"], "pb%d" % k, T.pb[:, k:k + 1], T.pj[:, 0:1], k, 1, OP.arith_shift_right, OP.bitwise_and)
     pf8 = T.cf[0:8, col["pf"]:col["pf"] + 1]
-    ts(["qg", "pf"], "sel8", T.sel8[:], T.qg[0:8, :], pf8, 512.0, OP.is_equal, OP.mult)
+    ts(["qg", "pf"], "sel8", T.sel8[:], T.qg[0:8, :], pf8, -512.0, OP.is_equal, OP.mult)
     v("tc", ["wkI"], ["wkH"], T.wkH[:], T.wkI[:])
     mm(["sel8", "wkH"], ["k0"], T.k0[:, 0:256], T.sel8[:], T.wkH[:])
     v("tc", ["payS"], ["payF"], T.payF[:], T.payS[:])
     for k in range(3):
         act(["payF"], ["b%d" % k], T.payB[:, 512 * k:512 * k + 512], T.payF[:], AF.Sign, bias=0.5 - 1024 * (k + 1))
     act(["payF"], ["payA"], T.payA[:], T.payF[:], AF.Identity, bias=-15.5 / 32, scale=1 / 32)
-    fill("Qp", T.Q[:, B:VW], VW - B, float(NONE))
-    fill("VTp", T.VT[:, B:VW], VW - B, VO)
     ts(["qg", "gf"], "BLKb", T.BLKb[:], T.qg[:], c("gf"), None, OP.is_equal)
     ts(["imp"], "Ib", T.Ib[:], T.imp[:], 0.0, None, OP.is_equal)
     for k in range(4):
@@ -245,60 +271,51 @@ def rank_program(g, core, T, topo):
     v("tc", ["k0"], ["L0"], T.L0[:], T.k0[:, 0:256])
     ts(["GM"], "GM", T.GM[:], T.GM[:], LIFT, None, OP.min)
     ts(["BLKb", "f01", "f3"], "WT", T.WT[:], T.BLKb[:], c("f01"), c("f3"), OP.mult, OP.mult)
-    for name, by in (("N512", -512.0), ("If", 1.0), ("NIb", -1.0), ("N32", -32.0)):
+    for name, by in (("N512", -512.0), ("If", 1.0), ("NIf", -1.0), ("NIb", -1.0), ("N32", -32.0)):
         scaled(name, "Ib", by)
-    ts(["Qin"], "Qm", T.Q[:, 0:B], T.Qin[:], float(LO), None, OP.add)
     act(["payA"], ["payA"], T.payA[:], T.payA[:], AF.Identity, bias=MAGIC)
     act(["payA"], ["b3"], T.payB[:, 1536:2048], T.payA[:], AF.Identity, bias=-MAGIC)
     acc("k3", T.k3[:], [("If", ["payF"], T.payF[:]), ("N32", ["b3"], T.payB[:, 1536:2048])])
     act(["k3"], ["b4"], T.payB[:, 2048:2560], T.k3[:])
     colop("n15", ["jf"], "ts", c("jf"), 15.0, None, OP.is_lt)
-    for k in range(3):
-        end = T.payB[:, 512 * k + 511:512 * k + 512]
-        ts(["b%d" % k, "n15"], "b%d" % k, end, end, c("n15"), None, OP.mult)
-    PTf = ["PTa"] + ["PTb%d" % k for k in range(4)]
-    for j in range(5):
-        dma("y", ["b%d" % j, "Am"] + PTf, ["PT%d" % j], T.PT[j::16, LO:LO + 8192], T.payB[:, 512 * j:512 * j + 512])
+    PTf = ["PTa"] + ["PTb%d" % k for k in range(3)]
+
+    def payee_table():
+        v("ms", [], ["PTb2"], T.PT[:, LO + 5120:LO + 8192], 1.0)
+        for k in range(3):
+            end = T.payB[:, 512 * k + 511:512 * k + 512]
+            ts(["b%d" % k, "n15"], "b%d" % k, end, end, c("n15"), None, OP.mult)
+        for j in range(5):
+            dma("y", ["b%d" % j, "Am"] + PTf, ["PT%d" % j], T.PT[j::16, LO:LO + 8192], T.payB[:, 512 * j:512 * j + 512])
 
     def later_constants():
         colop("g16", ["gf"], "ts", c("gf"), 16.0, None, OP.mult)
-        if "d1" in ONS:
-            colop("los", ["jf"], "ts", c("jf"), 2.0 * 2048, -29.0 * 2048, OP.mult, OP.add)
-            scaled("B256", "BLKb", 256.0)
-            v("ms", [], ["MONE"], T.MONE[:], -1.0)
-        else:
-            colop("los", ["jf"], "ts", c("jf"), 2.0 * 4096, -30.0 * 4096, OP.mult, OP.add)
-        if "m0" in ONS or "m1" in ONS:
-            scaled("BLKg", "BLKb", 0.5)
+        colop("pco", ["corr"], "ts", c("corr"), 1024.0, None, OP.add)
         colop("n4", ["jf"], "ts", c("jf"), 4.0, None, OP.not_equal)
         colop("j256", ["jf"], "ts", c("jf"), 256.0, -1040.0 - LO, OP.mult, OP.add)
-        byrow([("icol", "j256", [("eq", 4, 2 * (1040 + LO) - 1025), ("eq", 5, 8192 + 1040 + LO - 1280)]),
-               ("jw", 0.0, [("lt", 3, -512 * 512), ("eq", 3, 512 * 32), ("eq", 4, 512), ("eq", 5, -512 * 1536)]),
-               ("jq", 0.0, [("lt", 4, 8192), ("eq", 4, LO - 8192)]),
-               ("jt", 0.0, [("ge", 4, 64 * KILL), ("ge", 6, -128 * KILL)]),
-               ("dm", 0.0, [("lt", 3, -2 * KILL)]), ("da", 0.0, [("lt", 3, KILL), ("eq", 5, 3 * KILL)])])
-        if SHARED:
-            ts(["tt"], "H8", T.H8[:], T.tt[:, 0:128], 4.0 * (min(SHARED) - 4), 0.5, OP.is_ge, OP.mult)
+        rows = byrow([("dm", 0.0, [("lt", 3, -2 * KILL)]), ("da", 0.0, [("lt", 3, KILL), ("eq", 5, 3 * KILL)]),
+                      ("jw", 0.0, [("lt", 3, -512 * 512), ("eq", 3, 512 * 32), ("eq", 4, 512), ("eq", 5, -512 * 1536)]),
+                      ("icol", "j256", [("eq", 4, 2 * (1040 + LO) - 1025), ("eq", 5, 8192 + 1040 + LO - 1280)]),
+                      ("jq", 0.0, [("lt", 4, 8192), ("eq", 4, LO - 8192)]),
+                      ("jt", 0.0, [("ge", 4, 64 * KILL), ("ge", 6, -128 * KILL)])])
+        next(rows)
         ts(["ebi", "g16"], "EB", T.EB[:], T.ebi[:], c("g16"), None, OP.is_equal)
-        ts(["ebi", "g16"], "EBh", T.EBh[:], T.ebi[:], c("g16"), 0.5, OP.is_equal, OP.mult)
-        ts(["imp"], "u1", T.u1[:], T.imp[:], 0.0, 1.96875, OP.is_lt, OP.mult)
-        ts(["Ib"], "u2", T.u2[:], T.Ib[:], -1.03125, 0.03125, OP.mult, OP.add)
         ts(["tt", "jf"], "u3", T.u3[:], T.tt[:, 0:128], c("jf"), None, OP.is_gt)
-        ts(["GM"], "GM2", T.GM2[:], T.GM[:], 2 / LIFT, -64.0, OP.mult, OP.max)
-        ts(["l16", "jf"], "LC", T.LC[:], T.l16[:], c("jf"), 1280.0 + B, OP.add, OP.add)
-        for name, by in (("B512", 512.0), ("BLKf", 1.0), ("BLKh", 1.0), ("WBm", "jw"), ("B4q", "jq")):
-            scaled(name, "BLKb", by)
+        scaled("BLKh", "BLKb", 1.0)
         for name, by in (("B4n", -8192.0), ("B4a", 512.0)):
             ts(["BLKb", "lt4"], name, T[name][:], T.BLKb[:], c("lt4"), by, OP.mult, OP.mult)
-        scaled("I8k", "Ib", 8192.0)
-        v("tt", ["u1", "u2"], ["u1"], T.u1[:], T.u1[:], T.u2[:], OP.add)
+        empty_slots(0)
+        empty_slots(1)
+        yield
+        next(rows, None)
         ts(["u3", "dm", "da"], "u3", T.u3[:], T.u3[:], c("dm"), c("da"), OP.mult, OP.add)
+        own_group("DG", "u3")
+        empty_slots(2)
+        empty_slots(3)
         ts(["thr", "lt4", "jt"], "thr2", T.thr2[:], T.thr[:], c("lt4"), c("jt"), OP.mult, OP.add)
         ts(["ONE", "n4"], "STEP", T.STEP[:], T.ONE[:, 0:256], c("n4"), None, OP.mult)
-        if SHARED:
-            v("tt", ["H8", "BLKb"], ["H8"], T.H8[:], T.H8[:], T.BLKb[:], OP.mult)
-        v("tt", ["u1", "BLKb"], ["TRI"], T.TRI[:], T.u1[:], T.BLKb[:], OP.mult)
-        v("tt", ["u3", "BLKb"], ["DG"], T.DG[:], T.u3[:], T.BLKb[:], OP.mult)
+        for name, src, by in (("B512", "BLKb", 512.0), ("BLKf", "BLKb", 1.0), ("WBm", "BLKb", "jw"), ("B4q", "BLKb", "jq"), ("I8k", "Ib", 8192.0)):
+            scaled(name, src, by)
 
     PTs = PTf + ["PT%d" % j for j in range(5)]
     route = split_engines(topo, cores, core)
@@ -318,9 +335,12 @@ def rank_program(g, core, T, topo):
             tr.append(RemoteDMATransfer(dst_ids=[DstId(rid=topo.addr(d)[0], pnc=topo.addr(d)[1])], dma_engine_mask=m, remote_sem=T.sem["rx%d" % s],
                                         src=T.XW[:, at + r * 256:at + r * 256 + 64], dst=T[land][:, q * 64:q * 64 + 64]))
             sent[0] += len(route[d])
-        g.remote_dma_fused(tr, local_sem=T.sem.lx)
+        calls.append(("g", lambda: g.remote_dma_fused(tr, local_sem=T.sem.lx), None, 0))
         readers["XW"]["lx"] = total["lx"] = sent[0]
-        v("tc", ["XW"], [land + "o"], T[land][:, q * 64:q * 64 + 64], T.XW[:, at + q * 256:at + q * 256 + 64])
+        if "ex" in ONS:
+            act(["XW"], [land + "o"], T[land][:, q * 64:q * 64 + 64], T.XW[:, at + q * 256:at + q * 256 + 64])
+        else:
+            v("tc", ["XW"], [land + "o"], T[land][:, q * 64:q * 64 + 64], T.XW[:, at + q * 256:at + q * 256 + 64])
         lastw[land] = ("rx%d" % s, arrive)
         total["rx%d" % s] = arrive
 
@@ -336,29 +356,51 @@ def rank_program(g, core, T, topo):
     def bank_offsets(s):
         v("scan", ["GM", "L%d" % s, "L%do" % s], ["SC"], T.SC[:], T.GM[:], T["L%d" % s][:], 0.0, OP.add, OP.max)
         yield
-        ts(["SC", "corr"], "WL", T.WL[:], T.SC[:, 15::16], c("corr"), 1 / 512, OP.subtract, OP.mult)
+        ts(["SC", "corr"], "WL", T.WL[:], T.SC[:, 15::16], c("corr"), -1 / 512, OP.subtract, OP.mult)
 
-    def queue_rows():
-        ts(QQ + ["WL"], "nU", T.nU[:], T.Q[:].indirect(T.WL[:]), 0.25, None, OP.add)
+    def queue_rows(s):
+        if s:
+            ts(QQ + ["WL"], "nU", T.nU[:], T.Q[:].indirect(T.WL[:]), 0.25, None, OP.add)
+        else:
+            ts(["Qin", "Qip", "WL"], "nU", T.nU[:], T.Qin[:].indirect(T.WL[:]), float(LO), None, OP.add)
+
+    def row_numbers(s):
+        if s and "nf" in ONS:
+            act(QQ + ["WL"], ["nF"], T.nF[:], T.Q[:].indirect(T.WL[:]), AF.Identity, bias=0.25)
+        else:
+            v("tc", ["nU"], ["nF"], T.nF[:], T.nU[:])
+
+    def last_constants():
+        scaled("Ih", "Ib", 1.0)
+        ts(["l16", "jf", "pco"], "LC", T.LC[:], T.l16[:], c("jf"), c("pco"), OP.add, OP.add)
 
     def old_positions(s):
         if s:
             act(VT + ["WL"], ["Vg"], T.Vg[:], T.VT[:].indirect(T.WL[:]), AF.Identity, bias=-EMPTY)
         else:
-            ts(VV + ["WL"], "Vg", T.Vg[:], T.V[:].indirect(T.WL[:]), VO - EMPTY, None, OP.add)
+            v("tc", VV + ["WL"], ["x"], T.x[:], T.V[:].indirect(T.WL[:]))
 
     def unpack(s):
         L, Lk = T["L%d" % s], ["L%d" % s, "L%do" % s]
-        ts(Lk, "bR", T.bR[:], L[:], 1 / 512, float(B), OP.mult, OP.add)
-        acc("k0", T.k0[:, 0:256], [("If", Lk, L[:]), ("N512", ["bR"], T.bR[:])])
+        if "up" in ONS and s:
+            act(Lk, ["bR"], T.bR[:], L[:], AF.Identity, scale=-1 / 512, bias=float(B))
+        else:
+            ts(Lk, "bR", T.bR[:], L[:], -1 / 512, float(B), OP.mult, OP.add)
+        if s:
+            acc("k0", T.k0[:, 0:256], [("NIf", Lk, L[:]), ("N512", ["bR"], T.bR[:])])
 
-    def positions():
-        v("tt", ["Vg", "k0"], ["y"], T.y[:], T.Vg[:], T.k0[:, 0:256], OP.subtract)
+    def positions(s):
+        if s:
+            v("tt", ["Vg", "k0"], ["y"], T.y[:], T.Vg[:], T.k0[:, 0:256], OP.subtract)
         yield
-        ts(["y"], "x", T.x[:], T.y[:], VO, -255.0, OP.subtract, OP.max)
+        if s:
+            ts(["y"], "x", T.x[:], T.y[:], VO, -255.0, OP.subtract, OP.max)
         acc("k1", T.k1[:, 0:256], [("NIb", ["x"], T.x[:])])
         yield
-        ts(["x"], "mm", T.mm[:], T.x[:], -1.0, 0.0, OP.mult, OP.max)
+        if "mm" in ONS:
+            act(["x"], ["mm"], T.mm[:], T.x[:], AF.Relu, scale=-1.0)
+        else:
+            ts(["x"], "mm", T.mm[:], T.x[:], -1.0, 0.0, OP.mult, OP.max)
         acc("k5", T.k5[:, 256:512], [("BLKb", ["mm"], T.mm[:])])
         acc("k7", T.k7[:, 256:512], [("Ib", ["mm"], T.mm[:])])
 
@@ -470,9 +512,9 @@ def rank_program(g, core, T, topo):
         act(AA + of("pL", h), of("Ap", h), T.Ap[:, o], T.A[:].indirect(T.pL[:, w]))
 
     def payee_banks(h):
-        o, d = half(h)[0], ("k0", "k1", "k1")[h]
+        o, d = half(h)[0], ("k0", "k1")[h]
         acc(d, T[d][:, o], [("WBm", of("PG", h), T.PG[:, o])])
-        act([d], of("Xb", h), T.Xb[:, o], T[d][:, o])
+        act([d], of("Xb", h), T.Xb[:, o], T[d][:, o], AF.Copy, scale=-1.0)
 
     def draws(h):
         o = half(h)[0]
@@ -503,19 +545,17 @@ def rank_program(g, core, T, topo):
 
     def place(s, h):
         o, w = half(h)
-        v("tt", of("Xb", h) + of("t", h) + of("sL", h) + ["XE%d" % k for k in range(s, STEPS)], ["XW"],
-          T.XW[:, 1024 * s:1024 * s + XWIN].indirect(T.sL[:, w]), T.Xb[:, o], T.t[:, o], OP.add)
+        v("tt", of("Xb", h) + of("t", h) + of("sL", h) + ["XE%d_%d" % (k, r) for k in range(s, STEPS) for r in range(4)], ["XW"],
+          T.XW[:, 1024 * s:1024 * s + XWIN].indirect(T.sL[:, w]), T.Xb[:, o], T.t[:, o], OP.subtract)
 
     def bank_list():
-        v("scan", ["GM2", "D1"], ["SD"], T.SD[:], T.GM2[:], T.D1[:], 0.0, OP.add, OP.max)
+        acc("k6", T.k6[:, 256:512], [("Ih", ["bR"], T.bR[:]), ("I8k", ["D1"], T.D1[:])])
         yield
-        ts(["SD", "los"], "wa", T.wa[:], T.SD[:, 15::16], 2048.0 if "d1" in ONS else 4096.0, c("los"), OP.mult, OP.add)
+        v("scan", ["GM", "k6"], ["SD"], T.SD[:], T.GM[:], T.k6[:, 256:512], 0.0, OP.add, OP.max)
         yield
-        v("tt", ["wa", "Wf"], ["wa"], T.wa[:], T.wa[:], T.Wf[:], OP.add)
+        v("tt", ["SD", "LC"], ["wa"], T.wa[:], T.SD[:, 15::16], T.LC[:], OP.min)
         yield
-        v("tt", ["wa", "LC"], ["wa"], T.wa[:], T.wa[:], T.LC[:], OP.min)
-        yield
-        ts(["wa"], "wU", T.wU[:], T.wa[:], float(B), None, OP.subtract)
+        ts(["wa", "pco"], "wU", T.wU[:], T.wa[:], c("pco"), None, OP.subtract)
 
     def best_rows(h):
         o = half(h)[0]
@@ -538,17 +578,18 @@ def rank_program(g, core, T, topo):
     def convert(s, n):
         if s == 0 and n == 0:
             act(["Vm"], ["VTm"], T.VT[:, 0:B], T.V[:, 0:B], AF.Identity, bias=VO)
+        if s == 0 and n == 1:
+            fill("Qp", T.Q[:, B:VW], VW - B, float(NONE))
+            fill("VTp", T.VT[:, B:VW], VW - B, VO)
         if s == STEPS - 1 and n == 0:
             act(VT, ["Vr"], T.Vr[:], T.VT[:, 0:B], AF.Identity, bias=MAGIC)
         if s == STEPS - 1 and n == 1:
             act(["Vr"], ["Vm"], T.V[:, 0:B], T.Vr[:], AF.Identity, bias=-MAGIC - VO)
 
     def line_list():
-        ts(["sL0", "sL1"], "pa", T.pa[:], T.sL[:], 1024.0, None, OP.subtract)
+        v("tt", ["SS0", "SS1", "pWc"], ["pa"], T.pa[:], T.SS[:, 15::16], T.pWc[:], OP.max)
         yield
-        v("tt", ["pa", "pWf0", "pWf1"], ["pa"], T.pa[:], T.pa[:], T.pWf[:], OP.max)
-        yield
-        v("tc", ["pa"], ["pU"], T.pU[:], T.pa[:])
+        ts(["pa", "pco"], "pU", T.pU[:], T.pa[:], c("pco"), None, OP.subtract)
 
     def write_lines(last):
         if last:
@@ -559,14 +600,16 @@ def rank_program(g, core, T, topo):
     def stage(name, s):
         last = s == STEPS - 1
         kind, n = name[:2], int(name[2:3] or 0)
-        if last and (kind in ("br", "nr", "wr", "wb", "ll", "an") or name in HEAD.split()):
+        if last and (kind in ("br", "nr", "wr", "wb", "ll", "pw", "an") or name in HEAD.split()):
             return
         if name[3:] > "a":
             return next(begun[name[:3]], None)
-        begun[name[:3]] = {"bo": lambda: bank_offsets(s + 1), "qr": queue_rows, "op": lambda: old_positions(s + 1), "up": lambda: unpack(s + 1),
+        begun[name[:3]] = {"bo": lambda: bank_offsets(s + 1), "qr": lambda: queue_rows(s + 1), "ld": last_constants, "pt": payee_table,
+         "qc": lambda: ts(["Qin"], "Qm", T.Q[:, 0:B], T.Qin[:, 0:B], float(LO), None, OP.add),
+         "pw": lambda: act(["pWf0", "pWf1", "pco"], ["pWc"], T.pWc[:], T.pWf[:], AF.Identity, bias=c("pco")), "op": lambda: old_positions(s + 1), "up": lambda: unpack(s + 1),
          "wf": lambda: ts(["WL"], "Wf", T.Wf[:], T.WL[:], float(B), None, OP.add),
-         "am": lambda: amounts(n, s), "bt": lambda: bank_twins(n), "po": positions, "ca": lambda: compare(n, 0), "cb": lambda: compare(n, 1),
-         "sg": lambda: signs(n), "nf": lambda: v("tc", ["nU"], ["nF"], T.nF[:], T.nU[:]), "dz": covered,
+         "am": lambda: amounts(n, s), "bt": lambda: bank_twins(n), "po": lambda: positions(s), "ca": lambda: compare(n, 0), "cb": lambda: compare(n, 1),
+         "sg": lambda: signs(n), "nf": lambda: row_numbers(s), "dz": covered,
          "lo": losers, "bl": bank_list, "we": lambda: weigh(n), "pk": lambda: pick(n), "ln": lambda: lines(n),
          "py": lambda: payees(n), "lt": lambda: line_twins(n), "lu": lambda: all_line_twins(n), "rk": lambda: ranks(n), "bk": lambda: payee_banks(n), "tm": lambda: draws(n),
          "an": kept, "br": lambda: best_rows(n), "ct": lambda: counts(n), "sl": lambda: slots(n), "dr": lambda: drawn(last), "pl": lambda: place(s, n),
@@ -580,15 +623,24 @@ def rank_program(g, core, T, topo):
     for name in FIRST.split():
         stage(name, -1 if name in HEAD.split() else 0)
     for s in range(STEPS):
-        for name in ORDER.split():
-            if s or name in HEAD.split() or name not in FIRST.split():
-                stage(name, s)
+        for name in step_order(s, ORDER.split()):
+            stage(name, s)
     dma("y", VV, ["yv"], T.yv[:], T.V[:, 0:B])
     L, Lk = T["L%d" % STEPS], ["L%d" % STEPS, "L%do" % STEPS]
     ts(Lk, "k0", T.k0[:, 0:256], L[:], 512 * MAGIC, 512 * MAGIC, OP.add, OP.subtract)
-    v("tt", Lk + ["k0"], ["cb"], T.cb[:], L[:], T.k0[:, 0:256], OP.subtract)
+    v("tt", Lk + ["k0"], ["cb"], T.cb[:], T.k0[:, 0:256], L[:], OP.subtract)
     dma("y", ["cb"], ["yc"], T.yc[:], T.cb[:])
-    act(["k0"], ["yw32"], T.yw32[:], T.k0[:, 0:256], AF.Copy, scale=1 / 512)
+    act(["k0"], ["yw32"], T.yw32[:], T.k0[:, 0:256], AF.Copy, scale=-1 / 512)
     dma("s", ["yw32"], ["yw"], T.yw[:], T.yw32[0:128:16, :])
     for sem in sorted(total):
         need_wait("g", sem, total[sem])
+    waited = {(sem, val) for e, call, sem, val in calls if call is None}
+    raised = {sem: 0 for sem in cnt}
+    for e, call, sem, val in calls:
+        if call is None:
+            queue[e].wait_ge(T.sem[sem], val)
+        elif (sem, val) in waited:
+            call().then_inc(T.sem[sem], val - raised[sem])
+            raised[sem] = val
+        else:
+            call()

@@ -1,27 +1,25 @@
 from concourse.bass import DstId, RemoteDMATransfer
-from concourse.mybir import AluOpType as OP, ActivationFunctionType as AF
+from concourse.mybir import AluOpType as OP, ActivationFunctionType as AF, AxisListType as AX
 
 STEPS, B = 4, 1024
 LO = 32
 NONE = LO + 8191
 VO = 1600.0
-VW, AW, XWIN = 1536, LO + 8464, LO + 9488
-EMPTY = 512.0 * B
+QW, VW, AW, XWIN = B + 16, 1536, LO + 8464, LO + 9488
+EMPTY = 512 * (B + 1024)
 LIFT = 2.0 ** 20
 RHO, TOP = 1.75, 2.0 ** 88
-KILL = 2.0 ** 90
+KILL = 2.0 ** 92
 MAGIC = 1.5 * 2.0 ** 23
-ONS = "d2".split()
-SHARED = ()
-HEAD = "bo0a bo0b qr up wf op"
-FIRST = "up lc0a bo0a pt bo0b wf qr bt0 bt1 bt2 bt3 nf am0 lc0b op po0a po0b po0c lo"
-LATE = "ld bl0a qc bl0b bl0c bl0d"
-HELP = [0, 0, 0, 0]
+GS, GB, FS, FB = 0.004397, 11.6005, 0.004395, 10.533
 BATCH = 2
-WIDE = (0, 1, 2, 3)
-ORDER = """am0 bt0 am1 bt1 bt2 po0a bt3 po0b po0c nf am2 lo am3 cb3 cb0 cb2 cb1 bl0a ca7 ca4 we0 cb4 cb7 pk0a ca5 dz cv0 pk0b cb5 ca6 cb6 ln0a we1 ln0b ln0c py0 ln0d lt0
-    lt1 pk1a bl0b cv1 rk0 pk1b ct0a bk0 ct0b ln1a ln1b ct0c lt2 ln1c ln1d lt3 lt4 br2 pw py1 lt5 rk1 sl0a tm1 tm0 ct1a bl0c bk1 ct1b sl0b dr ct1c pl0 sl1a bl0d
-    sl1b ll0a pl1 an ll0b ex nr wl bo0a wb bo0b wr up op qr wf"""
+FILL = (2048, 4096)
+CYC, PCYC, GATHER, SCATTER, HOP, DMA, RATE, REMOTE, FIRST = 0.83, 0.42, 1.6, 4.0, 250, 900, 400, 900, 1700
+TURNS = 2
+EARLY = (0, 0, 0, 0)
+THREE, WRITE2 = True, False
+TRIES, SEED, SHIFTS = 1200, 1, (-2500, -1200, -600, -300, -100, 100, 300, 600, 1200, 2500)
+HOOK = []
 SCRATCH = {}
 
 
@@ -31,50 +29,44 @@ def _buf(dtype, n, names, parts=128):
 
 
 _buf("bfloat16", VW, "V")
-_buf("float32", VW, "Q VT")
+_buf("float32", VW, "VT")
+_buf("float32", AW, "Q")
 _buf("float32", B, "Vr")
 _buf("int32", B + 16, "Qin")
 _buf("bfloat16", AW, "A")
 _buf("bfloat16", LO + 8192, "PT")
 _buf("float32", 1024 * (STEPS - 1) + XWIN, "XW")
 _buf("int32", 512, "payS")
-_buf("float32", 512, "payF payA")
-_buf("bfloat16", 2560, "payB")
-_buf("bfloat16", 1024, "ONE cS")
+_buf("float32", 512, "payF")
+_buf("float16", 512, "payR payH")
+_buf("bfloat16", 3072, "payB")
+_buf("bfloat16", 1024, "ONE")
 _buf("int32", 256, "wkI", 8)
 _buf("float16", 256, "wkH", 8)
 _buf("float16", 128, "sel8", 8)
-_buf("float32", 128, "imp qg BLKf BLKg If")
-_buf("bfloat16", 128, "u1 u2 u3 B256 MONE H8")
+_buf("float32", 128, "imp qg BLKf If")
 _buf("float32", 144, "ebi")
-_buf("bfloat16", 144, "EB EBh")
-_buf("float32", 256, "SC SD SP SS nF np qn vn Vg yw32 FALL")
-_buf("float32", 256, "Xb t")
-_buf("float32", 128, "NIf")
-_buf("int32", 8, "pc pj pg pb")
+_buf("float16", 144, "EB")
+_buf("float32", 256, "SC SD SP SS nF np qn vn Vg yw32 FALL Xb u")
+_buf("int32", 8, "pc pj pg")
 _buf("float32", 64, "cf")
-_buf("float32", 16, "l16 LC Wf wa pWf pWc pa")
-_buf("uint16", 16, "WL wU pL sL pU")
-_buf("float16", 128, "N512 BLKh Ih")
-_buf("bfloat16", 128, "Ib NIb N32 BLKb B512 B4a B4q B4n I8k DG WBm WT TRI")
-_buf("bfloat16", 256, "tt GM STEP ZERO thr thr2 x mm D1 D2 e Mb PG Ap An tp OA cb")
-_buf("float16", 256, "Z bR y")
+_buf("float32", 16, "l16 LC Wf wa E16")
+_buf("float32", 32, "pWc pa")
+_buf("uint16", 16, "WL wU pL sL")
+_buf("uint16", 32, "pU")
+_buf("float16", 128, "N512 BLKh BLK1 Ih NIh")
+_buf("bfloat16", 128, "u1 Ib NIb N32 BLKb B256 B4a B4n I4k WBm WT W4 TRI MONE")
+_buf("bfloat16", 2048, "WH")
+_buf("bfloat16", 256, "tt GM STEP ZERO thr x D1 D2 e PG Ap An tp OA cb")
+_buf("float16", 256, "Z Cn bR y xc xo F")
 _buf("uint16", 256, "nU pR")
-_buf("bfloat16", 4096, "eq G cmp")
+_buf("bfloat16", 4096, "eq")
+_buf("float16", 4096, "G cmp")
 for _s in range(STEPS + 1):
     _buf("float32", 256, "L%d" % _s)
-PSUM = ["k%d" % s for s in range(8)]
-for _s in PSUM:
-    SCRATCH[_s] = ("psum", [128, 512], "float32")
+for _s in range(8):
+    SCRATCH["k%d" % _s] = ("psum", [128, 512], "float32")
 SEMAPHORES = ["sv", "ss", "st", "sg", "lx"] + ["rx%d" % s for s in range(STEPS)] + ["d%d" % k for k in range(16)]
-
-
-def step_order(s, order):
-    if s:
-        return order
-    order = [n for n in order if (n in HEAD.split() or n not in FIRST.split()) and n not in LATE.split()]
-    at = order.index("ex") + 1
-    return order[:at] + LATE.split() + order[at:]
 
 
 def split_engines(topo, cores, src):
@@ -95,552 +87,529 @@ def split_engines(topo, cores, src):
     return out
 
 
+def issue_order(calls):
+    n = len(calls)
+    before, behind = [[] for c in calls], [[] for c in calls]
+    for i, c in enumerate(calls):
+        for j, wrote in c["needs"].items():
+            gap = calls[j]["late"] + HOP if waits(calls[j], c, wrote) else 0
+            before[i].append((j, gap))
+            behind[j].append((i, gap))
+
+    def place(order, needs):
+        taken, start, end = {}, [0.0] * n, [0.0] * n
+        for i in order:
+            e, time, banks = calls[i]["queue"], calls[i]["time"], calls[i]["banks"]
+            t, was = max([0.0] + [end[j] + gap for j, gap in needs[i]]), -1.0
+            while t > was:
+                was = t
+                for u in range(int(t) >> 10, (int(t + time) >> 10) + 1):
+                    for a, b, who in taken.get((e, u), ()):
+                        if a < t + time and b > t:
+                            t = b
+                    for bank in banks:
+                        for a, b, who in taken.get((bank, u), ()):
+                            if who != e and a < t + time and b > t:
+                                t = b
+            start[i], end[i] = t, t + time
+            for r, pad in [(e, 0)] + [(bank, HOP) for bank in banks]:
+                for u in range(int(t - pad) >> 10, (int(t + time + pad) >> 10) + 1):
+                    taken.setdefault((r, u), []).append((t - pad, t + time + pad, e))
+        return start, end
+
+    done, way = [False] * n, [0.0] * n
+
+    def longest(i):
+        if not done[i]:
+            way[i], done[i] = calls[i]["time"] + max([calls[i]["late"]] + [gap + longest(j) for j, gap in behind[i]]), True
+        return way[i]
+    for i in range(n - 1, -1, -1):
+        longest(i)
+    start, end = place(sorted(range(n), key=lambda i: (-way[i], i)), before)
+    best = (max(end), start)
+    for turn in range(TURNS):
+        start, end = place(sorted(range(n), key=lambda i: (-end[i], -i)), behind)
+        start, end = place(sorted(range(n), key=lambda i: (-end[i], i)), before)
+        best = min(best, (max(end), start))
+    if HOOK:
+        return HOOK[0](calls, place, before, behind, way, best)
+    draw = [SEED]
+
+    def pick(among):
+        draw[0] = (draw[0] * 1103515245 + 12345) % 2 ** 31
+        return among[(draw[0] >> 8) % len(among)]
+    for turn in range(TRIES):
+        moved = {pick(calls)["kind"]: pick(SHIFTS) for k in range(pick((1, 1, 2, 4)))}
+        key = [best[1][i] + moved.get(c["kind"], 0) for i, c in enumerate(calls)]
+        if turn % 2:
+            for i in range(n):
+                key[i] = max([key[i]] + [key[j] + 0.001 for j, gap in before[i]])
+        else:
+            for i in range(n - 1, -1, -1):
+                key[i] = min([key[i]] + [key[j] - 0.001 for j, gap in behind[i]])
+        start, end = place(sorted(range(n), key=lambda i: (key[i], i)), before)
+        if max(end) <= best[0]:
+            best = (max(end), start)
+    return sorted(range(n), key=lambda i: (best[1][i], i))
+
+
+def waits(a, b, wrote):
+    return wrote is not None and not a["queue"] == b["queue"] == "t"
+
+
 def rank_program(g, core, T, topo):
     q = T.rank_of(core)
     if q is None:
         return
     cores = list(T.cores)
     queue = {"v": g.vector, "s": g.scalar, "t": g.tensor, "g": g, "y": g.sync}
-    semof = {"v": "sv", "s": "ss", "t": "st", "g": "sg"}
-    cnt = {"sv": 0, "ss": 0, "st": 0, "sg": 0}
-    know = {e: {} for e in queue}
-    snap, lastw, readers, total = {}, {}, {}, {}
-    ndma = [0]
-    calls = []
+    calls, uses, group, early = [], {}, {}, [EARLY[0]]
 
-    def need_wait(e, sem, val):
-        if know[e].get(sem, 0) >= val:
-            return
-        calls.append((e, None, sem, val))
-        for s2, v2 in snap.get((sem, val), {}).items():
-            know[e][s2] = max(know[e].get(s2, 0), v2)
-        know[e][sem] = max(know[e].get(sem, 0), val)
+    def X(name, cols=None, rows=None):
+        where, shape, dtype = SCRATCH[name]
+        cols = slice(0, shape[1]) if cols is None else slice(cols, cols + 1) if isinstance(cols, int) else cols
+        r = range(shape[1])[cols]
+        return {"ap": T[name][rows or slice(0, shape[0]), cols], "name": name, "lo": r[0], "hi": r[-1] + 1, "n": len(r), "rows": rows,
+                "wide": dtype in ("float32", "int32"), "psum": where == "psum", "by": None}
 
-    def waits(e, R, W, X=()):
-        need = {}
-        for b in R:
-            if b in lastw:
-                s, v = lastw[b]
-                need[s] = max(need.get(s, 0), v)
-        for b in list(W) + list(X):
-            deps = list(readers.get(b, {}).items())
-            if b in lastw:
-                deps.append(lastw[b])
-            for s, v in deps:
-                if s != semof.get(e) or (e != "t" and b in W):
-                    need[s] = max(need.get(s, 0), v)
-        for s in sorted(need):
-            need_wait(e, s, need[s])
+    def by(win, off):
+        return dict(win, ap=win["ap"].indirect(off["ap"]), n=16 * off["n"], by=off)
 
-    def note(sem, val, R, W, e):
-        sn = dict(know[e])
-        sn[sem] = val
-        snap[(sem, val)] = sn
-        total[sem] = val
-        for b in R:
-            readers.setdefault(b, {})[sem] = val
-        for b in W:
-            lastw[b] = (sem, val)
-            readers[b] = {}
+    def record(e, issue, time, R, W, late=0, sem=None):
+        needs = {}
+        for x, writes in [(x, False) for x in R] + [(x, True) for x in W]:
+            for y, wrote, j in uses.get(x["name"], []):
+                apart = x["rows"] and y["rows"] and x["rows"].step and x["rows"] != y["rows"]
+                if (writes or wrote) and x["lo"] < y["hi"] and y["lo"] < x["hi"] and not apart:
+                    needs[j] = needs.get(j, False) or wrote
+        for x, writes in [(x, False) for x in R] + [(x, True) for x in W]:
+            keep = [u for u in uses.get(x["name"], []) if not (writes and not x["rows"] and x["lo"] <= u[0]["lo"] and u[0]["hi"] <= x["hi"])]
+            uses[x["name"]] = keep + [(x, writes, len(calls))]
+        calls.append({"queue": e, "issue": issue, "time": time, "late": late, "needs": needs, "sem": sem, "early": early[0], "kind": (e, W[0]["name"], W[0]["lo"], R[0]["name"] if R else "") if W else e,
+                      "banks": sorted({x["name"] for x in R + W if x["psum"]})})
 
-    def op(e, name, R, W, *a, **k):
-        waits(e, R, W, [b for b in R if b in PSUM and b not in W])
+    def op(e, name, out, *a, after=(), **k):
+        R = [x for x in list(a) + list(k.values()) if isinstance(x, dict)]
+        sides = [x for x in [out] + R if x["n"] > 1 or x is out]
+        R += [x["by"] for x in [out] + R if x["by"]] + list(after)
+        n = max(x["n"] for x in sides)
+        if name == "matmul":
+            time = 20 + PCYC * max(64, out["n"]) * (4 if a[0]["wide"] else 1)
+        elif e == "g":
+            time = 150 + 2 * CYC * n
+        elif any(x["by"] for x in sides):
+            time = 60 + CYC * n * (SCATTER if out["by"] else GATHER)
+        elif e == "s":
+            time = 80 + CYC * n
+        else:
+            per = (1 if a[0]["psum"] or a[1]["psum"] else 2) if name == "tensor_tensor" else 1 if any(x["wide"] for x in sides) else 0.5
+            time = 10 + CYC * max(64, n * per)
+        args = [x["ap"] if isinstance(x, dict) else x for x in (out,) + a]
+        keys = {u: x["ap"] if isinstance(x, dict) else x for u, x in k.items()}
         eng = queue[e]
-        call = {"tc": lambda: eng.tensor_copy(*a), "tt": lambda: eng.tensor_tensor(*a), "ts": lambda: eng.tensor_scalar(*a),
-                "scan": lambda: eng.tensor_tensor_scan(*a), "ms": lambda: eng.memset(*a), "act": lambda: eng.activation(*a, **k),
-                "mm": lambda: eng.matmul(*a), "iota": lambda: eng.iota(*a, **k), "sel": lambda: eng.affine_select(*a)}[name]
-        sem = semof[e]
-        cnt[sem] += 1
-        calls.append((e, call, sem, cnt[sem]))
-        note(sem, cnt[sem], R, W, e)
+        issue = {"tensor_copy": lambda: eng.tensor_copy(*args), "tensor_tensor": lambda: eng.tensor_tensor(*args), "tensor_scalar": lambda: eng.tensor_scalar(*args),
+                 "scan": lambda: eng.tensor_tensor_scan(*args), "memset": lambda: eng.memset(*args), "reduce": lambda: eng.tensor_reduce(*args),
+                 "activation": lambda: eng.activation(*args, **keys), "matmul": lambda: eng.matmul(*args),
+                 "iota": lambda: eng.iota(*args, **keys), "select": lambda: eng.affine_select(*args)}[name]
+        record(e, issue, time, R, [out])
+        if name == "matmul":
+            if a[2] and out["name"] in group:
+                calls[-1]["needs"].setdefault(group[out["name"]], False)
+            group[out["name"]] = len(calls) - 1
 
-    def dma(e, R, W, out, in_):
-        waits(e, R, W)
+    ndma = [0]
+
+    def dma(e, out, in_, size, after=()):
         sem = "d%d" % ndma[0]
         ndma[0] += 1
-        calls.append((e, lambda: queue[e].dma_start(out, in_).then_inc(T.sem[sem], 16), None, 0))
-        note(sem, 16, R, W, e)
+        o, i = [x["ap"] if isinstance(x, dict) else x for x in (out, in_)]
+        record(e, lambda: queue[e].dma_start(o, i).then_inc(T.sem[sem], 16), 50 if e == "s" else size / RATE,
+               [x for x in [in_] if isinstance(x, dict)] + list(after), [x for x in [out] if isinstance(x, dict)], DMA, (sem, 16, sem, 16))
 
-    def v(name, R, W, *a):
-        op("v", name, R, W, *a)
+    line = {}
 
-    def ts(R, W, out, in_, *a):
-        v("ts", R, [W], out, in_, *a)
+    def in_line(name):
+        if name in line:
+            calls[-1]["needs"].setdefault(line[name], None)
+        line[name] = len(calls) - 1
 
-    def act(R, W, out, in_, func=AF.Copy, **k):
-        op("s", "act", R, W, out, in_, func, **k)
+    def tc(*a):
+        op("v", "tensor_copy", *a)
 
-    def mm(R, W, out, lhsT, rhs, start=True, stop=True):
-        op("t", "mm", R, W, out, lhsT, rhs, start, stop)
+    def tt(*a):
+        op("v", "tensor_tensor", *a)
 
-    def acc(bank, out, terms):
-        for k, (m, R, rhs) in enumerate(terms):
-            mm([m] + R, [bank], out, T[m][:], rhs, k == 0, k == len(terms) - 1)
+    def ts(out, in_, s1, op0, s2=None, op1=None):
+        op("v", "tensor_scalar", out, in_, s1, s2, *([op0, op1] if op1 else [op0]))
 
-    dma("y", [], ["wkI"], T.wkI[:], T.wk[:])
-    dma("y", [], ["payS"], T.payS[:], T.pay[:])
-    dma("y", [], ["Qin"], T.Qin[:, 0:B], T.qu[:])
-    dma("y", [], ["Am"], T.A[:, LO:LO + 8192], T.am[:])
-    dma("y", [], ["Vm"], T.V[:, 0:B], T.vp[:])
+    def scan(*a):
+        op("v", "scan", *a)
 
-    def iota(buf, out, pattern, base, cm):
-        op("g", "iota", [], [buf], out, pattern, base, cm, allow_small_or_imprecise_dtypes=True)
-    iota("pc", T.pc[:, 0:1], [[1, 1]], 0, 1)
-    iota("qg", T.qg[:], [[1, 8], [0, 16]], 0, 0)
-    iota("imp", T.imp[:], [[1, 128]], 0, -1)
-    iota("tt", T.tt[:], [[0, 16], [1, 16]], 0, 0)
-    iota("l16", T.l16[:], [[16, 16]], 1280, 0)
-    iota("ebi", T.ebi[:], [[1, 144]], -15, 0)
-    iota("Apd", T.A[:, LO + 8192:AW], [[0, AW - LO - 8192]], 0, 0)
-    iota("Vp", T.V[:, B:VW], [[0, VW - B]], 0, 0)
+    def act(out, in_, func=AF.Copy, **k):
+        op("s", "activation", out, in_, func, **k)
 
-    def empty_slots(s):
-        for r in range(4):
-            at = 1024 * s + 256 * r
-            iota("XE%d_%d" % (s, r), T.XW[:, at:at + 64], [[0, 64]], -int(EMPTY), 0)
+    def mm(out, lhsT, rhs, start=True, stop=True, after=()):
+        op("t", "matmul", out, lhsT, rhs, start, stop, after=after)
 
-    def select(out, src, *a):
-        op("g", "sel", [src], [out], T[out][:], T[src][:], *a)
+    def acc(out, terms):
+        for k, (m, rhs) in enumerate(terms):
+            mm(out, X(m), rhs, k == 0, k == len(terms) - 1)
 
-    def own_group(out, src):
-        select(src, src, [[-16, 8], [0, 16]], OP.is_ge, 0.0, 0, 1)
-        select(out, src, [[16, 8], [0, 16]], OP.is_ge, 0.0, 15, -1)
+    def iota(out, pattern, base, cm=0):
+        op("g", "iota", out, pattern, base, cm, allow_small_or_imprecise_dtypes=True)
 
+    def select(name, *a):
+        op("g", "select", X(name), X(name), *a)
+
+    def memset(out, val):
+        op("v", "memset", out, val)
+
+    dma("y", X("wkI"), T.wk[:], 8192)
+    dma("y", X("payS"), T.pay[:], 1 << 18)
+    dma("y", X("Qin", slice(0, B)), T.qu[:], 1 << 19)
+    dma("y", X("A", slice(LO, LO + 8192)), T.am[:], 1 << 21)
+    dma("y", X("V", slice(0, B)), T.vp[:], 1 << 18)
+    for k in range(1, 5):
+        calls[k]["needs"][k - 1] = None
+
+    iota(X("pc", 0), [[1, 1]], 0, 1)
+    iota(X("qg"), [[1, 8], [0, 16]], 0)
+    iota(X("imp"), [[1, 128]], 0, -1)
+    iota(X("tt"), [[0, 16], [1, 16]], 0)
+    iota(X("l16"), [[16, 16]], 1280)
+    iota(X("ebi"), [[1, 144]], -15)
+    iota(X("A", slice(LO + 8192, AW)), [[0, AW - LO - 8192]], 0)
+    iota(X("V", slice(B, B + 16)), [[0, 16]], 0)
+    for at in range(0, 1024 * STEPS, 256):
+        iota(X("XW", slice(at, at + 64)), [[0, 64]], -EMPTY)
     col = {}
 
     def c(name):
-        return T.cf[:, col[name]:col[name] + 1]
+        return X("cf", col[name])
 
-    def colop(name, R, call, *a):
+    def column(name, *a):
         col[name] = len(col)
-        v(call, R, [name], c(name), *a)
+        ts(c(name), *a)
 
-    def byrow(table):
-        for is_ in sorted({t[:2] for name, start, terms in table for t in terms}):
-            colop("%s%d" % is_, ["jf"], "ts", c("jf"), float(is_[1]), None, {"lt": OP.is_lt, "eq": OP.is_equal, "ge": OP.is_ge}[is_[0]])
-        yield
-        for n in range(max(len(terms) for name, start, terms in table)):
-            for name, start, terms in table:
-                if n < len(terms):
-                    is_, plus = "%s%d" % terms[n][:2], "%s_%d" % (name, n - 1) if n else start
-                    colop(name if n == len(terms) - 1 else "%s_%d" % (name, n), [is_, plus], "ts", c(is_), float(terms[n][2]),
-                          c(plus) if plus in col else plus, OP.mult, OP.add)
+    def byrow(name, start, terms):
+        for n, (is_, k, value) in enumerate(terms):
+            if (is_, k) not in col:
+                column((is_, k), c("jf"), float(k), {"lt": OP.is_lt, "eq": OP.is_equal, "ge": OP.is_ge}[is_])
+            column(name if n == len(terms) - 1 else (name, n), c((is_, k)), float(value), OP.mult, c((name, n - 1)) if n else start, OP.add)
 
-    def fill(W, out, n, val):
-        act(["ONE"], [W], out, T.ONE[:, 0:n], AF.Copy, scale=val)
+    memset(X("ONE"), 1.0)
+    memset(X("MONE"), -1.0)
+    memset(X("ZERO"), 0.0)
+    memset(X("FALL"), 1 / RHO)
+    memset(X("A", slice(0, LO)), 0.0)
+    memset(X("Qin", slice(B, B + 16)), 8191)
+    memset(X("Q", slice(B, QW)), float(NONE))
+    memset(X("VT", slice(B, B + 16)), VO)
+    memset(X("TRI"), 1 / 32)
+    select("TRI", [[1, 128]], OP.is_ge, 2.0, 0, -1)
+    select("TRI", [[1, 128]], OP.not_equal, -1.0, 0, -1)
+    select("TRI", [[-16, 8], [0, 16]], OP.is_ge, 0.0, 0, 1)
+    select("TRI", [[16, 8], [0, 16]], OP.is_ge, 0.0, 15, -1)
+    scan(X("thr"), X("FALL"), X("ZERO"), 2.54 * RHO * TOP, OP.mult, OP.add)
+    ts(X("pj", 0), X("pc", 0), 15, OP.bitwise_and)
+    ts(X("pg", 0), X("pc", 0), 4, OP.arith_shift_right)
+    for name, src in (("jf", "pj"), ("gf", "pg"), ("pf", "pc")):
+        column(name, X(src, 0), 0.0, OP.add)
+    column("jh", c("jf"), 0.5, OP.add)
+    for name, plus in (("corr", 0.0), ("cor2", -512.0 * B), ("pco", 1024.0), ("cor3", -3072.0), ("cor4", -4096.0)):
+        column(name, c("jf"), -LIFT, OP.mult, 15 * LIFT + plus, OP.add)
+    column("ncor", c("jf"), LIFT, OP.mult, 4096 - 15 * LIFT, OP.add)
+    column("g16", c("gf"), 16.0, OP.mult)
+    column("j256", c("jf"), 256.0, OP.mult, -1040.0 - LO, OP.add)
+    column("jr", c("jf"), -2.0 ** 19 / KILL, OP.mult)
+    byrow("jw", 0.0, [("eq", 4, -5 * 2 ** 19), ("eq", 6, 512 * 32), ("eq", 7, 512)])
+    byrow("icol", c("j256"), [("eq", 4, -1023), ("eq", 5, 1040 + LO - 1280 - 8192), ("ge", 6, -4096)])
+    byrow("ja", 0.0, [("lt", 4, 512), ("eq", 5, -512)])
+    byrow("jz", -1.0, [("lt", 4, 2), ("ge", 6, 1)])
+    byrow("n4", 1.0, [("eq", 4, 1)])
+    byrow("n15", 0.0, [("lt", 15, 1)])
+    column("jv", c("jr"), c(("lt", 4)), OP.mult, c("jw"), OP.add)
+    ts(X("GM"), X("tt"), c("jh"), OP.subtract, 64 * LIFT, OP.mult)
+    ts(X("GM"), X("GM"), LIFT, OP.min)
+    ts(X("BLKb"), X("qg"), c("gf"), OP.is_equal)
+    ts(X("Ib"), X("imp"), 0.0, OP.is_equal)
+    ts(X("EB"), X("ebi"), c("g16"), OP.is_equal, 2.0 ** 15, OP.mult)
+    ts(X("STEP"), X("ONE", slice(0, 256)), c("n4"), OP.mult)
+    ts(X("LC"), X("l16"), c("jf"), OP.add, c("cor3"), OP.add)
+    ts(X("E16"), X("tt", slice(0, 16)), c("jf"), OP.is_equal)
+    tt(X("E16"), X("E16"), X("thr", slice(0, 16)), OP.mult)
+    col["wj"] = len(col)
+    op("v", "reduce", c("wj"), X("E16"), AX.X, OP.max)
+    ts(X("WT"), X("BLKb"), c("wj"), OP.mult, 1 / (2.54 * TOP), OP.mult)
+    for name, src, times in (("N512", "Ib", -512.0), ("If", "Ib", 1.0), ("NIb", "Ib", -1.0), ("N32", "Ib", -32.0), ("Ih", "Ib", 1.0), ("NIh", "Ib", -1.0),
+                             ("I4k", "Ib", 4096.0), ("B256", "BLKb", 256.0), ("BLKf", "BLKb", 1.0), ("BLK1", "BLKb", 1.0), ("WBm", "BLKb", c("jv")),
+                             ("B4a", "BLKb", c("ja")), ("BLKh", "BLKb", c("jz"))):
+        ts(X(name), X(src), times, OP.mult)
+    ts(X("B4n"), X("BLKb"), c(("lt", 4)), OP.mult, -8192.0, OP.mult)
+    ts(X("u1"), X("tt", slice(0, 128)), 4.0, OP.is_lt)
+    tt(X("W4"), X("WT"), X("u1"), OP.mult)
+    for h in range(16):
+        ts(X("WH", slice(128 * h, 128 * h + 128)), X("W4"), TOP * RHO ** (-16 * h), OP.mult)
 
-    def scaled(name, src, by):
-        ts([src, by], name, T[name][:], T[src][:], c(by) if by in col else by, None, OP.mult)
+    rows8 = slice(0, 8)
+    ts(X("sel8"), X("qg", rows=rows8), X("cf", col["pf"], rows8), OP.is_equal, -512.0, OP.mult)
+    ts(X("wkH"), X("wkI"), float(B), OP.add)
+    mm(X("k0", slice(0, 256)), X("sel8"), X("wkH"))
+    tc(X("L0"), X("k0", slice(0, 256)))
 
-    v("ms", [], ["ONE"], T.ONE[:], 1.0)
-    v("ms", [], ["u1"], T.u1[:], 1 / 32)
-    select("u1", "u1", [[1, 128]], OP.is_ge, 2.0, 0, -1)
-    select("u1", "u1", [[1, 128]], OP.not_equal, -1.0, 0, -1)
-    own_group("TRI", "u1")
-    iota("PTa", T.PT[:, 0:LO + 3072], [[0, LO + 3072]], 1, 0)
-    for k in range(2):
-        fill("PTb%d" % k, T.PT[:, LO + 3072 + 1024 * k:LO + 4096 + 1024 * k], 1024, 1.0)
-    v("ms", [], ["ZERO"], T.ZERO[:], 0.0)
-    v("ms", [], ["FALL"], T.FALL[:], 1 / RHO)
-    v("ms", [], ["Apl"], T.A[:, 0:LO], 0.0)
-    v("ms", [], ["Qip"], T.Qin[:, B:B + 16], 8191)
-    v("scan", ["FALL", "ZERO"], ["thr"], T.thr[:], T.FALL[:], T.ZERO[:], 2.54 * RHO * TOP, OP.mult, OP.add)
-    ts(["pc"], "pj", T.pj[:, 0:1], T.pc[:, 0:1], 15, None, OP.bitwise_and)
-    ts(["pc"], "pg", T.pg[:, 0:1], T.pc[:, 0:1], 4, None, OP.arith_shift_right)
-    colop("jf", ["pj"], "tc", T.pj[:, 0:1])
-    colop("gf", ["pg"], "tc", T.pg[:, 0:1])
-    colop("pf", ["pc"], "tc", T.pc[:, 0:1])
-    for k in range(4):
-        ts(["pj"], "pb%d" % k, T.pb[:, k:k + 1], T.pj[:, 0:1], k, 1, OP.arith_shift_right, OP.bitwise_and)
-    pf8 = T.cf[0:8, col["pf"]:col["pf"] + 1]
-    ts(["qg", "pf"], "sel8", T.sel8[:], T.qg[0:8, :], pf8, -512.0, OP.is_equal, OP.mult)
-    v("tc", ["wkI"], ["wkH"], T.wkH[:], T.wkI[:])
-    mm(["sel8", "wkH"], ["k0"], T.k0[:, 0:256], T.sel8[:], T.wkH[:])
-    v("tc", ["payS"], ["payF"], T.payF[:], T.payS[:])
-    for k in range(3):
-        act(["payF"], ["b%d" % k], T.payB[:, 512 * k:512 * k + 512], T.payF[:], AF.Sign, bias=0.5 - 1024 * (k + 1))
-    act(["payF"], ["payA"], T.payA[:], T.payF[:], AF.Identity, bias=-15.5 / 32, scale=1 / 32)
-    ts(["qg", "gf"], "BLKb", T.BLKb[:], T.qg[:], c("gf"), None, OP.is_equal)
-    ts(["imp"], "Ib", T.Ib[:], T.imp[:], 0.0, None, OP.is_equal)
-    for k in range(4):
-        colop("f%d" % k, ["pb%d" % k], "ts", T.pb[:, k:k + 1], RHO ** -(2 ** k) - 1.0, 1.0, OP.mult, OP.add)
-    colop("jh", ["jf"], "ts", c("jf"), 0.5, None, OP.add)
-    colop("corr", ["jf"], "ts", c("jf"), -LIFT, 15 * LIFT, OP.mult, OP.add)
-    colop("f01", ["f0", "f1", "f2"], "ts", c("f0"), c("f1"), c("f2"), OP.mult, OP.mult)
-    ts(["tt", "jh"], "GM", T.GM[:], T.tt[:], c("jh"), 64 * LIFT, OP.subtract, OP.mult)
-    v("tc", ["k0"], ["L0"], T.L0[:], T.k0[:, 0:256])
-    ts(["GM"], "GM", T.GM[:], T.GM[:], LIFT, None, OP.min)
-    ts(["BLKb", "f01", "f3"], "WT", T.WT[:], T.BLKb[:], c("f01"), c("f3"), OP.mult, OP.mult)
-    for name, by in (("N512", -512.0), ("If", 1.0), ("NIf", -1.0), ("NIb", -1.0), ("N32", -32.0)):
-        scaled(name, "Ib", by)
-    act(["payA"], ["payA"], T.payA[:], T.payA[:], AF.Identity, bias=MAGIC)
-    act(["payA"], ["b3"], T.payB[:, 1536:2048], T.payA[:], AF.Identity, bias=-MAGIC)
-    acc("k3", T.k3[:], [("If", ["payF"], T.payF[:]), ("N32", ["b3"], T.payB[:, 1536:2048])])
-    act(["k3"], ["b4"], T.payB[:, 2048:2560], T.k3[:])
-    colop("n15", ["jf"], "ts", c("jf"), 15.0, None, OP.is_lt)
-    PTf = ["PTa"] + ["PTb%d" % k for k in range(3)]
+    a, b = FILL[0], FILL[0] + FILL[1]
+    iota(X("PT", slice(0, a)), [[0, a]], 1)
+    for at in range(a, b, 1024):
+        act(X("PT", slice(at, at + 1024)), X("ONE"), AF.Silu, scale=1.27846)
+        calls[-1]["time"] += 1300 * (at == a)
+        in_line("fill")
+    for at in range(b, LO + 8192, 1024):
+        memset(X("PT", slice(at, min(at + 1024, LO + 8192))), 1.0)
+    tc(X("payF"), X("payS"))
+    act(X("payR"), X("payF"), AF.Identity, scale=1 / 1024, bias=1025 - 0.4995)
+    act(X("payH"), X("payF"), AF.Identity, scale=1 / 32, bias=1025 - 15.5 / 32)
+    ts(X("payR", 511), X("payR", 511), c("n15"), OP.mult)
+    part = [X("payB", slice(512 * k, 512 * k + 512)) for k in range(6)]
+    for r in range(4):
+        ts(part[r], X("payR"), 1025.0 + r, OP.not_equal, -KILL, OP.mult)
+    ts(part[4], X("payH"), 1025.0, OP.subtract)
+    acc(X("k7"), [("If", X("payF")), ("N32", part[4])])
+    act(part[5], X("k7"))
+    for k, j in enumerate((0, 1, 2, 3, 6, 7)):
+        dma("y", X("PT", slice(LO, LO + 8192), slice(j, 128, 16)), part[k], 1 << 17, after=[X("V", slice(0, B))])
 
-    def payee_table():
-        v("ms", [], ["PTb2"], T.PT[:, LO + 5120:LO + 8192], 1.0)
-        for k in range(3):
-            end = T.payB[:, 512 * k + 511:512 * k + 512]
-            ts(["b%d" % k, "n15"], "b%d" % k, end, end, c("n15"), None, OP.mult)
-        for j in range(5):
-            dma("y", ["b%d" % j, "Am"] + PTf, ["PT%d" % j], T.PT[j::16, LO:LO + 8192], T.payB[:, 512 * j:512 * j + 512])
-
-    def later_constants():
-        colop("g16", ["gf"], "ts", c("gf"), 16.0, None, OP.mult)
-        colop("pco", ["corr"], "ts", c("corr"), 1024.0, None, OP.add)
-        colop("n4", ["jf"], "ts", c("jf"), 4.0, None, OP.not_equal)
-        colop("j256", ["jf"], "ts", c("jf"), 256.0, -1040.0 - LO, OP.mult, OP.add)
-        rows = byrow([("dm", 0.0, [("lt", 3, -2 * KILL)]), ("da", 0.0, [("lt", 3, KILL), ("eq", 5, 3 * KILL)]),
-                      ("jw", 0.0, [("lt", 3, -512 * 512), ("eq", 3, 512 * 32), ("eq", 4, 512), ("eq", 5, -512 * 1536)]),
-                      ("icol", "j256", [("eq", 4, 2 * (1040 + LO) - 1025), ("eq", 5, 8192 + 1040 + LO - 1280)]),
-                      ("jq", 0.0, [("lt", 4, 8192), ("eq", 4, LO - 8192)]),
-                      ("jt", 0.0, [("ge", 4, 64 * KILL), ("ge", 6, -128 * KILL)])])
-        next(rows)
-        ts(["ebi", "g16"], "EB", T.EB[:], T.ebi[:], c("g16"), None, OP.is_equal)
-        ts(["tt", "jf"], "u3", T.u3[:], T.tt[:, 0:128], c("jf"), None, OP.is_gt)
-        scaled("BLKh", "BLKb", 1.0)
-        for name, by in (("B4n", -8192.0), ("B4a", 512.0)):
-            ts(["BLKb", "lt4"], name, T[name][:], T.BLKb[:], c("lt4"), by, OP.mult, OP.mult)
-        empty_slots(0)
-        empty_slots(1)
-        yield
-        next(rows, None)
-        ts(["u3", "dm", "da"], "u3", T.u3[:], T.u3[:], c("dm"), c("da"), OP.mult, OP.add)
-        own_group("DG", "u3")
-        empty_slots(2)
-        empty_slots(3)
-        ts(["thr", "lt4", "jt"], "thr2", T.thr2[:], T.thr[:], c("lt4"), c("jt"), OP.mult, OP.add)
-        ts(["ONE", "n4"], "STEP", T.STEP[:], T.ONE[:, 0:256], c("n4"), None, OP.mult)
-        for name, src, by in (("B512", "BLKb", 512.0), ("BLKf", "BLKb", 1.0), ("WBm", "BLKb", "jw"), ("B4q", "BLKb", "jq"), ("I8k", "Ib", 8192.0)):
-            scaled(name, src, by)
-
-    PTs = PTf + ["PT%d" % j for j in range(5)]
     route = split_engines(topo, cores, core)
     arrive = sum(len(split_engines(topo, cores, s)[core]) for s in cores if s != core)
-    sent = [0]
+    leave = sum(len(e) for e in route.values())
 
     def exchange(s):
-        land, at = "L%d" % (s + 1), 1024 * s
-        waits("g", ["XW"], [])
-        tr = []
+        land, tr = "L%d" % (s + 1), []
+        slots = [X("XW", slice(1024 * s + r * 256, 1024 * s + r * 256 + 64)) for r in range(4)]
         for r, d in enumerate(cores):
-            if d == core:
-                continue
-            m = 0
-            for e in route[d]:
-                m |= 1 << e
-            tr.append(RemoteDMATransfer(dst_ids=[DstId(rid=topo.addr(d)[0], pnc=topo.addr(d)[1])], dma_engine_mask=m, remote_sem=T.sem["rx%d" % s],
-                                        src=T.XW[:, at + r * 256:at + r * 256 + 64], dst=T[land][:, q * 64:q * 64 + 64]))
-            sent[0] += len(route[d])
-        calls.append(("g", lambda: g.remote_dma_fused(tr, local_sem=T.sem.lx), None, 0))
-        readers["XW"]["lx"] = total["lx"] = sent[0]
-        if "ex" in ONS:
-            act(["XW"], [land + "o"], T[land][:, q * 64:q * 64 + 64], T.XW[:, at + q * 256:at + q * 256 + 64])
+            if d != core:
+                tr.append(RemoteDMATransfer(dst_ids=[DstId(rid=topo.addr(d)[0], pnc=topo.addr(d)[1])], dma_engine_mask=sum(1 << e for e in route[d]),
+                                            remote_sem=T.sem["rx%d" % s], src=slots[r]["ap"], dst=T[land][:, q * 64:q * 64 + 64]))
+        record("g", lambda: g.remote_dma_fused(tr, local_sem=T.sem.lx), 100, [x for r, x in enumerate(slots) if r != q],
+               [X(land, slice(64 * r, 64 * r + 64)) for r in range(4) if r != q], REMOTE + FIRST * (s == 0), ("rx%d" % s, arrive, "lx", leave * (s + 1)))
+        tc(X(land, slice(64 * q, 64 * q + 64)), slots[q])
+
+    def w(o, plus=0):
+        return slice(plus + o.start // 16, plus + o.stop // 16)
+
+    def ends(name, o):
+        return X(name, slice(o.start + 15, o.stop, 16))
+
+    def ps(name, o):
+        if name in ("twin", "slot"):
+            bank, at = 5 + o.start // 128, {"twin": 128, "slot": 256}[name]
         else:
-            v("tc", ["XW"], [land + "o"], T[land][:, q * 64:q * 64 + 64], T.XW[:, at + q * 256:at + q * 256 + 64])
-        lastw[land] = ("rx%d" % s, arrive)
-        total["rx%d" % s] = arrive
+            bank, at = {0: 3, 128: 4, 192: 7}[o.start], {"score": 0, "won": 128, "best": 256, "line": 384}[name]
+        return X("k%d" % bank, slice(at, at + o.stop - o.start))
 
-    AA, VV, QQ, VT = ["Am", "Apd", "Apl"], ["Vm", "Vp"], ["Qm", "Qp"], ["VTm", "VTp"]
-    ddk = ["k2", "k6"]
+    ALL, HALF = slice(0, 256), [slice(0, 128), slice(128, 256)]
+    own = slice(64 * q, 64 * q + 64)
+    pieces = [own] + [slice(64 * r, 64 * r + 64) for r in range(4) if r != q]
+    parts = [HALF[0], slice(128, 192), slice(192, 256)] if THREE else HALF
+    parts = sorted(parts, key=lambda o: o != own)
 
-    def half(h):
-        return (slice(128 * h, 128 * h + 128), slice(8 * h, 8 * h + 8)) if h < 2 else (slice(0, 256), slice(0, 16))
+    def twins(out, h, o, row, s1, op0, s2, op1, matrix, start, stop):
+        eq = X("eq", slice(256 * h + o.start, 256 * h + o.stop))
+        ts(eq, X(row, o), s1, op0, s2, op1)
+        in_line("twins")
+        return lambda after: mm(out, matrix, eq, start, stop, after), eq
 
-    def of(name, h):
-        return [name + "0", name + "1"] if h == 2 else ["%s%d" % (name, h)]
+    def batches(pairs):
+        pairs = list(pairs)
+        for k, (add, made) in enumerate(pairs):
+            add([m for a_, m in pairs[k - k % BATCH:k - k % BATCH + BATCH]])
 
-    def bank_offsets(s):
-        v("scan", ["GM", "L%d" % s, "L%do" % s], ["SC"], T.SC[:], T.GM[:], T["L%d" % s][:], 0.0, OP.add, OP.max)
-        yield
-        ts(["SC", "corr"], "WL", T.WL[:], T.SC[:, 15::16], c("corr"), -1 / 512, OP.subtract, OP.mult)
-
-    def queue_rows(s):
+    def head(s, o):
+        words = X("XW", slice(1024 * (s - 1) + 256 * q, 1024 * (s - 1) + 256 * q + 64)) if s and o == own else X("L%d" % s, o)
+        scan(X("SC", o), X("GM", o), words, 0.0, OP.add, OP.max)
+        in_line("banks")
+        ts(X("WL", w(o)), ends("SC", o), c("cor2"), OP.subtract, -1 / 512, OP.mult)
+        in_line("lists")
         if s:
-            ts(QQ + ["WL"], "nU", T.nU[:], T.Q[:].indirect(T.WL[:]), 0.25, None, OP.add)
+            ts(X("nU", o), by(X("Q", slice(0, QW)), X("WL", w(o))), 0.25, OP.add)
         else:
-            ts(["Qin", "Qip", "WL"], "nU", T.nU[:], T.Qin[:].indirect(T.WL[:]), float(LO), None, OP.add)
+            ts(X("nU", o), by(X("Qin"), X("WL", w(o))), float(LO), OP.add)
+        in_line("rows")
 
-    def row_numbers(s):
-        if s and "nf" in ONS:
-            act(QQ + ["WL"], ["nF"], T.nF[:], T.Q[:].indirect(T.WL[:]), AF.Identity, bias=0.25)
-        else:
-            v("tc", ["nU"], ["nF"], T.nF[:], T.nU[:])
-
-    def last_constants():
-        scaled("Ih", "Ib", 1.0)
-        ts(["l16", "jf", "pco"], "LC", T.LC[:], T.l16[:], c("jf"), c("pco"), OP.add, OP.add)
-
-    def old_positions(s):
-        if s:
-            act(VT + ["WL"], ["Vg"], T.Vg[:], T.VT[:].indirect(T.WL[:]), AF.Identity, bias=-EMPTY)
-        else:
-            v("tc", VV + ["WL"], ["x"], T.x[:], T.V[:].indirect(T.WL[:]))
-
-    def unpack(s):
-        L, Lk = T["L%d" % s], ["L%d" % s, "L%do" % s]
-        if "up" in ONS and s:
-            act(Lk, ["bR"], T.bR[:], L[:], AF.Identity, scale=-1 / 512, bias=float(B))
-        else:
-            ts(Lk, "bR", T.bR[:], L[:], -1 / 512, float(B), OP.mult, OP.add)
-        if s:
-            acc("k0", T.k0[:, 0:256], [("NIf", Lk, L[:]), ("N512", ["bR"], T.bR[:])])
+    def amounts(o):
+        act(X("G", slice(16 * o.start, 16 * o.stop)), by(X("A"), X("nU", o)), AF.Silu, scale=GS, bias=-GB)
+        in_line("amounts")
 
     def positions(s):
+        L = X("L%d" % s)
+        ts(X("bR"), L, -1 / 512, OP.mult)
         if s:
-            v("tt", ["Vg", "k0"], ["y"], T.y[:], T.Vg[:], T.k0[:, 0:256], OP.subtract)
-        yield
-        if s:
-            ts(["y"], "x", T.x[:], T.y[:], VO, -255.0, OP.subtract, OP.max)
-        acc("k1", T.k1[:, 0:256], [("NIb", ["x"], T.x[:])])
-        yield
-        if "mm" in ONS:
-            act(["x"], ["mm"], T.mm[:], T.x[:], AF.Relu, scale=-1.0)
+            acc(X("k0", ALL), [("N512", X("bR"))])
+            tt(X("Vg"), by(X("VT", slice(0, QW)), X("WL")), L, OP.add)
+            tt(X("y"), X("Vg"), X("k0", ALL), OP.subtract)
         else:
-            ts(["x"], "mm", T.mm[:], T.x[:], -1.0, 0.0, OP.mult, OP.max)
-        acc("k5", T.k5[:, 256:512], [("BLKb", ["mm"], T.mm[:])])
-        acc("k7", T.k7[:, 256:512], [("Ib", ["mm"], T.mm[:])])
-
-    def twins(h0, lo, hi, Rk, Rb, Wk, Wb, stop=False):
-        for b in range(h0, h0 + 4, BATCH):
-            es = ["eq%d_%d" % (h, max(lo, 16 * h) // 128) for h in range(b, b + BATCH)]
-            for h in range(b, b + BATCH):
-                l0 = max(lo, 16 * h)
-                ts(Rk + [Wk], es[h - b], T.eq[:, 256 * h + l0:256 * h + hi], Rb[:, l0:hi], Wb[:, h:h + 1], TOP * RHO ** (-16 * h), OP.is_equal, OP.mult)
-            for h in range(b, b + BATCH):
-                l0 = max(lo, 16 * h)
-                mm(["WT"] + es, ["k2"], T.k2[:, l0:hi], T.WT[:], T.eq[:, 256 * h + l0:256 * h + hi], h == 0, stop and h == 15)
-
-    def bank_twins(n):
-        twins(4 * n, 0, 256, ["bR"], T.bR, "Wf", T.Wf, "d1" not in ONS)
-
-    def line_twins(n):
-        o, h0 = min(n // 2, 1), 4 * n - 8 * (n > 1)
-        twins(h0, 128 * o, 128 * o + 128, ["pR%d" % o], T.pR, "pWf%d" % (h0 // 8), T.pWf)
-
-    def all_line_twins(n):
-        twins(4 * n, 0, 256, of("pR", 2), T.pR, "pWf%d" % (n // 2), T.pWf)
-
-    def amounts(k, s):
-        a, b = (64 * k, min(64 * k + 64, 256 - HELP[s])) if k < 4 else (256 - HELP[s], 256)
-        if k < 4:
-            act(AA + ["nU"], ["g%d" % k], T.G[:, 16 * a:16 * b], T.A[:].indirect(T.nU[:, a:b]))
-        elif HELP[s]:
-            v("tc", AA + ["nU"], ["g4"], T.G[:, 16 * a:16 * b], T.A[:].indirect(T.nU[:, a:b]))
-
-    scored = [0, 0]
-
-    def compare(n, second):
-        h, wide = n // 4, n in WIDE
-        l0, w = (128 * h, 128) if wide else (128 * h + 64 * second, 64)
-        out = T.k3[:, half(h)[0]]
-        for i in range(4 * (n % 4), 4 * (n % 4) + 4):
-            if i % BATCH == 0 and n not in SHARED and (second or not wide):
-                for k in range(i, i + BATCH):
-                    v("tt", ["g%d" % (l0 // 64), "g%d" % (2 * h + second), "k1"] + ["g4"] * (h * second), ["c%d_%d" % (k, 2 * h + second)],
-                      T.cmp[:, 256 * k + l0:256 * k + l0 + w], T.G[:, 16 * l0 + k:16 * (l0 + w):16], T.k1[:, l0:l0 + w], OP.is_ge)
-            ck = ["c%d_%d" % (k, 2 * h + u) for k in range(i - i % BATCH, i - i % BATCH + BATCH) for u in range(2)]
-            if second:
-                scored[h] = scored[h] % 16 + 1
-                if scored[h] == 1 and h and SHARED:
-                    mm(["H8", "ONE"], ["k3"], out, T.H8[:], T.ONE[:, 0:128], True, False)
-                first = scored[h] == 1 and not (h and SHARED)
-                if n in SHARED:
-                    at = 512 * (n % 2) + 128 * (i % 4)
-                    mm(["cS%d" % (n % 2), "EBh"], ["k3"], out, T.EBh[:, 15 - i:143 - i], T.cS[:, at:at + 128], first, scored[h] == 16)
-                else:
-                    mm(ck + ["EB"], ["k3"], out, T.EB[:, 15 - i:143 - i], T.cmp[:, 256 * i + 128 * h:256 * i + 128 * h + 128], first, scored[h] == 16)
-
-    def signs(n):
-        if n in SHARED:
-            h, d = n // 4, ("k6", "k0")[n % 2]
-            for i in range(4):
-                acc(d, T[d][:, 128 * i:128 * i + 128], [("Ib", ["x"], T.x[:, half(h)[0]]),
-                                                        ("Ib", ["g%d" % (2 * h), "g%d" % (2 * h + 1), "g4"], T.G[:, 2048 * h + 4 * (n % 4) + i:2048 * h + 2048:16])])
-            act([d], ["cS%d" % (n % 2)], T.cS[:, 512 * (n % 2):512 * (n % 2) + 512], T[d][:], AF.Sign, bias=0.5)
-
-    def weigh(h):
-        o = half(h)[0]
-        act(["k3"], of("e", h), T.e[:, o], T.k3[:, o], AF.Silu, bias=-85.6, scale=4.6)
-        acc("k4", T.k4[:, o], [("TRI", of("e", h), T.e[:, o])])
-
-    def covered():
-        if "d2" in ONS:
-            act(["k5"], ["D2"], T.D2[:], T.k5[:, 256:512], AF.Relu, bias=1.0, scale=-1.0)
+            ts(X("y"), by(X("V", slice(0, QW)), X("WL")), VO, OP.add)
+        ts(X("xc"), X("y"), VO - 255, OP.max, VO, OP.min)
+        act(X("F"), X("xc"), AF.Silu, scale=FS, bias=-FB - FS * VO)
+        in_line("amounts")
+        if s == STEPS - 1:
+            ts(X("x"), X("y"), VO, OP.subtract, -255.0, OP.max)
         else:
-            ts(["k5"], "D2", T.D2[:], T.k5[:, 256:512], 0.5, None, OP.is_lt)
+            ts(X("xo"), X("y"), VO - 255, OP.max)
 
-    def pick(h):
-        o = half(h)[0]
-        M = T.k4[:, 256 + o.start:256 + o.stop]
-        terms = [("B512", ["D2"], T.D2[:, o])]
-        terms += [("B256", ["ONE"], T.ONE[:, o]), ("B256", ["D1"], T.D1[:, o])] if "d1" in ONS else [("B512", ["D1"], T.D1[:, o])]
-        if "m%d" % h in ONS:
-            act(["k4"], ["k4"], M, T.k4[:, o], AF.Sign)
-            terms += [("BLKg", ["nF"], T.nF[:, o]), ("BLKg", of("np", h), T.np[:, o])]
-        else:
-            ts(["k4"], "k4", M, T.k4[:, o], 0.0, None, OP.is_gt)
-            terms += [("BLKf", of("np", h), T.np[:, o])]
-        yield
-        v("tt", ["k4", "nF"], of("np", h), T.np[:, o], M, T.nF[:, o], OP.mult)
-        acc("k5", T.k5[:, o], terms)
+    def banks():
+        ts(X("Wf"), X("WL"), float(B), OP.add)
+        mm(X("k2", ALL), X("MONE", rows=slice(0, 1)), X("thr", rows=slice(0, 1)), True, False)
+        batches(twins(X("k2", slice(16 * h, 256)), h, slice(16 * h, 256), "bR", X("Wf", h), OP.is_equal, TOP * RHO ** (-16 * h), OP.mult,
+                      X("WT"), False, h == 15) for h in range(16))
+        act(X("D1"), X("k2", ALL), AF.Sign)
+        acc(X("k0", slice(256, 512)), [("BLK1", X("xc")), ("B256", X("D1"))])
+        act(X("D2"), X("k0", slice(256, 512)), AF.Sign, bias=4096.5 - 16 * VO)
+        acc(X("k2", slice(256, 512)), [("Ih", X("bR")), ("I4k", X("D1"))])
+        scan(X("SD"), X("GM"), X("k2", slice(256, 512)), 0.0, OP.add, OP.max)
+        tt(X("wa"), ends("SD", ALL), X("LC"), OP.min)
+        ts(X("wU"), X("wa"), c("cor3"), OP.subtract)
 
-    def losers():
-        if "d1" in ONS:
-            mm(["MONE", "thr"], ["k2"], T.k2[:, 0:256], T.MONE[0:1, :], T.thr[0:1, :], False, True)
-            act(["k2"], ["D1"], T.D1[:], T.k2[:, 0:256], AF.Sign)
-        else:
-            v("tt", ["k2", "thr"], ["D1"], T.D1[:], T.k2[:, 0:256], T.thr[:], OP.is_ge)
+    def compare(o, i):
+        made = X("cmp", slice(256 * i + o.start, 256 * i + o.stop))
+        scan(made, X("G", slice(16 * o.start + i, 16 * o.stop, 16)), X("F", o), 0.0, OP.min, OP.mult)
+        in_line("rows")
+        return lambda after: mm(ps("score", o), X("EB", slice(15 - i, 143 - i)), made, i == 0, i == 15, after), made
 
-    def lines(h):
-        o, w = half(h)
-        v("scan", ["GM", "k5"], of("SP", h), T.SP[:, o], T.GM[:, o], T.k5[:, o], 0.0, OP.add, OP.max)
-        yield
-        v("tc", ["k5"], of("pR", h), T.pR[:, o], T.k5[:, o])
-        yield
-        sp = T.SP[:, o.start + 15:o.stop:16]
-        v("ts", of("SP", h) + ["corr"], of("pL", h), T.pL[:, w], sp, c("corr"), float(NONE), OP.subtract, OP.min)
-        yield
-        v("ts", of("SP", h) + ["corr"], of("pWf", h), T.pWf[:, w], sp, c("corr"), float(NONE), OP.subtract, OP.min)
+    def lines(s, o):
+        tc(X("nF", o), X("nU", o))
+        batches(compare(o, i) for i in range(16))
+        act(X("e", o), ps("score", o), AF.Silu, bias=-85.6, scale=4.6 * 512)
+        acc(ps("won", o), [("TRI", X("e", o))])
+        mm(ps("line", o), X("B256"), X("D2", o), True, False)
+        ts(ps("best", o), ps("won", o), 0.0, OP.is_gt, float(NONE), OP.mult)
+        tt(X("np", o), ps("best", o), X("nF", o), OP.min)
+        mm(ps("line", o), X("BLKf"), X("np", o), False, True)
+        ts(X("pR", o), ps("line", o), 4096.0, OP.add)
+        scan(X("SP", o), X("GM", o), ps("line", o), 0.0, OP.add, OP.max)
+        ts(X("pL", w(o)), ends("SP", o), c("cor4"), OP.subtract, float(NONE), OP.min)
+        act(X("PG", o), by(X("PT"), X("pL", w(o))))
+        act(X("Ap", o), by(X("A"), X("pL", w(o))))
+        if s < STEPS - 1:
+            tt(X("qn", o), ps("best", o), X("nF", o), OP.max)
 
-    def payees(h):
-        o, w = half(h)
-        act(PTs + of("pL", h), of("PG", h), T.PG[:, o], T.PT[:].indirect(T.pL[:, w]))
-        act(AA + of("pL", h), of("Ap", h), T.Ap[:, o], T.A[:].indirect(T.pL[:, w]))
+    def draws(s, h):
+        o = HALF[h]
+        twin = ps("twin", o)
+        mm(twin, X("MONE", rows=slice(0, 1)), X("thr", o, slice(0, 1)), True, False)
+        batches(twins(X(twin["name"], slice(128 + max(16 * k - o.start, 0), 256)), k, slice(max(16 * k, o.start), o.stop), "pR", X("SP", 16 * k + 15), OP.subtract,
+                      c("ncor"), OP.is_equal, X("WH", slice(128 * k, 128 * k + 128)), False, k == o.stop // 16 - 1) for k in range(o.stop // 16))
+        tt(X("OA", o), twin, X("PG", o), OP.is_lt)
+        scan(X("Cn", o), X("OA", o), X("STEP", o), X("Cn", 127) if h else c("icol"), OP.add, OP.subtract)
+        scan(X("Z", o), X("Cn", o), X("OA", o), 0.0, OP.min, OP.mult)
+        acc(ps("slot", o), [("B4n", X("OA", o)), ("BLKh", X("Z", o))])
+        scan(X("SS", o), X("GM", o), ps("slot", o), 0.0, OP.add, OP.max)
+        ts(X("sL", w(o)), ends("SS", o), c("corr"), OP.subtract)
+        left, base = X("k1", slice(256 + o.start, 256 + o.stop)), X("k1", o)
+        acc(left, [("Ih", X("xc", o)), ("Ib", X("Ap", o))])
+        act(X("u", o), left, AF.Relu, scale=-1.0, bias=VO)
+        act(X("An", o), left, AF.Relu, bias=-VO)
+        acc(base, [("NIh", X("xc", o)), ("WBm", X("PG", o))])
+        act(X("Xb", o), base, AF.Identity, scale=-1.0, bias=-VO)
+        tt(by(X("XW", slice(1024 * s, 1024 * s + XWIN)), X("sL", w(o))), X("Xb", o), X("u", o), OP.add)
 
-    def payee_banks(h):
-        o, d = half(h)[0], ("k0", "k1")[h]
-        acc(d, T[d][:, o], [("WBm", of("PG", h), T.PG[:, o])])
-        act([d], of("Xb", h), T.Xb[:, o], T[d][:, o], AF.Copy, scale=-1.0)
-
-    def draws(h):
-        o = half(h)[0]
-        v("tt", of("Ap", h) + ["k7"], of("t", h), T.t[:, o], T.Ap[:, o], T.k7[:, 256 + o.start:256 + o.stop], OP.min)
-
-    def kept():
-        acc("k1", T.k1[:, 256:512], [("NIb", ["mm"], T.mm[:]), ("Ib", of("Ap", 2), T.Ap[:])])
-        act(["k1"], ["An"], T.An[:], T.k1[:, 256:512], AF.Relu)
-
-    def ranks(h):
-        o = half(h)[0]
-        mm(["DG"] + of("PG", h), ["k2"], T.k2[:, o], T.DG[:], T.PG[:, o], False, True)
-
-    def counts(h):
-        o = half(h)[0]
-        v("tt", ["k2", "thr2"], of("OA", h), T.OA[:, o], T.k2[:, o], T.thr2[:, o], OP.is_lt)
-        yield
-        v("scan", of("OA", h) + ["STEP", "icol", "k7"], ["k7"], T.k7[:, o], T.OA[:, o], T.STEP[:, o], T.k7[:, 127:128] if h == 1 else c("icol"), OP.add, OP.subtract)
-        yield
-        v("tt", ["k7"] + of("OA", h), of("Z", h), T.Z[:, o], T.k7[:, o], T.OA[:, o], OP.mult)
-        acc("k6", T.k6[:, o], [("B4n", of("OA", h), T.OA[:, o]), ("BLKh", of("Z", h), T.Z[:, o])])
-
-    def slots(h):
-        o, w = half(h)
-        v("scan", ["GM", "k6"], of("SS", h), T.SS[:, o], T.GM[:, o], T.k6[:, o], 0.0, OP.add, OP.max)
-        yield
-        v("ts", of("SS", h) + ["corr"], of("sL", h), T.sL[:, w], T.SS[:, o.start + 15:o.stop:16], c("corr"), None, OP.subtract)
-
-    def place(s, h):
-        o, w = half(h)
-        v("tt", of("Xb", h) + of("t", h) + of("sL", h) + ["XE%d_%d" % (k, r) for k in range(s, STEPS) for r in range(4)], ["XW"],
-          T.XW[:, 1024 * s:1024 * s + XWIN].indirect(T.sL[:, w]), T.Xb[:, o], T.t[:, o], OP.subtract)
-
-    def bank_list():
-        acc("k6", T.k6[:, 256:512], [("Ih", ["bR"], T.bR[:]), ("I8k", ["D1"], T.D1[:])])
-        yield
-        v("scan", ["GM", "k6"], ["SD"], T.SD[:], T.GM[:], T.k6[:, 256:512], 0.0, OP.add, OP.max)
-        yield
-        v("tt", ["SD", "LC"], ["wa"], T.wa[:], T.SD[:, 15::16], T.LC[:], OP.min)
-        yield
-        ts(["wa", "pco"], "wU", T.wU[:], T.wa[:], c("pco"), None, OP.subtract)
-
-    def best_rows(h):
-        o = half(h)[0]
-        act(["k4"], of("Mb", h), T.Mb[:, o], T.k4[:, 256 + o.start:256 + o.stop], AF.Relu)
-
-    def drawn(last):
-        if not last:
-            acc("k4", T.k4[:, 0:256], [("I8k", of("Mb", 2), T.Mb[:]), ("B4q", of("OA", 2), T.OA[:])])
-        acc("k3", T.k3[:, 0:256], [("If", of("t", 2), T.t[:]), ("B4a", of("OA", 2), T.OA[:])])
-        act(["k3"], ["tp"], T.tp[:], T.k3[:, 0:256], AF.Relu, bias=-512.0)
-
-    def write_rows():
-        act(["qn", "wU"], QQ, T.Q[:].indirect(T.wU[:]), T.qn[:], AF.Silu)
-
-    def write_banks():
-        acc("k3", T.k3[:, 256:512], [("Ib", ["x"], T.x[:]), ("Ib", ["tp"], T.tp[:])])
-        act(["k3"], ["vn"], T.vn[:], T.k3[:, 256:512], AF.Identity, bias=VO)
-        act(["vn", "wU"], VT, T.VT[:].indirect(T.wU[:]), T.vn[:], AF.Silu)
-
-    def convert(s, n):
-        if s == 0 and n == 0:
-            act(["Vm"], ["VTm"], T.VT[:, 0:B], T.V[:, 0:B], AF.Identity, bias=VO)
-        if s == 0 and n == 1:
-            fill("Qp", T.Q[:, B:VW], VW - B, float(NONE))
-            fill("VTp", T.VT[:, B:VW], VW - B, VO)
-        if s == STEPS - 1 and n == 0:
-            act(VT, ["Vr"], T.Vr[:], T.VT[:, 0:B], AF.Identity, bias=MAGIC)
-        if s == STEPS - 1 and n == 1:
-            act(["Vr"], ["Vm"], T.V[:, 0:B], T.Vr[:], AF.Identity, bias=-MAGIC - VO)
-
-    def line_list():
-        v("tt", ["SS0", "SS1", "pWc"], ["pa"], T.pa[:], T.SS[:, 15::16], T.pWc[:], OP.max)
-        yield
-        ts(["pa", "pco"], "pU", T.pU[:], T.pa[:], c("pco"), None, OP.subtract)
-
-    def write_lines(last):
-        if last:
-            v("tt", ["x", "tp", "wU"], VV, T.V[:].indirect(T.wU[:]), T.x[:], T.tp[:], OP.add)
-        else:
-            v("tc", ["An", "pU"], AA, T.A[:].indirect(T.pU[:]), T.An[:])
-
-    def stage(name, s):
-        last = s == STEPS - 1
-        kind, n = name[:2], int(name[2:3] or 0)
-        if last and (kind in ("br", "nr", "wr", "wb", "ll", "pw", "an") or name in HEAD.split()):
+    def writes(s, o):
+        draw = [("Ib", X("Ap", o)), ("NIb", X("An", o)), ("B4a", X("OA", o))]
+        if s == STEPS - 1:
+            acc(X("k0", o), draw)
+            act(X("tp", o), X("k0", o), AF.Relu)
+            tt(by(X("V"), X("wU", w(o))), X("x", o), X("tp", o), OP.add)
             return
-        if name[3:] > "a":
-            return next(begun[name[:3]], None)
-        begun[name[:3]] = {"bo": lambda: bank_offsets(s + 1), "qr": lambda: queue_rows(s + 1), "ld": last_constants, "pt": payee_table,
-         "qc": lambda: ts(["Qin"], "Qm", T.Q[:, 0:B], T.Qin[:, 0:B], float(LO), None, OP.add),
-         "pw": lambda: act(["pWf0", "pWf1", "pco"], ["pWc"], T.pWc[:], T.pWf[:], AF.Identity, bias=c("pco")), "op": lambda: old_positions(s + 1), "up": lambda: unpack(s + 1),
-         "wf": lambda: ts(["WL"], "Wf", T.Wf[:], T.WL[:], float(B), None, OP.add),
-         "am": lambda: amounts(n, s), "bt": lambda: bank_twins(n), "po": lambda: positions(s), "ca": lambda: compare(n, 0), "cb": lambda: compare(n, 1),
-         "sg": lambda: signs(n), "nf": lambda: row_numbers(s), "dz": covered,
-         "lo": losers, "bl": bank_list, "we": lambda: weigh(n), "pk": lambda: pick(n), "ln": lambda: lines(n),
-         "py": lambda: payees(n), "lt": lambda: line_twins(n), "lu": lambda: all_line_twins(n), "rk": lambda: ranks(n), "bk": lambda: payee_banks(n), "tm": lambda: draws(n),
-         "an": kept, "br": lambda: best_rows(n), "ct": lambda: counts(n), "sl": lambda: slots(n), "dr": lambda: drawn(last), "pl": lambda: place(s, n),
-         "nr": lambda: v("tt", ["k4", "nF"], ["qn"], T.qn[:], T.k4[:, 0:256], T.nF[:], OP.max),
-         "lc": later_constants, "wr": write_rows, "wb": write_banks, "cv": lambda: convert(s, n),
-         "ex": lambda: exchange(s), "ll": line_list, "wl": lambda: write_lines(last)}[kind]()
-        if name[3:]:
-            next(begun[name[:3]])
+        acc(X("k0", o), [("Ih", X("xo", o))] + draw)
+        tt(X("vn", o), X("k0", o), X("xo", o), OP.max)
+        act(by(X("VT"), X("wU", w(o))), X("vn", o), AF.Silu)
 
-    begun = {}
-    for name in FIRST.split():
-        stage(name, -1 if name in HEAD.split() else 0)
+    def used(o):
+        ts(X("pWc", w(o)), X("pL", w(o)), c("pco"), OP.add)
+        ts(X("pWc", w(o, 16)), X("Wf", w(o)), c("corr"), OP.add)
+        for plus in (16, 0):
+            tt(X("pa", w(o, plus)), ends("SS", o), X("pWc", w(o, plus)), OP.max)
+            if o != ALL:
+                ts(X("pU", w(o, plus)), X("pa", w(o, plus)), c("pco"), OP.subtract)
+        if o == ALL:
+            ts(X("pU"), X("pa"), c("pco"), OP.subtract)
+        act(by(X("Q"), X("pU", w(o, 16))), X("qn", o), AF.Silu)
+        tc(by(X("A"), X("pU", w(o))), X("An", o))
+
     for s in range(STEPS):
-        for name in step_order(s, ORDER.split()):
-            stage(name, s)
-    dma("y", VV, ["yv"], T.yv[:], T.V[:, 0:B])
-    L, Lk = T["L%d" % STEPS], ["L%d" % STEPS, "L%do" % STEPS]
-    ts(Lk, "k0", T.k0[:, 0:256], L[:], 512 * MAGIC, 512 * MAGIC, OP.add, OP.subtract)
-    v("tt", Lk + ["k0"], ["cb"], T.cb[:], T.k0[:, 0:256], L[:], OP.subtract)
-    dma("y", ["cb"], ["yc"], T.yc[:], T.cb[:])
-    act(["k0"], ["yw32"], T.yw32[:], T.k0[:, 0:256], AF.Copy, scale=-1 / 512)
-    dma("s", ["yw32"], ["yw"], T.yw[:], T.yw32[0:128:16, :])
+        early[0] = 0
+        for o in pieces:
+            head(s, o)
+        amounts(pieces[0])
+        amounts(pieces[1])
+        positions(s)
+        amounts(pieces[2])
+        amounts(pieces[3])
+        early[0] = EARLY[1]
+        banks()
+        early[0] = EARLY[0]
+        if s == 0:
+            ts(X("Q", slice(0, B)), X("Qin", slice(0, B)), float(LO), OP.add)
+            act(X("VT", slice(0, B)), X("V", slice(0, B)), AF.Identity, bias=VO)
+        if s == STEPS - 1:
+            act(X("Vr"), X("VT", slice(0, B)), AF.Identity, bias=MAGIC)
+            act(X("V", slice(0, B)), X("Vr"), AF.Identity, bias=-MAGIC - VO)
+        early[0] = 0
+        for o in parts:
+            lines(s, o)
+        for h in range(2):
+            draws(s, h)
+        exchange(s)
+        for o in HALF if WRITE2 else [ALL]:
+            if s < STEPS - 1:
+                used(o)
+        for o in HALF:
+            writes(s, o)
+    dma("y", T.yv[:], X("V", slice(0, B)), 1 << 18)
+    L = X("L%d" % STEPS)
+    ts(X("k0", ALL), L, 512 * MAGIC, OP.add, 512 * MAGIC, OP.subtract)
+    tt(X("cb"), X("k0", ALL), L, OP.subtract)
+    dma("y", T.yc[:], X("cb"), 1 << 16)
+    act(X("yw32"), X("k0", ALL), AF.Identity, scale=-1 / 512, bias=-float(B))
+    dma("s", T.yw[:], X("yw32", rows=slice(0, 128, 16)), 8192)
+
+    semof = {"v": "sv", "s": "ss", "t": "st", "g": "sg"}
+    count = {e: 0 for e in semof}
+    know, seen, user, total, program = {e: {} for e in queue}, {}, {}, {}, []
+
+    def wait(e, sem, val):
+        if know[e].get(sem, 0) < val:
+            program.append((e, None, sem, val))
+            for s2, v2 in list(seen.get((sem, val), {}).items()) + [(sem, val)]:
+                know[e][s2] = max(know[e].get(s2, 0), v2)
+
+    for i in issue_order(calls):
+        call = calls[i]
+        e, need = call["queue"], {}
+        marks = [calls[j]["sem"][0:2] if wrote else calls[j]["sem"][2:4] for j, wrote in call["needs"].items() if waits(calls[j], call, wrote)]
+        for sem, val in marks + [m for bank in call["banks"] for u, m in user.get(bank, {}).items() if u != e]:
+            need[sem] = max(need.get(sem, 0), val)
+        for sem in sorted(need):
+            wait(e, sem, need[sem])
+        if call["sem"] is None:
+            count[e] += 1
+            call["sem"] = (semof[e], count[e]) * 2
+            program.append((e, call["issue"], semof[e], count[e]))
+        else:
+            program.append((e, call["issue"], None, 0))
+        for sem, val in (call["sem"][0:2], call["sem"][2:4]):
+            seen[(sem, val)] = {} if sem[0] == "r" else dict(know[e])
+            total[sem] = val
+        for bank in call["banks"]:
+            user.setdefault(bank, {})[e] = call["sem"][0:2]
     for sem in sorted(total):
-        need_wait("g", sem, total[sem])
-    waited = {(sem, val) for e, call, sem, val in calls if call is None}
-    raised = {sem: 0 for sem in cnt}
-    for e, call, sem, val in calls:
-        if call is None:
+        wait("g", sem, total[sem])
+    waited = {(sem, val) for e, issue, sem, val in program if issue is None}
+    raised = {sem: 0 for sem in semof.values()}
+    for e, issue, sem, val in program:
+        if issue is None:
             queue[e].wait_ge(T.sem[sem], val)
         elif (sem, val) in waited:
-            call().then_inc(T.sem[sem], val - raised[sem])
+            issue().then_inc(T.sem[sem], val - raised[sem])
             raised[sem] = val
         else:
-            call()
+            issue()

@@ -14,11 +14,14 @@ MAGIC = 1.5 * 2.0 ** 23
 GS, GB, FS, FB = 0.004397, 11.6005, 0.004395, 10.533
 BATCH = 2
 FILL = (2048, 4096)
-CYC, PCYC, GATHER, SCATTER, HOP, DMA, RATE, REMOTE, FIRST = 0.83, 0.42, 1.6, 4.0, 250, 900, 400, 900, 1700
+CYC, PCYC, GATHER, SCATTER, HOP, DMA, RATE, REMOTE, FIRST = 0.83, 0.42, 1.35, 3.8, 260, 900, 400, 800, 1700
+SFIX = 75
 TURNS = 2
-EARLY = (0, 0, 0, 0)
-THREE, WRITE2 = True, False
-TRIES, SEED, SHIFTS = 1200, 1, (-2500, -1200, -600, -300, -100, 100, 300, 600, 1200, 2500)
+THREE, WRITE2, CUT, SPLIT, ONV = True, "AQ", False, False, ("D1", "D2", "VT")
+PAIR, JOIN, FOUR, BFIRST, HELP, MERGE = 1, True, False, 1, True, 128
+GFILL, SLOW = 2048, 1.5
+ONS, WHS = ("If", "BLKf", "N512", "NIb"), 12
+TRIES, SEED, SHIFTS, SLACK = 2100, 1, (1, 1, 100, 300, 600, 1200), (0, 10, 20)
 HOOK = []
 SCRATCH = {}
 
@@ -47,10 +50,11 @@ _buf("float16", 128, "sel8", 8)
 _buf("float32", 128, "imp qg BLKf If")
 _buf("float32", 144, "ebi")
 _buf("float16", 144, "EB")
-_buf("float32", 256, "SC SD SP SS nF np qn vn Vg yw32 FALL Xb u")
+_buf("float32", 256, "SC SD SP SS qn vn Vg yw32 FALL Xb u")
+_buf("float32", 512, "nF np")
 _buf("int32", 8, "pc pj pg")
 _buf("float32", 64, "cf")
-_buf("float32", 16, "l16 LC Wf wa E16")
+_buf("float32", 16, "l16 LC Wf wa E16 EQ LT")
 _buf("float32", 32, "pWc pa")
 _buf("uint16", 16, "WL wU pL sL")
 _buf("uint16", 32, "pU")
@@ -59,6 +63,7 @@ _buf("bfloat16", 128, "u1 Ib NIb N32 BLKb B256 B4a B4n I4k WBm WT W4 TRI MONE")
 _buf("bfloat16", 2048, "WH")
 _buf("bfloat16", 256, "tt GM STEP ZERO thr x D1 D2 e PG Ap An tp OA cb")
 _buf("float16", 256, "Z Cn bR y xc xo F")
+_buf("float16", 512, "F2")
 _buf("uint16", 256, "nU pR")
 _buf("bfloat16", 4096, "eq")
 _buf("float16", 4096, "G cmp")
@@ -66,7 +71,7 @@ for _s in range(STEPS + 1):
     _buf("float32", 256, "L%d" % _s)
 for _s in range(8):
     SCRATCH["k%d" % _s] = ("psum", [128, 512], "float32")
-SEMAPHORES = ["sv", "ss", "st", "sg", "lx"] + ["rx%d" % s for s in range(STEPS)] + ["d%d" % k for k in range(16)]
+SEMAPHORES = ["sv", "ss", "st", "sg", "lx"] + ["rx%d" % s for s in range(STEPS)] + ["d%d" % k for k in range(24)]
 
 
 def split_engines(topo, cores, src):
@@ -87,34 +92,46 @@ def split_engines(topo, cores, src):
     return out
 
 
-def issue_order(calls):
+def issue_order(calls, tries):
     n = len(calls)
+    facts = [(c["queue"], int(c["time"]), c["banks"]) for c in calls]
+    places = {c["queue"] for c in calls} | {bank for c in calls for bank in c["banks"]}
     before, behind = [[] for c in calls], [[] for c in calls]
     for i, c in enumerate(calls):
         for j, wrote in c["needs"].items():
             gap = calls[j]["late"] + HOP if waits(calls[j], c, wrote) else 0
             before[i].append((j, gap))
+    gaps = [dict(b) for b in before]
+    for i in range(n):
+        before[i] = [(j, gap) for j, gap in before[i] if not any(j in gaps[k] and gaps[k][j] + facts[k][1] + via >= gap for k, via in gaps[i].items())]
+        for j, gap in before[i]:
             behind[j].append((i, gap))
 
     def place(order, needs):
-        taken, start, end = {}, [0.0] * n, [0.0] * n
+        taken = {r: [[] for u in range(400)] for r in places}
+        start, end = [0] * n, [0] * n
         for i in order:
-            e, time, banks = calls[i]["queue"], calls[i]["time"], calls[i]["banks"]
-            t, was = max([0.0] + [end[j] + gap for j, gap in needs[i]]), -1.0
+            e, time, banks = facts[i]
+            t, was = HOP, -1
+            for j, gap in needs[i]:
+                if end[j] + gap > t:
+                    t = end[j] + gap
             while t > was:
                 was = t
-                for u in range(int(t) >> 10, (int(t + time) >> 10) + 1):
-                    for a, b, who in taken.get((e, u), ()):
-                        if a < t + time and b > t:
+                for u in range(t >> 9, (t + time >> 9) + 1):
+                    for a, b in taken[e][u]:
+                        if b > t and a < t + time:
                             t = b
                     for bank in banks:
-                        for a, b, who in taken.get((bank, u), ()):
-                            if who != e and a < t + time and b > t:
+                        for a, b, who in taken[bank][u]:
+                            if b > t and a < t + time and who != e:
                                 t = b
             start[i], end[i] = t, t + time
-            for r, pad in [(e, 0)] + [(bank, HOP) for bank in banks]:
-                for u in range(int(t - pad) >> 10, (int(t + time + pad) >> 10) + 1):
-                    taken.setdefault((r, u), []).append((t - pad, t + time + pad, e))
+            for u in range(t >> 9, (t + time >> 9) + 1):
+                taken[e][u].append((t, t + time))
+            for bank in banks:
+                for u in range(t - HOP >> 9, (t + time + HOP >> 9) + 1):
+                    taken[bank][u].append((t - HOP, t + time + HOP, e))
         return start, end
 
     done, way = [False] * n, [0.0] * n
@@ -138,18 +155,37 @@ def issue_order(calls):
     def pick(among):
         draw[0] = (draw[0] * 1103515245 + 12345) % 2 ** 31
         return among[(draw[0] >> 8) % len(among)]
-    for turn in range(TRIES):
-        moved = {pick(calls)["kind"]: pick(SHIFTS) for k in range(pick((1, 1, 2, 4)))}
-        key = [best[1][i] + moved.get(c["kind"], 0) for i, c in enumerate(calls)]
-        if turn % 2:
-            for i in range(n):
-                key[i] = max([key[i]] + [key[j] + 0.001 for j, gap in before[i]])
-        else:
-            for i in range(n - 1, -1, -1):
-                key[i] = min([key[i]] + [key[j] - 0.001 for j, gap in behind[i]])
+
+
+    def held(start):
+        end = [start[i] + facts[i][1] for i in range(n)]
+        left = {(facts[i][0], end[i]): i for i in range(n)}
+        left.update({(bank, end[i] + HOP): i for i in range(n) for bank in facts[i][2]})
+        i, pairs = end.index(max(end)), []
+        while True:
+            needed = [j for j, gap in before[i] if end[j] + gap == start[i]]
+            holders = [left[r, start[i]] for r in [facts[i][0]] + facts[i][2] if (r, start[i]) in left]
+            if not needed and not holders:
+                return pairs
+            if not needed:
+                pairs.append((i, holders[0]))
+            i = pick(needed) if needed else holders[0]
+    kinds = [[c[name] for c in calls] for name in ("kind", "sort")]
+    now, pairs = best, held(best[1])
+    for turn in range(tries):
+        i, j = pick(pairs) if pairs and turn % 5 else (pick(range(n)), pick(range(n)))
+        past = abs(now[1][i] - now[1][j]) if turn % 5 else 0
+        moved, shift = pick([(i, -past - pick(SHIFTS)), (j, past + pick(SHIFTS)), (j, -3 * pick(SHIFTS))])
+        kind = pick(kinds)
+        key = [t + shift if u == kind[moved] else t for t, u in zip(now[1], kind)]
+        for i in range(n) if shift > 0 else range(n - 1, -1, -1):
+            for j, gap in before[i] if shift > 0 else behind[i]:
+                if (key[j] >= key[i]) == (shift > 0) or key[j] == key[i]:
+                    key[i] = key[j] + (0.001 if shift > 0 else -0.001)
         start, end = place(sorted(range(n), key=lambda i: (key[i], i)), before)
-        if max(end) <= best[0]:
-            best = (max(end), start)
+        if max(end) <= now[0] + pick(SLACK):
+            now, pairs = (max(end), start), held(start)
+            best = min(best, now)
     return sorted(range(n), key=lambda i: (best[1][i], i))
 
 
@@ -163,7 +199,7 @@ def rank_program(g, core, T, topo):
         return
     cores = list(T.cores)
     queue = {"v": g.vector, "s": g.scalar, "t": g.tensor, "g": g, "y": g.sync}
-    calls, uses, group, early = [], {}, {}, [EARLY[0]]
+    calls, uses, group, stage = [], {}, {}, [None]
 
     def X(name, cols=None, rows=None):
         where, shape, dtype = SCRATCH[name]
@@ -185,7 +221,8 @@ def rank_program(g, core, T, topo):
         for x, writes in [(x, False) for x in R] + [(x, True) for x in W]:
             keep = [u for u in uses.get(x["name"], []) if not (writes and not x["rows"] and x["lo"] <= u[0]["lo"] and u[0]["hi"] <= x["hi"])]
             uses[x["name"]] = keep + [(x, writes, len(calls))]
-        calls.append({"queue": e, "issue": issue, "time": time, "late": late, "needs": needs, "sem": sem, "early": early[0], "kind": (e, W[0]["name"], W[0]["lo"], R[0]["name"] if R else "") if W else e,
+        calls.append({"queue": e, "issue": issue, "time": time, "late": late, "needs": needs, "sem": sem, "kind": (e, W[0]["name"], W[0]["lo"], R[0]["name"] if R else "") if W else e,
+                      "sort": (e, W[0]["name"], stage[0] or W[0]["lo"], R[0]["name"] if R else "") if W else e,
                       "banks": sorted({x["name"] for x in R + W if x["psum"]})})
 
     def op(e, name, out, *a, after=(), **k):
@@ -198,9 +235,9 @@ def rank_program(g, core, T, topo):
         elif e == "g":
             time = 150 + 2 * CYC * n
         elif any(x["by"] for x in sides):
-            time = 60 + CYC * n * (SCATTER if out["by"] else GATHER)
+            time = (SFIX if e == "s" else 30) + CYC * n * (SCATTER if out["by"] else GATHER)
         elif e == "s":
-            time = 80 + CYC * n
+            time = SFIX + CYC * n
         else:
             per = (1 if a[0]["psum"] or a[1]["psum"] else 2) if name == "tensor_tensor" else 1 if any(x["wide"] for x in sides) else 0.5
             time = 10 + CYC * max(64, n * per)
@@ -208,12 +245,12 @@ def rank_program(g, core, T, topo):
         keys = {u: x["ap"] if isinstance(x, dict) else x for u, x in k.items()}
         eng = queue[e]
         issue = {"tensor_copy": lambda: eng.tensor_copy(*args), "tensor_tensor": lambda: eng.tensor_tensor(*args), "tensor_scalar": lambda: eng.tensor_scalar(*args),
-                 "scan": lambda: eng.tensor_tensor_scan(*args), "memset": lambda: eng.memset(*args), "reduce": lambda: eng.tensor_reduce(*args),
+                 "scan": lambda: eng.tensor_tensor_scan(*args), "memset": lambda: eng.memset(*args), "reciprocal": lambda: eng.reciprocal(*args), "reduce": lambda: eng.tensor_reduce(*args),
                  "activation": lambda: eng.activation(*args, **keys), "matmul": lambda: eng.matmul(*args),
                  "iota": lambda: eng.iota(*args, **keys), "select": lambda: eng.affine_select(*args)}[name]
         record(e, issue, time, R, [out])
         if name == "matmul":
-            if a[2] and out["name"] in group:
+            if out["name"] in group:
                 calls[-1]["needs"].setdefault(group[out["name"]], False)
             group[out["name"]] = len(calls) - 1
 
@@ -293,63 +330,65 @@ def rank_program(g, core, T, topo):
 
     def byrow(name, start, terms):
         for n, (is_, k, value) in enumerate(terms):
-            if (is_, k) not in col:
-                column((is_, k), c("jf"), float(k), {"lt": OP.is_lt, "eq": OP.is_equal, "ge": OP.is_ge}[is_])
-            column(name if n == len(terms) - 1 else (name, n), c((is_, k)), float(value), OP.mult, c((name, n - 1)) if n else start, OP.add)
+            column(name if n == len(terms) - 1 else (name, n), X(is_, k), float(value), OP.mult, c((name, n - 1)) if n else start, OP.add)
 
-    memset(X("ONE"), 1.0)
-    memset(X("MONE"), -1.0)
-    memset(X("ZERO"), 0.0)
-    memset(X("FALL"), 1 / RHO)
-    memset(X("A", slice(0, LO)), 0.0)
-    memset(X("Qin", slice(B, B + 16)), 8191)
-    memset(X("Q", slice(B, QW)), float(NONE))
-    memset(X("VT", slice(B, B + 16)), VO)
-    memset(X("TRI"), 1 / 32)
-    select("TRI", [[1, 128]], OP.is_ge, 2.0, 0, -1)
-    select("TRI", [[1, 128]], OP.not_equal, -1.0, 0, -1)
-    select("TRI", [[-16, 8], [0, 16]], OP.is_ge, 0.0, 0, 1)
-    select("TRI", [[16, 8], [0, 16]], OP.is_ge, 0.0, 15, -1)
+    for name, a, b, value in (("A", 0, LO, 0), ("Qin", B, QW, 8191), ("Q", B, QW, NONE), ("VT", B, QW, int(VO))):
+        iota(X(name, slice(a, b)), [[0, b - a]], value)
+    for name, n, value in (("FALL", 256, 1 / RHO), ("ZERO", 256, 0.0), ("MONE", 128, -1.0), ("ONE", (8192 - GFILL) // 8, 1.0)):
+        memset(X(name, slice(0, n)), value)
+    memset(X("u1"), 1 / 32)
+    select("u1", [[1, 128]], OP.is_ge, 1.1, 0, -1)
+    select("u1", [[1, 128]], OP.not_equal, -1.0, 0, -1)
+    select("u1", [[-16, 8], [0, 16]], OP.is_ge, 0.0, 0, 1)
+    select("u1", [[16, 8], [0, 16]], OP.is_ge, 0.0, 15, -1)
+    ts(X("TRI"), X("u1"), 2.0 ** 58, OP.mult, 2.0 ** 58, OP.mult)
+    iota(X("nF"), [[0, 512]], 0)
+    for bank in ("k3", "k4"):
+        memset(X(bank, slice(128, 384)), 0.0)
     scan(X("thr"), X("FALL"), X("ZERO"), 2.54 * RHO * TOP, OP.mult, OP.add)
     ts(X("pj", 0), X("pc", 0), 15, OP.bitwise_and)
     ts(X("pg", 0), X("pc", 0), 4, OP.arith_shift_right)
     for name, src in (("jf", "pj"), ("gf", "pg"), ("pf", "pc")):
         column(name, X(src, 0), 0.0, OP.add)
     column("jh", c("jf"), 0.5, OP.add)
-    for name, plus in (("corr", 0.0), ("cor2", -512.0 * B), ("pco", 1024.0), ("cor3", -3072.0), ("cor4", -4096.0)):
+    for name, plus in (("corr", 0.0), ("cor2", -512.0 * B), ("pco", 1024.0), ("cor3", 1024.0 if "D1" in ONV else -3072.0), ("cor4", 0.0 if "D2" in ONV else -4096.0)):
         column(name, c("jf"), -LIFT, OP.mult, 15 * LIFT + plus, OP.add)
-    column("ncor", c("jf"), LIFT, OP.mult, 4096 - 15 * LIFT, OP.add)
+    column("ncor", c("jf"), LIFT, OP.mult, (0.0 if "D2" in ONV else 4096.0) - 15 * LIFT, OP.add)
+    column("ncor0", c("jf"), LIFT, OP.mult, -15 * LIFT, OP.add)
     column("g16", c("gf"), 16.0, OP.mult)
-    column("j256", c("jf"), 256.0, OP.mult, -1040.0 - LO, OP.add)
-    column("jr", c("jf"), -2.0 ** 19 / KILL, OP.mult)
-    byrow("jw", 0.0, [("eq", 4, -5 * 2 ** 19), ("eq", 6, 512 * 32), ("eq", 7, 512)])
-    byrow("icol", c("j256"), [("eq", 4, -1023), ("eq", 5, 1040 + LO - 1280 - 8192), ("ge", 6, -4096)])
-    byrow("ja", 0.0, [("lt", 4, 512), ("eq", 5, -512)])
-    byrow("jz", -1.0, [("lt", 4, 2), ("ge", 6, 1)])
-    byrow("n4", 1.0, [("eq", 4, 1)])
-    byrow("n15", 0.0, [("lt", 15, 1)])
-    column("jv", c("jr"), c(("lt", 4)), OP.mult, c("jw"), OP.add)
+    ts(X("EQ"), X("tt", slice(0, 16)), c("jf"), OP.is_equal)
+    ts(X("LT"), X("tt", slice(0, 16)), c("jf"), OP.is_gt)
+    column("j256", c("jf"), 256.0, OP.mult, -1040.0 - LO - 4096, OP.add)
+    column("jr", c("jf"), -2.0 ** 19 / KILL, OP.mult, X("LT", 4), OP.mult)
+    byrow("jw", c("jr"), [("EQ", 8, 512 * 32), ("EQ", 9, 512)])
+    byrow("icol", c("j256"), [("EQ", 4, -1023), ("EQ", 5, 1040 + LO - 1280 - 8192), ("LT", 6, 4096)])
+    byrow("ja", 0.0, [("LT", 4, 512), ("EQ", 5, -512)])
+    byrow("jz", 0.0, [("LT", 4, 2), ("LT", 6, -1)])
     ts(X("GM"), X("tt"), c("jh"), OP.subtract, 64 * LIFT, OP.mult)
     ts(X("GM"), X("GM"), LIFT, OP.min)
     ts(X("BLKb"), X("qg"), c("gf"), OP.is_equal)
     ts(X("Ib"), X("imp"), 0.0, OP.is_equal)
     ts(X("EB"), X("ebi"), c("g16"), OP.is_equal, 2.0 ** 15, OP.mult)
-    ts(X("STEP"), X("ONE", slice(0, 256)), c("n4"), OP.mult)
+    ts(X("STEP"), X("ZERO"), X("EQ", 4), OP.add, 1.0, OP.add)
     ts(X("LC"), X("l16"), c("jf"), OP.add, c("cor3"), OP.add)
-    ts(X("E16"), X("tt", slice(0, 16)), c("jf"), OP.is_equal)
-    tt(X("E16"), X("E16"), X("thr", slice(0, 16)), OP.mult)
+    tt(X("E16"), X("EQ"), X("thr", slice(0, 16)), OP.mult)
     col["wj"] = len(col)
     op("v", "reduce", c("wj"), X("E16"), AX.X, OP.max)
     ts(X("WT"), X("BLKb"), c("wj"), OP.mult, 1 / (2.54 * TOP), OP.mult)
     for name, src, times in (("N512", "Ib", -512.0), ("If", "Ib", 1.0), ("NIb", "Ib", -1.0), ("N32", "Ib", -32.0), ("Ih", "Ib", 1.0), ("NIh", "Ib", -1.0),
-                             ("I4k", "Ib", 4096.0), ("B256", "BLKb", 256.0), ("BLKf", "BLKb", 1.0), ("BLK1", "BLKb", 1.0), ("WBm", "BLKb", c("jv")),
+                             ("I4k", "Ib", 4096.0), ("B256", "BLKb", 256.0), ("BLKf", "BLKb", 1.0), ("BLK1", "BLKb", 1.0), ("WBm", "BLKb", c("jw")),
                              ("B4a", "BLKb", c("ja")), ("BLKh", "BLKb", c("jz"))):
-        ts(X(name), X(src), times, OP.mult)
-    ts(X("B4n"), X("BLKb"), c(("lt", 4)), OP.mult, -8192.0, OP.mult)
-    ts(X("u1"), X("tt", slice(0, 128)), 4.0, OP.is_lt)
-    tt(X("W4"), X("WT"), X("u1"), OP.mult)
+        if name in ONS:
+            act(X(name), X(src), AF.Identity, scale=times)
+        else:
+            ts(X(name), X(src), times, OP.mult)
+    ts(X("B4n"), X("BLKb"), X("LT", 4), OP.mult, -8192.0, OP.mult)
+    op("g", "select", X("W4"), X("WT"), [[0, 8], [-1, 16]], OP.is_ge, 0.0, 3, 0)
     for h in range(16):
-        ts(X("WH", slice(128 * h, 128 * h + 128)), X("W4"), TOP * RHO ** (-16 * h), OP.mult)
+        if h < WHS:
+            act(X("WH", slice(128 * h, 128 * h + 128)), X("W4"), scale=TOP * RHO ** (-16 * h))
+        else:
+            ts(X("WH", slice(128 * h, 128 * h + 128)), X("W4"), TOP * RHO ** (-16 * h), OP.mult)
 
     rows8 = slice(0, 8)
     ts(X("sel8"), X("qg", rows=rows8), X("cf", col["pf"], rows8), OP.is_equal, -512.0, OP.mult)
@@ -357,26 +396,27 @@ def rank_program(g, core, T, topo):
     mm(X("k0", slice(0, 256)), X("sel8"), X("wkH"))
     tc(X("L0"), X("k0", slice(0, 256)))
 
-    a, b = FILL[0], FILL[0] + FILL[1]
-    iota(X("PT", slice(0, a)), [[0, a]], 1)
-    for at in range(a, b, 1024):
-        act(X("PT", slice(at, at + 1024)), X("ONE"), AF.Silu, scale=1.27846)
-        calls[-1]["time"] += 1300 * (at == a)
-        in_line("fill")
-    for at in range(b, LO + 8192, 1024):
-        memset(X("PT", slice(at, min(at + 1024, LO + 8192))), 1.0)
+    act(X("PT", slice(0, LO)), X("FALL", slice(0, LO)), AF.Silu)
+    calls[-1]["time"] += 1300
+    in_line("amounts")
     tc(X("payF"), X("payS"))
     act(X("payR"), X("payF"), AF.Identity, scale=1 / 1024, bias=1025 - 0.4995)
     act(X("payH"), X("payF"), AF.Identity, scale=1 / 32, bias=1025 - 15.5 / 32)
-    ts(X("payR", 511), X("payR", 511), c("n15"), OP.mult)
+    ts(X("payR", 511), X("payR", 511), X("LT", 15), OP.mult)
     part = [X("payB", slice(512 * k, 512 * k + 512)) for k in range(6)]
     for r in range(4):
         ts(part[r], X("payR"), 1025.0 + r, OP.not_equal, -KILL, OP.mult)
     ts(part[4], X("payH"), 1025.0, OP.subtract)
     acc(X("k7"), [("If", X("payF")), ("N32", part[4])])
     act(part[5], X("k7"))
-    for k, j in enumerate((0, 1, 2, 3, 6, 7)):
-        dma("y", X("PT", slice(LO, LO + 8192), slice(j, 128, 16)), part[k], 1 << 17, after=[X("V", slice(0, B))])
+    in_line("amounts")
+    if GFILL:
+        iota(X("PT", slice(LO, LO + GFILL)), [[0, GFILL]], 1)
+    for j, step in ((4, 8), (5, 8), (6, 8), (7, 8), (10, 16), (11, 16)):
+        dma("y", X("PT", slice(LO + GFILL, LO + 8192), slice(j, 128, step)), X("ONE", slice(0, (8192 - GFILL) // 8), slice(0, 1024 // step)),
+            (8192 - GFILL) * 256 // step * SLOW, after=[X("V", slice(0, B))])
+    for k, j in enumerate((0, 1, 2, 3, 8, 9)):
+        dma("y", X("PT", slice(LO, LO + 8192), slice(j, 128, 16)), part[k], (1 << 17) * SLOW, after=[X("V", slice(0, B))])
 
     route = split_engines(topo, cores, core)
     arrive = sum(len(split_engines(topo, cores, s)[core]) for s in cores if s != core)
@@ -401,20 +441,25 @@ def rank_program(g, core, T, topo):
 
     def ps(name, o):
         if name in ("twin", "slot"):
-            bank, at = 5 + o.start // 128, {"twin": 128, "slot": 256}[name]
+            bank, at = 5 + o.start // 128, {"twin": 0, "slot": 256}[name]
+        elif FOUR:
+            bank, at = (7, 3, 4, 7)[parts.index(o)], {"score": 0, "won": 64, "best": 128, "line": 192}[name] + 256 * (o == parts[3])
         else:
-            bank, at = {0: 3, 128: 4, 192: 7}[o.start], {"score": 0, "won": 128, "best": 256, "line": 384}[name]
+            bank, at = {0: 3, 128: 4, 192: 7}[o.start], {"score": 0, "won": 128, "best": 0, "line": 384}[name]
         return X("k%d" % bank, slice(at, at + o.stop - o.start))
 
     ALL, HALF = slice(0, 256), [slice(0, 128), slice(128, 256)]
     own = slice(64 * q, 64 * q + 64)
     pieces = [own] + [slice(64 * r, 64 * r + 64) for r in range(4) if r != q]
     parts = [HALF[0], slice(128, 192), slice(192, 256)] if THREE else HALF
-    parts = sorted(parts, key=lambda o: o != own)
+    parts = pieces if FOUR else sorted(parts, key=lambda o: o != own)
+    helped = slice(128, 192)
+    cut = parts[-1].start if CUT else 128
+    shares = [slice(0, cut), slice(cut, 256)]
 
     def twins(out, h, o, row, s1, op0, s2, op1, matrix, start, stop):
         eq = X("eq", slice(256 * h + o.start, 256 * h + o.stop))
-        ts(eq, X(row, o), s1, op0, s2, op1)
+        ts(eq, row, s1, op0, s2, op1)
         in_line("twins")
         return lambda after: mm(out, matrix, eq, start, stop, after), eq
 
@@ -435,7 +480,11 @@ def rank_program(g, core, T, topo):
             ts(X("nU", o), by(X("Qin"), X("WL", w(o))), float(LO), OP.add)
         in_line("rows")
 
-    def amounts(o):
+    def amounts(s, o):
+        if s == 0 and o == helped and HELP:
+            ts(X("G", slice(16 * o.start, 16 * o.stop)), by(X("A"), X("nU", o)), 130.0, OP.add, -2.0 ** -21, OP.mult)
+            in_line("help")
+            return
         act(X("G", slice(16 * o.start, 16 * o.stop)), by(X("A"), X("nU", o)), AF.Silu, scale=GS, bias=-GB)
         in_line("amounts")
 
@@ -448,9 +497,17 @@ def rank_program(g, core, T, topo):
             tt(X("y"), X("Vg"), X("k0", ALL), OP.subtract)
         else:
             ts(X("y"), by(X("V", slice(0, QW)), X("WL")), VO, OP.add)
+            in_line("help")
         ts(X("xc"), X("y"), VO - 255, OP.max, VO, OP.min)
         act(X("F"), X("xc"), AF.Silu, scale=FS, bias=-FB - FS * VO)
         in_line("amounts")
+        if s == 0 and HELP:
+            ts(X("Vg", helped), X("xc", helped), VO + 129.5, OP.subtract, 16.0, OP.mult)
+            op("v", "reciprocal", X("vn", helped), X("Vg", helped))
+            calls[-1]["time"] = 190 + 6 * 64 * CYC
+        for o, src in [(helped, "vn"), (slice(192, 256), "F")] if s == 0 and HELP else [(HALF[1], "F")]:
+            for u in range(2):
+                tc(X("F2", slice(2 * o.start + u, 2 * o.stop, 2)), X(src, o))
         if s == STEPS - 1:
             ts(X("x"), X("y"), VO, OP.subtract, -255.0, OP.max)
         else:
@@ -459,47 +516,83 @@ def rank_program(g, core, T, topo):
     def banks():
         ts(X("Wf"), X("WL"), float(B), OP.add)
         mm(X("k2", ALL), X("MONE", rows=slice(0, 1)), X("thr", rows=slice(0, 1)), True, False)
-        batches(twins(X("k2", slice(16 * h, 256)), h, slice(16 * h, 256), "bR", X("Wf", h), OP.is_equal, TOP * RHO ** (-16 * h), OP.mult,
+        batches(twins(X("k2", slice(16 * h, 256)), h, slice(16 * h, 256), X("bR", slice(16 * h, 256)), X("Wf", h), OP.is_equal, TOP * RHO ** (-16 * h), OP.mult,
                       X("WT"), False, h == 15) for h in range(16))
-        act(X("D1"), X("k2", ALL), AF.Sign)
+        if BFIRST:
+            line["rows"] = line["twins"]
+        if "D1" in ONV:
+            ts(X("D1"), X("k2", ALL), 0.0, OP.is_gt, 2.0, OP.mult)
+        else:
+            act(X("D1"), X("k2", ALL), AF.Sign)
+        one = 0.0 if "D1" in ONV else 4096.0
         acc(X("k0", slice(256, 512)), [("BLK1", X("xc")), ("B256", X("D1"))])
-        act(X("D2"), X("k0", slice(256, 512)), AF.Sign, bias=4096.5 - 16 * VO)
+        if "D2" in ONV:
+            ts(X("D2"), X("k0", slice(256, 512)), 16 * VO - one - 0.5, OP.is_gt, 2.0, OP.mult)
+        else:
+            act(X("D2"), X("k0", slice(256, 512)), AF.Sign, bias=one + 0.5 - 16 * VO)
         acc(X("k2", slice(256, 512)), [("Ih", X("bR")), ("I4k", X("D1"))])
         scan(X("SD"), X("GM"), X("k2", slice(256, 512)), 0.0, OP.add, OP.max)
         tt(X("wa"), ends("SD", ALL), X("LC"), OP.min)
         ts(X("wU"), X("wa"), c("cor3"), OP.subtract)
 
     def compare(o, i):
-        made = X("cmp", slice(256 * i + o.start, 256 * i + o.stop))
-        scan(made, X("G", slice(16 * o.start + i, 16 * o.stop, 16)), X("F", o), 0.0, OP.min, OP.mult)
-        in_line("rows")
-        return lambda after: mm(ps("score", o), X("EB", slice(15 - i, 143 - i)), made, i == 0, i == 15, after), made
+        if PAIR and o.stop - o.start == 64:
+            i = i // 2 + 8 * (i % 2)
+            at = 512 * (i % 8) + 2 * o.start
+            made, both = X("cmp", slice(at + i // 8, at + 128, 2)), X("cmp", slice(at, at + 128))
+            if i < 8:
+                scan(both, X("G", slice(16 * o.start + i, 16 * o.stop, 8)), X("F2", slice(2 * o.start, 2 * o.stop)), 0.0, OP.min, OP.mult)
+                in_line("rows")
+        else:
+            made = both = X("cmp", slice(256 * i + o.start - 128 * PAIR * (i % 2), 256 * i + o.stop - 128 * PAIR * (i % 2)))
+            scan(made, X("G", slice(16 * o.start + i, 16 * o.stop, 16)), X("F", o), 0.0, OP.min, OP.mult)
+            in_line("rows")
+        return lambda after: mm(ps("score", o), X("EB", slice(15 - i, 143 - i)), made, i == 0, i == 15, after), both
 
     def lines(s, o):
-        tc(X("nF", o), X("nU", o))
+        both, even = slice(2 * o.start, 2 * o.stop), slice(2 * o.start, 2 * o.stop, 2)
+        won = ps("won", o)
+        won, won2 = X(won["name"], slice(128, 128 + both.stop - both.start, 2)), X(won["name"], slice(128, 128 + both.stop - both.start))
+        tc(X("nF", even), X("nU", o))
         batches(compare(o, i) for i in range(16))
-        act(X("e", o), ps("score", o), AF.Silu, bias=-85.6, scale=4.6 * 512)
-        acc(ps("won", o), [("TRI", X("e", o))])
+        act(X("e", o), ps("score", o), AF.Silu, bias=-74.4, scale=3.9 * 512)
+        acc(won, [("TRI", X("e", o))])
         mm(ps("line", o), X("B256"), X("D2", o), True, False)
-        ts(ps("best", o), ps("won", o), 0.0, OP.is_gt, float(NONE), OP.mult)
-        tt(X("np", o), ps("best", o), X("nF", o), OP.min)
-        mm(ps("line", o), X("BLKf"), X("np", o), False, True)
-        ts(X("pR", o), ps("line", o), 4096.0, OP.add)
+        merge = o.stop - o.start <= MERGE
+        if merge:
+            scan(X("np", both), won2, X("nF", both), 0.0, OP.max, OP.min)
+        else:
+            ts(ps("best", o), won, 0.0, OP.is_gt, float(NONE), OP.mult)
+            tt(X("np", even), ps("best", o), X("nF", even), OP.min)
+        mm(ps("line", o), X("BLKf"), X("np", even), False, True)
+        if o != parts[-1] or o != shares[-1]:
+            ts(X("pR", o), ps("line", o), 0.0 if "D2" in ONV else 4096.0, OP.add)
         scan(X("SP", o), X("GM", o), ps("line", o), 0.0, OP.add, OP.max)
         ts(X("pL", w(o)), ends("SP", o), c("cor4"), OP.subtract, float(NONE), OP.min)
         act(X("PG", o), by(X("PT"), X("pL", w(o))))
         act(X("Ap", o), by(X("A"), X("pL", w(o))))
         if s < STEPS - 1:
-            tt(X("qn", o), ps("best", o), X("nF", o), OP.max)
+            if merge:
+                ts(ps("best", o), won, 0.0, OP.is_gt, float(NONE), OP.mult)
+            tt(X("qn", o), ps("best", o), X("nF", even), OP.max)
 
-    def draws(s, h):
-        o = HALF[h]
+    def draws(s, o):
         twin = ps("twin", o)
         mm(twin, X("MONE", rows=slice(0, 1)), X("thr", o, slice(0, 1)), True, False)
-        batches(twins(X(twin["name"], slice(128 + max(16 * k - o.start, 0), 256)), k, slice(max(16 * k, o.start), o.stop), "pR", X("SP", 16 * k + 15), OP.subtract,
-                      c("ncor"), OP.is_equal, X("WH", slice(128 * k, 128 * k + 128)), False, k == o.stop // 16 - 1) for k in range(o.stop // 16))
+        todo = [(k, slice(max(16 * k, o.start), o.stop)) for k in range(o.stop // 16)]
+        if SPLIT and o.start < own.start and o.start == parts[-1].start:
+            late = range(o.start // 16, own.start // 16)
+            todo = ([(k, slice(max(16 * k, own.start), o.stop)) for k, u in todo if k not in late] + [(k, parts[-1]) for k in range(late[0])] + [todo[k] for k in late])
+        last, fresh = parts[-1], ps("line", parts[-1])
+
+        def row(u):
+            if last.start <= u.start and u.stop <= last.stop:
+                return X(fresh["name"], slice(fresh["lo"] + u.start - last.start, fresh["lo"] + u.stop - last.start)), c("ncor0")
+            return X("pR", u), c("ncor")
+        batches(twins(X(twin["name"], slice(u.start - o.start, u.stop - o.start)), k, u, row(u)[0], X("SP", 16 * k + 15), OP.subtract,
+                      row(u)[1], OP.is_equal, X("WH", slice(128 * k, 128 * k + 128)), False, (k, u) == todo[-1]) for k, u in todo)
         tt(X("OA", o), twin, X("PG", o), OP.is_lt)
-        scan(X("Cn", o), X("OA", o), X("STEP", o), X("Cn", 127) if h else c("icol"), OP.add, OP.subtract)
+        scan(X("Cn", o), X("OA", o), X("STEP", o), X("Cn", o.start - 1) if o.start else c("icol"), OP.add, OP.subtract)
         scan(X("Z", o), X("Cn", o), X("OA", o), 0.0, OP.min, OP.mult)
         acc(ps("slot", o), [("B4n", X("OA", o)), ("BLKh", X("Z", o))])
         scan(X("SS", o), X("GM", o), ps("slot", o), 0.0, OP.add, OP.max)
@@ -509,7 +602,7 @@ def rank_program(g, core, T, topo):
         act(X("u", o), left, AF.Relu, scale=-1.0, bias=VO)
         act(X("An", o), left, AF.Relu, bias=-VO)
         acc(base, [("NIh", X("xc", o)), ("WBm", X("PG", o))])
-        act(X("Xb", o), base, AF.Identity, scale=-1.0, bias=-VO)
+        act(X("Xb", o), base, AF.Identity, scale=-1.0, bias=5 * 2.0 ** 19 - VO)
         tt(by(X("XW", slice(1024 * s, 1024 * s + XWIN)), X("sL", w(o))), X("Xb", o), X("u", o), OP.add)
 
     def writes(s, o):
@@ -521,55 +614,68 @@ def rank_program(g, core, T, topo):
             return
         acc(X("k0", o), [("Ih", X("xo", o))] + draw)
         tt(X("vn", o), X("k0", o), X("xo", o), OP.max)
-        act(by(X("VT"), X("wU", w(o))), X("vn", o), AF.Silu)
+        if o.start and "VT" in ONV:
+            tc(by(X("VT"), X("wU", w(o))), X("vn", o))
+        else:
+            act(by(X("VT"), X("wU", w(o))), X("vn", o), AF.Silu)
 
-    def used(o):
-        ts(X("pWc", w(o)), X("pL", w(o)), c("pco"), OP.add)
-        ts(X("pWc", w(o, 16)), X("Wf", w(o)), c("corr"), OP.add)
-        for plus in (16, 0):
-            tt(X("pa", w(o, plus)), ends("SS", o), X("pWc", w(o, plus)), OP.max)
-            if o != ALL:
+    def used():
+        ts(X("pWc", w(ALL, 16)), X("Wf"), c("corr"), OP.add)
+        for table, plus in (("Q", 16), ("A", 0)):
+            for o in shares if table in WRITE2 else [ALL]:
+                if table == "A":
+                    ts(X("pWc", w(o)), X("pL", w(o)), c("pco"), OP.add)
+                tt(X("pa", w(o, plus)), ends("SS", o), X("pWc", w(o, plus)), OP.max)
                 ts(X("pU", w(o, plus)), X("pa", w(o, plus)), c("pco"), OP.subtract)
-        if o == ALL:
-            ts(X("pU"), X("pa"), c("pco"), OP.subtract)
-        act(by(X("Q"), X("pU", w(o, 16))), X("qn", o), AF.Silu)
-        tc(by(X("A"), X("pU", w(o))), X("An", o))
+                if table == "A":
+                    tc(by(X("A"), X("pU", w(o))), X("An", o))
+                else:
+                    act(by(X("Q"), X("pU", w(o, 16))), X("qn", o), AF.Silu)
 
     for s in range(STEPS):
-        early[0] = 0
-        for o in pieces:
-            head(s, o)
-        amounts(pieces[0])
-        amounts(pieces[1])
-        positions(s)
-        amounts(pieces[2])
-        amounts(pieces[3])
-        early[0] = EARLY[1]
+        stage[0] = None
+        if s:
+            for o in pieces[:2] + ([slice(pieces[2].start, pieces[3].stop)] if pieces[2].stop == pieces[3].start else pieces[2:]):
+                head(s, o)
+            amounts(s, pieces[0])
+            amounts(s, pieces[1])
+            positions(s)
+            amounts(s, pieces[2])
+            amounts(s, pieces[3])
+        else:
+            head(s, ALL)
+            amounts(s, helped)
+            amounts(s, HALF[0])
+            positions(s)
+            amounts(s, slice(helped.stop, 256))
+        stage[0] = "banks"
         banks()
-        early[0] = EARLY[0]
         if s == 0:
-            ts(X("Q", slice(0, B)), X("Qin", slice(0, B)), float(LO), OP.add)
-            act(X("VT", slice(0, B)), X("V", slice(0, B)), AF.Identity, bias=VO)
+            for o in [slice(at, at + 256) for at in range(0, B, 256)]:
+                ts(X("Q", o), X("Qin", o), float(LO), OP.add)
+                act(X("VT", o), X("V", o), AF.Identity, bias=VO)
         if s == STEPS - 1:
             act(X("Vr"), X("VT", slice(0, B)), AF.Identity, bias=MAGIC)
             act(X("V", slice(0, B)), X("Vr"), AF.Identity, bias=-MAGIC - VO)
-        early[0] = 0
-        for o in parts:
+        for o in parts if s else [HALF[0], helped, slice(192, 256)][::1]:
+            stage[0] = "lines%d" % o.start
             lines(s, o)
-        for h in range(2):
-            draws(s, h)
+        for o in shares:
+            stage[0] = "draws%d" % o.start
+            draws(s, o)
+        stage[0] = None
         exchange(s)
-        for o in HALF if WRITE2 else [ALL]:
-            if s < STEPS - 1:
-                used(o)
-        for o in HALF:
+        if s < STEPS - 1:
+            used()
+        for o in shares:
             writes(s, o)
     dma("y", T.yv[:], X("V", slice(0, B)), 1 << 18)
     L = X("L%d" % STEPS)
     ts(X("k0", ALL), L, 512 * MAGIC, OP.add, 512 * MAGIC, OP.subtract)
     tt(X("cb"), X("k0", ALL), L, OP.subtract)
     dma("y", T.yc[:], X("cb"), 1 << 16)
-    act(X("yw32"), X("k0", ALL), AF.Identity, scale=-1 / 512, bias=-float(B))
+    act(X("u"), L, AF.Identity, scale=-1 / 512, bias=MAGIC)
+    act(X("yw32"), X("u"), AF.Identity, bias=-MAGIC - B)
     dma("s", T.yw[:], X("yw32", rows=slice(0, 128, 16)), 8192)
 
     semof = {"v": "sv", "s": "ss", "t": "st", "g": "sg"}
@@ -582,7 +688,7 @@ def rank_program(g, core, T, topo):
             for s2, v2 in list(seen.get((sem, val), {}).items()) + [(sem, val)]:
                 know[e][s2] = max(know[e].get(s2, 0), v2)
 
-    for i in issue_order(calls):
+    for i in issue_order(calls, TRIES // (1 + 2 * (q < 2))):
         call = calls[i]
         e, need = call["queue"], {}
         marks = [calls[j]["sem"][0:2] if wrote else calls[j]["sem"][2:4] for j, wrote in call["needs"].items() if waits(calls[j], call, wrote)]

from concourse.bass import DstId, RemoteDMATransfer
from concourse.mybir import AluOpType as OP, ActivationFunctionType as AF, AxisListType as AX

STEPS, B = 4, 1024
LO = 32
NONE = LO + 8191
VO = 1600.0
QW, VW, AW, XWIN = B + 16, 1536, LO + 8464, LO + 9488
EMPTY = 512 * (B + 1024)
LIFT = 2.0 ** 20
RHO, TOP = 1.75, 2.0 ** 88
KILL = 2.0 ** 92
MAGIC = 1.5 * 2.0 ** 23
GS, GB, FS, FB = 0.004397, 11.6005, 0.004395, 10.533
BATCH = 2
FILL = (2048, 4096)
CYC, PCYC, GATHER, SCATTER, HOP, DMA, RATE, REMOTE, FIRST = 0.83, 0.42, 1.35, 3.8, 260, 900, 400, 800, 1700
SFIX = 75
TURNS = 2
THREE, WRITE2, CUT, SPLIT, ONV = True, "AQ", False, False, ("D1", "D2", "VT")
PAIR, JOIN, FOUR, BFIRST, HELP, MERGE = 1, True, False, 1, True, 128
GFILL, SLOW = 2048, 1.5
ONS, WHS = ("If", "BLKf", "N512", "NIb"), 12
TRIES, SEED, SHIFTS, SLACK = 2100, 1, (1, 1, 100, 300, 600, 1200), (0, 10, 20)
HOOK = []
SCRATCH = {}


def _buf(dtype, n, names, parts=128):
    for b in names.split():
        SCRATCH[b] = ("sbuf", [parts, n], dtype)


_buf("bfloat16", VW, "V")
_buf("float32", VW, "VT")
_buf("float32", AW, "Q")
_buf("float32", B, "Vr")
_buf("int32", B + 16, "Qin")
_buf("bfloat16", AW, "A")
_buf("bfloat16", LO + 8192, "PT")
_buf("float32", 1024 * (STEPS - 1) + XWIN, "XW")
_buf("int32", 512, "payS")
_buf("float32", 512, "payF")
_buf("float16", 512, "payR payH")
_buf("bfloat16", 3072, "payB")
_buf("bfloat16", 1024, "ONE")
_buf("int32", 256, "wkI", 8)
_buf("float16", 256, "wkH", 8)
_buf("float16", 128, "sel8", 8)
_buf("float32", 128, "imp qg BLKf If")
_buf("float32", 144, "ebi")
_buf("float16", 144, "EB")
_buf("float32", 256, "SC SD SP SS qn vn Vg yw32 FALL Xb u")
_buf("float32", 512, "nF np")
_buf("int32", 8, "pc pj pg")
_buf("float32", 64, "cf")
_buf("float32", 16, "l16 LC Wf wa E16 EQ LT")
_buf("float32", 32, "pWc pa")
_buf("uint16", 16, "WL wU pL sL")
_buf("uint16", 32, "pU")
_buf("float16", 128, "N512 BLKh BLK1 Ih NIh")
_buf("bfloat16", 128, "u1 Ib NIb N32 BLKb B256 B4a B4n I4k WBm WT W4 TRI MONE")
_buf("bfloat16", 2048, "WH")
_buf("bfloat16", 256, "tt GM STEP ZERO thr x D1 D2 e PG Ap An tp OA cb")
_buf("float16", 256, "Z Cn bR y xc xo F")
_buf("float16", 512, "F2")
_buf("uint16", 256, "nU pR")
_buf("bfloat16", 4096, "eq")
_buf("float16", 4096, "G cmp")
for _s in range(STEPS + 1):
    _buf("float32", 256, "L%d" % _s)
for _s in range(8):
    SCRATCH["k%d" % _s] = ("psum", [128, 512], "float32")
SEMAPHORES = ["sv", "ss", "st", "sg", "lx"] + ["rx%d" % s for s in range(STEPS)] + ["d%d" % k for k in range(24)]


def split_engines(topo, cores, src):
    dst = [c for c in cores if c != src]
    off = [c for c in dst if topo.chip(c) != topo.chip(src)]
    on = [c for c in dst if topo.chip(c) == topo.chip(src)]
    out, used = {}, []
    for group in (off, on):
        if not group:
            continue
        free = [e for e in topo.engines(src, group[0]) if e not in used]
        n = 1
        while 2 * n * len(group) <= len(free):
            n *= 2
        for k, c in enumerate(group):
            out[c] = free[k * n:(k + 1) * n]
            used = used + out[c]
    return out


def issue_order(calls, tries):
    n = len(calls)
    facts = [(c["queue"], int(c["time"]), c["banks"]) for c in calls]
    places = {c["queue"] for c in calls} | {bank for c in calls for bank in c["banks"]}
    before, behind = [[] for c in calls], [[] for c in calls]
    for i, c in enumerate(calls):
        for j, wrote in c["needs"].items():
            gap = calls[j]["late"] + HOP if waits(calls[j], c, wrote) else 0
            before[i].append((j, gap))
    gaps = [dict(b) for b in before]
    for i in range(n):
        before[i] = [(j, gap) for j, gap in before[i] if not any(j in gaps[k] and gaps[k][j] + facts[k][1] + via >= gap for k, via in gaps[i].items())]
        for j, gap in before[i]:
            behind[j].append((i, gap))

    def place(order, needs):
        taken = {r: [[] for u in range(400)] for r in places}
        start, end = [0] * n, [0] * n
        for i in order:
            e, time, banks = facts[i]
            t, was = HOP, -1
            for j, gap in needs[i]:
                if end[j] + gap > t:
                    t = end[j] + gap
            while t > was:
                was = t
                for u in range(t >> 9, (t + time >> 9) + 1):
                    for a, b in taken[e][u]:
                        if b > t and a < t + time:
                            t = b
                    for bank in banks:
                        for a, b, who in taken[bank][u]:
                            if b > t and a < t + time and who != e:
                                t = b
            start[i], end[i] = t, t + time
            for u in range(t >> 9, (t + time >> 9) + 1):
                taken[e][u].append((t, t + time))
            for bank in banks:
                for u in range(t - HOP >> 9, (t + time + HOP >> 9) + 1):
                    taken[bank][u].append((t - HOP, t + time + HOP, e))
        return start, end

    done, way = [False] * n, [0.0] * n

    def longest(i):
        if not done[i]:
            way[i], done[i] = calls[i]["time"] + max([calls[i]["late"]] + [gap + longest(j) for j, gap in behind[i]]), True
        return way[i]
    for i in range(n - 1, -1, -1):
        longest(i)
    start, end = place(sorted(range(n), key=lambda i: (-way[i], i)), before)
    best = (max(end), start)
    for turn in range(TURNS):
        start, end = place(sorted(range(n), key=lambda i: (-end[i], -i)), behind)
        start, end = place(sorted(range(n), key=lambda i: (-end[i], i)), before)
        best = min(best, (max(end), start))
    if HOOK:
        return HOOK[0](calls, place, before, behind, way, best)
    draw = [SEED]

    def pick(among):
        draw[0] = (draw[0] * 1103515245 + 12345) % 2 ** 31
        return among[(draw[0] >> 8) % len(among)]


    def held(start):
        end = [start[i] + facts[i][1] for i in range(n)]
        left = {(facts[i][0], end[i]): i for i in range(n)}
        left.update({(bank, end[i] + HOP): i for i in range(n) for bank in facts[i][2]})
        i, pairs = end.index(max(end)), []
        while True:
            needed = [j for j, gap in before[i] if end[j] + gap == start[i]]
            holders = [left[r, start[i]] for r in [facts[i][0]] + facts[i][2] if (r, start[i]) in left]
            if not needed and not holders:
                return pairs
            if not needed:
                pairs.append((i, holders[0]))
            i = pick(needed) if needed else holders[0]
    kinds = [[c[name] for c in calls] for name in ("kind", "sort")]
    now, pairs = best, held(best[1])
    for turn in range(tries):
        i, j = pick(pairs) if pairs and turn % 5 else (pick(range(n)), pick(range(n)))
        past = abs(now[1][i] - now[1][j]) if turn % 5 else 0
        moved, shift = pick([(i, -past - pick(SHIFTS)), (j, past + pick(SHIFTS)), (j, -3 * pick(SHIFTS))])
        kind = pick(kinds)
        key = [t + shift if u == kind[moved] else t for t, u in zip(now[1], kind)]
        for i in range(n) if shift > 0 else range(n - 1, -1, -1):
            for j, gap in before[i] if shift > 0 else behind[i]:
                if (key[j] >= key[i]) == (shift > 0) or key[j] == key[i]:
                    key[i] = key[j] + (0.001 if shift > 0 else -0.001)
        start, end = place(sorted(range(n), key=lambda i: (key[i], i)), before)
        if max(end) <= now[0] + pick(SLACK):
            now, pairs = (max(end), start), held(start)
            best = min(best, now)
    return sorted(range(n), key=lambda i: (best[1][i], i))


def waits(a, b, wrote):
    return wrote is not None and not a["queue"] == b["queue"] == "t"


def rank_program(g, core, T, topo):
    q = T.rank_of(core)
    if q is None:
        return
    cores = list(T.cores)
    queue = {"v": g.vector, "s": g.scalar, "t": g.tensor, "g": g, "y": g.sync}
    calls, uses, group, stage = [], {}, {}, [None]

    def X(name, cols=None, rows=None):
        where, shape, dtype = SCRATCH[name]
        cols = slice(0, shape[1]) if cols is None else slice(cols, cols + 1) if isinstance(cols, int) else cols
        r = range(shape[1])[cols]
        return {"ap": T[name][rows or slice(0, shape[0]), cols], "name": name, "lo": r[0], "hi": r[-1] + 1, "n": len(r), "rows": rows,
                "wide": dtype in ("float32", "int32"), "psum": where == "psum", "by": None}

    def by(win, off):
        return dict(win, ap=win["ap"].indirect(off["ap"]), n=16 * off["n"], by=off)

    def record(e, issue, time, R, W, late=0, sem=None):
        needs = {}
        for x, writes in [(x, False) for x in R] + [(x, True) for x in W]:
            for y, wrote, j in uses.get(x["name"], []):
                apart = x["rows"] and y["rows"] and x["rows"].step and x["rows"] != y["rows"]
                if (writes or wrote) and x["lo"] < y["hi"] and y["lo"] < x["hi"] and not apart:
                    needs[j] = needs.get(j, False) or wrote
        for x, writes in [(x, False) for x in R] + [(x, True) for x in W]:
            keep = [u for u in uses.get(x["name"], []) if not (writes and not x["rows"] and x["lo"] <= u[0]["lo"] and u[0]["hi"] <= x["hi"])]
            uses[x["name"]] = keep + [(x, writes, len(calls))]
        calls.append({"queue": e, "issue": issue, "time": time, "late": late, "needs": needs, "sem": sem, "kind": (e, W[0]["name"], W[0]["lo"], R[0]["name"] if R else "") if W else e,
                      "sort": (e, W[0]["name"], stage[0] or W[0]["lo"], R[0]["name"] if R else "") if W else e,
                      "banks": sorted({x["name"] for x in R + W if x["psum"]})})

    def op(e, name, out, *a, after=(), **k):
        R = [x for x in list(a) + list(k.values()) if isinstance(x, dict)]
        sides = [x for x in [out] + R if x["n"] > 1 or x is out]
        R += [x["by"] for x in [out] + R if x["by"]] + list(after)
        n = max(x["n"] for x in sides)
        if name == "matmul":
            time = 20 + PCYC * max(64, out["n"]) * (4 if a[0]["wide"] else 1)
        elif e == "g":
            time = 150 + 2 * CYC * n
        elif any(x["by"] for x in sides):
            time = (SFIX if e == "s" else 30) + CYC * n * (SCATTER if out["by"] else GATHER)
        elif e == "s":
            time = SFIX + CYC * n
        else:
            per = (1 if a[0]["psum"] or a[1]["psum"] else 2) if name == "tensor_tensor" else 1 if any(x["wide"] for x in sides) else 0.5
            time = 10 + CYC * max(64, n * per)
        args = [x["ap"] if isinstance(x, dict) else x for x in (out,) + a]
        keys = {u: x["ap"] if isinstance(x, dict) else x for u, x in k.items()}
        eng = queue[e]
        issue = {"tensor_copy": lambda: eng.tensor_copy(*args), "tensor_tensor": lambda: eng.tensor_tensor(*args), "tensor_scalar": lambda: eng.tensor_scalar(*args),
                 "scan": lambda: eng.tensor_tensor_scan(*args), "memset": lambda: eng.memset(*args), "reciprocal": lambda: eng.reciprocal(*args), "reduce": lambda: eng.tensor_reduce(*args),
                 "activation": lambda: eng.activation(*args, **keys), "matmul": lambda: eng.matmul(*args),
                 "iota": lambda: eng.iota(*args, **keys), "select": lambda: eng.affine_select(*args)}[name]
        record(e, issue, time, R, [out])
        if name == "matmul":
            if out["name"] in group:
                calls[-1]["needs"].setdefault(group[out["name"]], False)
            group[out["name"]] = len(calls) - 1

    ndma = [0]

    def dma(e, out, in_, size, after=()):
        sem = "d%d" % ndma[0]
        ndma[0] += 1
        o, i = [x["ap"] if isinstance(x, dict) else x for x in (out, in_)]
        record(e, lambda: queue[e].dma_start(o, i).then_inc(T.sem[sem], 16), 50 if e == "s" else size / RATE,
               [x for x in [in_] if isinstance(x, dict)] + list(after), [x for x in [out] if isinstance(x, dict)], DMA, (sem, 16, sem, 16))

    line = {}

    def in_line(name):
        if name in line:
            calls[-1]["needs"].setdefault(line[name], None)
        line[name] = len(calls) - 1

    def tc(*a):
        op("v", "tensor_copy", *a)

    def tt(*a):
        op("v", "tensor_tensor", *a)

    def ts(out, in_, s1, op0, s2=None, op1=None):
        op("v", "tensor_scalar", out, in_, s1, s2, *([op0, op1] if op1 else [op0]))

    def scan(*a):
        op("v", "scan", *a)

    def act(out, in_, func=AF.Copy, **k):
        op("s", "activation", out, in_, func, **k)

    def mm(out, lhsT, rhs, start=True, stop=True, after=()):
        op("t", "matmul", out, lhsT, rhs, start, stop, after=after)

    def acc(out, terms):
        for k, (m, rhs) in enumerate(terms):
            mm(out, X(m), rhs, k == 0, k == len(terms) - 1)

    def iota(out, pattern, base, cm=0):
        op("g", "iota", out, pattern, base, cm, allow_small_or_imprecise_dtypes=True)

    def select(name, *a):
        op("g", "select", X(name), X(name), *a)

    def memset(out, val):
        op("v", "memset", out, val)

    dma("y", X("wkI"), T.wk[:], 8192)
    dma("y", X("payS"), T.pay[:], 1 << 18)
    dma("y", X("Qin", slice(0, B)), T.qu[:], 1 << 19)
    dma("y", X("A", slice(LO, LO + 8192)), T.am[:], 1 << 21)
    dma("y", X("V", slice(0, B)), T.vp[:], 1 << 18)
    for k in range(1, 5):
        calls[k]["needs"][k - 1] = None

    iota(X("pc", 0), [[1, 1]], 0, 1)
    iota(X("qg"), [[1, 8], [0, 16]], 0)
    iota(X("imp"), [[1, 128]], 0, -1)
    iota(X("tt"), [[0, 16], [1, 16]], 0)
    iota(X("l16"), [[16, 16]], 1280)
    iota(X("ebi"), [[1, 144]], -15)
    iota(X("A", slice(LO + 8192, AW)), [[0, AW - LO - 8192]], 0)
    iota(X("V", slice(B, B + 16)), [[0, 16]], 0)
    for at in range(0, 1024 * STEPS, 256):
        iota(X("XW", slice(at, at + 64)), [[0, 64]], -EMPTY)
    col = {}

    def c(name):
        return X("cf", col[name])

    def column(name, *a):
        col[name] = len(col)
        ts(c(name), *a)

    def byrow(name, start, terms):
        for n, (is_, k, value) in enumerate(terms):
            column(name if n == len(terms) - 1 else (name, n), X(is_, k), float(value), OP.mult, c((name, n - 1)) if n else start, OP.add)

    for name, a, b, value in (("A", 0, LO, 0), ("Qin", B, QW, 8191), ("Q", B, QW, NONE), ("VT", B, QW, int(VO))):
        iota(X(name, slice(a, b)), [[0, b - a]], value)
    for name, n, value in (("FALL", 256, 1 / RHO), ("ZERO", 256, 0.0), ("MONE", 128, -1.0), ("ONE", (8192 - GFILL) // 8, 1.0)):
        memset(X(name, slice(0, n)), value)
    memset(X("u1"), 1 / 32)
    select("u1", [[1, 128]], OP.is_ge, 1.1, 0, -1)
    select("u1", [[1, 128]], OP.not_equal, -1.0, 0, -1)
    select("u1", [[-16, 8], [0, 16]], OP.is_ge, 0.0, 0, 1)
    select("u1", [[16, 8], [0, 16]], OP.is_ge, 0.0, 15, -1)
    ts(X("TRI"), X("u1"), 2.0 ** 58, OP.mult, 2.0 ** 58, OP.mult)
    iota(X("nF"), [[0, 512]], 0)
    for bank in ("k3", "k4"):
        memset(X(bank, slice(128, 384)), 0.0)
    scan(X("thr"), X("FALL"), X("ZERO"), 2.54 * RHO * TOP, OP.mult, OP.add)
    ts(X("pj", 0), X("pc", 0), 15, OP.bitwise_and)
    ts(X("pg", 0), X("pc", 0), 4, OP.arith_shift_right)
    for name, src in (("jf", "pj"), ("gf", "pg"), ("pf", "pc")):
        column(name, X(src, 0), 0.0, OP.add)
    column("jh", c("jf"), 0.5, OP.add)
    for name, plus in (("corr", 0.0), ("cor2", -512.0 * B), ("pco", 1024.0), ("cor3", 1024.0 if "D1" in ONV else -3072.0), ("cor4", 0.0 if "D2" in ONV else -4096.0)):
        column(name, c("jf"), -LIFT, OP.mult, 15 * LIFT + plus, OP.add)
    column("ncor", c("jf"), LIFT, OP.mult, (0.0 if "D2" in ONV else 4096.0) - 15 * LIFT, OP.add)
    column("ncor0", c("jf"), LIFT, OP.mult, -15 * LIFT, OP.add)
    column("g16", c("gf"), 16.0, OP.mult)
    ts(X("EQ"), X("tt", slice(0, 16)), c("jf"), OP.is_equal)
    ts(X("LT"), X("tt", slice(0, 16)), c("jf"), OP.is_gt)
    column("j256", c("jf"), 256.0, OP.mult, -1040.0 - LO - 4096, OP.add)
    column("jr", c("jf"), -2.0 ** 19 / KILL, OP.mult, X("LT", 4), OP.mult)
    byrow("jw", c("jr"), [("EQ", 8, 512 * 32), ("EQ", 9, 512)])
    byrow("icol", c("j256"), [("EQ", 4, -1023), ("EQ", 5, 1040 + LO - 1280 - 8192), ("LT", 6, 4096)])
    byrow("ja", 0.0, [("LT", 4, 512), ("EQ", 5, -512)])
    byrow("jz", 0.0, [("LT", 4, 2), ("LT", 6, -1)])
    ts(X("GM"), X("tt"), c("jh"), OP.subtract, 64 * LIFT, OP.mult)
    ts(X("GM"), X("GM"), LIFT, OP.min)
    ts(X("BLKb"), X("qg"), c("gf"), OP.is_equal)
    ts(X("Ib"), X("imp"), 0.0, OP.is_equal)
    ts(X("EB"), X("ebi"), c("g16"), OP.is_equal, 2.0 ** 15, OP.mult)
    ts(X("STEP"), X("ZERO"), X("EQ", 4), OP.add, 1.0, OP.add)
    ts(X("LC"), X("l16"), c("jf"), OP.add, c("cor3"), OP.add)
    tt(X("E16"), X("EQ"), X("thr", slice(0, 16)), OP.mult)
    col["wj"] = len(col)
    op("v", "reduce", c("wj"), X("E16"), AX.X, OP.max)
    ts(X("WT"), X("BLKb"), c("wj"), OP.mult, 1 / (2.54 * TOP), OP.mult)
    for name, src, times in (("N512", "Ib", -512.0), ("If", "Ib", 1.0), ("NIb", "Ib", -1.0), ("N32", "Ib", -32.0), ("Ih", "Ib", 1.0), ("NIh", "Ib", -1.0),
                             ("I4k", "Ib", 4096.0), ("B256", "BLKb", 256.0), ("BLKf", "BLKb", 1.0), ("BLK1", "BLKb", 1.0), ("WBm", "BLKb", c("jw")),
                             ("B4a", "BLKb", c("ja")), ("BLKh", "BLKb", c("jz"))):
        if name in ONS:
            act(X(name), X(src), AF.Identity, scale=times)
        else:
            ts(X(name), X(src), times, OP.mult)
    ts(X("B4n"), X("BLKb"), X("LT", 4), OP.mult, -8192.0, OP.mult)
    op("g", "select", X("W4"), X("WT"), [[0, 8], [-1, 16]], OP.is_ge, 0.0, 3, 0)
    for h in range(16):
        if h < WHS:
            act(X("WH", slice(128 * h, 128 * h + 128)), X("W4"), scale=TOP * RHO ** (-16 * h))
        else:
            ts(X("WH", slice(128 * h, 128 * h + 128)), X("W4"), TOP * RHO ** (-16 * h), OP.mult)

    rows8 = slice(0, 8)
    ts(X("sel8"), X("qg", rows=rows8), X("cf", col["pf"], rows8), OP.is_equal, -512.0, OP.mult)
    ts(X("wkH"), X("wkI"), float(B), OP.add)
    mm(X("k0", slice(0, 256)), X("sel8"), X("wkH"))
    tc(X("L0"), X("k0", slice(0, 256)))

    act(X("PT", slice(0, LO)), X("FALL", slice(0, LO)), AF.Silu)
    calls[-1]["time"] += 1300
    in_line("amounts")
    tc(X("payF"), X("payS"))
    act(X("payR"), X("payF"), AF.Identity, scale=1 / 1024, bias=1025 - 0.4995)
    act(X("payH"), X("payF"), AF.Identity, scale=1 / 32, bias=1025 - 15.5 / 32)
    ts(X("payR", 511), X("payR", 511), X("LT", 15), OP.mult)
    part = [X("payB", slice(512 * k, 512 * k + 512)) for k in range(6)]
    for r in range(4):
        ts(part[r], X("payR"), 1025.0 + r, OP.not_equal, -KILL, OP.mult)
    ts(part[4], X("payH"), 1025.0, OP.subtract)
    acc(X("k7"), [("If", X("payF")), ("N32", part[4])])
    act(part[5], X("k7"))
    in_line("amounts")
    if GFILL:
        iota(X("PT", slice(LO, LO + GFILL)), [[0, GFILL]], 1)
    for j, step in ((4, 8), (5, 8), (6, 8), (7, 8), (10, 16), (11, 16)):
        dma("y", X("PT", slice(LO + GFILL, LO + 8192), slice(j, 128, step)), X("ONE", slice(0, (8192 - GFILL) // 8), slice(0, 1024 // step)),
            (8192 - GFILL) * 256 // step * SLOW, after=[X("V", slice(0, B))])
    for k, j in enumerate((0, 1, 2, 3, 8, 9)):
        dma("y", X("PT", slice(LO, LO + 8192), slice(j, 128, 16)), part[k], (1 << 17) * SLOW, after=[X("V", slice(0, B))])

    route = split_engines(topo, cores, core)
    arrive = sum(len(split_engines(topo, cores, s)[core]) for s in cores if s != core)
    leave = sum(len(e) for e in route.values())

    def exchange(s):
        land, tr = "L%d" % (s + 1), []
        slots = [X("XW", slice(1024 * s + r * 256, 1024 * s + r * 256 + 64)) for r in range(4)]
        for r, d in enumerate(cores):
            if d != core:
                tr.append(RemoteDMATransfer(dst_ids=[DstId(rid=topo.addr(d)[0], pnc=topo.addr(d)[1])], dma_engine_mask=sum(1 << e for e in route[d]),
                                            remote_sem=T.sem["rx%d" % s], src=slots[r]["ap"], dst=T[land][:, q * 64:q * 64 + 64]))
        record("g", lambda: g.remote_dma_fused(tr, local_sem=T.sem.lx), 100, [x for r, x in enumerate(slots) if r != q],
               [X(land, slice(64 * r, 64 * r + 64)) for r in range(4) if r != q], REMOTE + FIRST * (s == 0), ("rx%d" % s, arrive, "lx", leave * (s + 1)))
        tc(X(land, slice(64 * q, 64 * q + 64)), slots[q])

    def w(o, plus=0):
        return slice(plus + o.start // 16, plus + o.stop // 16)

    def ends(name, o):
        return X(name, slice(o.start + 15, o.stop, 16))

    def ps(name, o):
        if name in ("twin", "slot"):
            bank, at = 5 + o.start // 128, {"twin": 0, "slot": 256}[name]
        elif FOUR:
            bank, at = (7, 3, 4, 7)[parts.index(o)], {"score": 0, "won": 64, "best": 128, "line": 192}[name] + 256 * (o == parts[3])
        else:
            bank, at = {0: 3, 128: 4, 192: 7}[o.start], {"score": 0, "won": 128, "best": 0, "line": 384}[name]
        return X("k%d" % bank, slice(at, at + o.stop - o.start))

    ALL, HALF = slice(0, 256), [slice(0, 128), slice(128, 256)]
    own = slice(64 * q, 64 * q + 64)
    pieces = [own] + [slice(64 * r, 64 * r + 64) for r in range(4) if r != q]
    parts = [HALF[0], slice(128, 192), slice(192, 256)] if THREE else HALF
    parts = pieces if FOUR else sorted(parts, key=lambda o: o != own)
    helped = slice(128, 192)
    cut = parts[-1].start if CUT else 128
    shares = [slice(0, cut), slice(cut, 256)]

    def twins(out, h, o, row, s1, op0, s2, op1, matrix, start, stop):
        eq = X("eq", slice(256 * h + o.start, 256 * h + o.stop))
        ts(eq, row, s1, op0, s2, op1)
        in_line("twins")
        return lambda after: mm(out, matrix, eq, start, stop, after), eq

    def batches(pairs):
        pairs = list(pairs)
        for k, (add, made) in enumerate(pairs):
            add([m for a_, m in pairs[k - k % BATCH:k - k % BATCH + BATCH]])

    def head(s, o):
        words = X("XW", slice(1024 * (s - 1) + 256 * q, 1024 * (s - 1) + 256 * q + 64)) if s and o == own else X("L%d" % s, o)
        scan(X("SC", o), X("GM", o), words, 0.0, OP.add, OP.max)
        in_line("banks")
        ts(X("WL", w(o)), ends("SC", o), c("cor2"), OP.subtract, -1 / 512, OP.mult)
        in_line("lists")
        if s:
            ts(X("nU", o), by(X("Q", slice(0, QW)), X("WL", w(o))), 0.25, OP.add)
        else:
            ts(X("nU", o), by(X("Qin"), X("WL", w(o))), float(LO), OP.add)
        in_line("rows")

    def amounts(s, o):
        if s == 0 and o == helped and HELP:
            ts(X("G", slice(16 * o.start, 16 * o.stop)), by(X("A"), X("nU", o)), 130.0, OP.add, -2.0 ** -21, OP.mult)
            in_line("help")
            return
        act(X("G", slice(16 * o.start, 16 * o.stop)), by(X("A"), X("nU", o)), AF.Silu, scale=GS, bias=-GB)
        in_line("amounts")

    def positions(s):
        L = X("L%d" % s)
        ts(X("bR"), L, -1 / 512, OP.mult)
        if s:
            acc(X("k0", ALL), [("N512", X("bR"))])
            tt(X("Vg"), by(X("VT", slice(0, QW)), X("WL")), L, OP.add)
            tt(X("y"), X("Vg"), X("k0", ALL), OP.subtract)
        else:
            ts(X("y"), by(X("V", slice(0, QW)), X("WL")), VO, OP.add)
            in_line("help")
        ts(X("xc"), X("y"), VO - 255, OP.max, VO, OP.min)
        act(X("F"), X("xc"), AF.Silu, scale=FS, bias=-FB - FS * VO)
        in_line("amounts")
        if s == 0 and HELP:
            ts(X("Vg", helped), X("xc", helped), VO + 129.5, OP.subtract, 16.0, OP.mult)
            op("v", "reciprocal", X("vn", helped), X("Vg", helped))
            calls[-1]["time"] = 190 + 6 * 64 * CYC
        for o, src in [(helped, "vn"), (slice(192, 256), "F")] if s == 0 and HELP else [(HALF[1], "F")]:
            for u in range(2):
                tc(X("F2", slice(2 * o.start + u, 2 * o.stop, 2)), X(src, o))
        if s == STEPS - 1:
            ts(X("x"), X("y"), VO, OP.subtract, -255.0, OP.max)
        else:
            ts(X("xo"), X("y"), VO - 255, OP.max)

    def banks():
        ts(X("Wf"), X("WL"), float(B), OP.add)
        mm(X("k2", ALL), X("MONE", rows=slice(0, 1)), X("thr", rows=slice(0, 1)), True, False)
        batches(twins(X("k2", slice(16 * h, 256)), h, slice(16 * h, 256), X("bR", slice(16 * h, 256)), X("Wf", h), OP.is_equal, TOP * RHO ** (-16 * h), OP.mult,
                      X("WT"), False, h == 15) for h in range(16))
        if BFIRST:
            line["rows"] = line["twins"]
        if "D1" in ONV:
            ts(X("D1"), X("k2", ALL), 0.0, OP.is_gt, 2.0, OP.mult)
        else:
            act(X("D1"), X("k2", ALL), AF.Sign)
        one = 0.0 if "D1" in ONV else 4096.0
        acc(X("k0", slice(256, 512)), [("BLK1", X("xc")), ("B256", X("D1"))])
        if "D2" in ONV:
            ts(X("D2"), X("k0", slice(256, 512)), 16 * VO - one - 0.5, OP.is_gt, 2.0, OP.mult)
        else:
            act(X("D2"), X("k0", slice(256, 512)), AF.Sign, bias=one + 0.5 - 16 * VO)
        acc(X("k2", slice(256, 512)), [("Ih", X("bR")), ("I4k", X("D1"))])
        scan(X("SD"), X("GM"), X("k2", slice(256, 512)), 0.0, OP.add, OP.max)
        tt(X("wa"), ends("SD", ALL), X("LC"), OP.min)
        ts(X("wU"), X("wa"), c("cor3"), OP.subtract)

    def compare(o, i):
        if PAIR and o.stop - o.start == 64:
            i = i // 2 + 8 * (i % 2)
            at = 512 * (i % 8) + 2 * o.start
            made, both = X("cmp", slice(at + i // 8, at + 128, 2)), X("cmp", slice(at, at + 128))
            if i < 8:
                scan(both, X("G", slice(16 * o.start + i, 16 * o.stop, 8)), X("F2", slice(2 * o.start, 2 * o.stop)), 0.0, OP.min, OP.mult)
                in_line("rows")
        else:
            made = both = X("cmp", slice(256 * i + o.start - 128 * PAIR * (i % 2), 256 * i + o.stop - 128 * PAIR * (i % 2)))
            scan(made, X("G", slice(16 * o.start + i, 16 * o.stop, 16)), X("F", o), 0.0, OP.min, OP.mult)
            in_line("rows")
        return lambda after: mm(ps("score", o), X("EB", slice(15 - i, 143 - i)), made, i == 0, i == 15, after), both

    def lines(s, o):
        both, even = slice(2 * o.start, 2 * o.stop), slice(2 * o.start, 2 * o.stop, 2)
        won = ps("won", o)
        won, won2 = X(won["name"], slice(128, 128 + both.stop - both.start, 2)), X(won["name"], slice(128, 128 + both.stop - both.start))
        tc(X("nF", even), X("nU", o))
        batches(compare(o, i) for i in range(16))
        act(X("e", o), ps("score", o), AF.Silu, bias=-74.4, scale=3.9 * 512)
        acc(won, [("TRI", X("e", o))])
        mm(ps("line", o), X("B256"), X("D2", o), True, False)
        merge = o.stop - o.start <= MERGE
        if merge:
            scan(X("np", both), won2, X("nF", both), 0.0, OP.max, OP.min)
        else:
            ts(ps("best", o), won, 0.0, OP.is_gt, float(NONE), OP.mult)
            tt(X("np", even), ps("best", o), X("nF", even), OP.min)
        mm(ps("line", o), X("BLKf"), X("np", even), False, True)
        if o != parts[-1] or o != shares[-1]:
            ts(X("pR", o), ps("line", o), 0.0 if "D2" in ONV else 4096.0, OP.add)
        scan(X("SP", o), X("GM", o), ps("line", o), 0.0, OP.add, OP.max)
        ts(X("pL", w(o)), ends("SP", o), c("cor4"), OP.subtract, float(NONE), OP.min)
        act(X("PG", o), by(X("PT"), X("pL", w(o))))
        act(X("Ap", o), by(X("A"), X("pL", w(o))))
        if s < STEPS - 1:
            if merge:
                ts(ps("best", o), won, 0.0, OP.is_gt, float(NONE), OP.mult)
            tt(X("qn", o), ps("best", o), X("nF", even), OP.max)

    def draws(s, o):
        twin = ps("twin", o)
        mm(twin, X("MONE", rows=slice(0, 1)), X("thr", o, slice(0, 1)), True, False)
        todo = [(k, slice(max(16 * k, o.start), o.stop)) for k in range(o.stop // 16)]
        if SPLIT and o.start < own.start and o.start == parts[-1].start:
            late = range(o.start // 16, own.start // 16)
            todo = ([(k, slice(max(16 * k, own.start), o.stop)) for k, u in todo if k not in late] + [(k, parts[-1]) for k in range(late[0])] + [todo[k] for k in late])
        last, fresh = parts[-1], ps("line", parts[-1])

        def row(u):
            if last.start <= u.start and u.stop <= last.stop:
                return X(fresh["name"], slice(fresh["lo"] + u.start - last.start, fresh["lo"] + u.stop - last.start)), c("ncor0")
            return X("pR", u), c("ncor")
        batches(twins(X(twin["name"], slice(u.start - o.start, u.stop - o.start)), k, u, row(u)[0], X("SP", 16 * k + 15), OP.subtract,
                      row(u)[1], OP.is_equal, X("WH", slice(128 * k, 128 * k + 128)), False, (k, u) == todo[-1]) for k, u in todo)
        tt(X("OA", o), twin, X("PG", o), OP.is_lt)
        scan(X("Cn", o), X("OA", o), X("STEP", o), X("Cn", o.start - 1) if o.start else c("icol"), OP.add, OP.subtract)
        scan(X("Z", o), X("Cn", o), X("OA", o), 0.0, OP.min, OP.mult)
        acc(ps("slot", o), [("B4n", X("OA", o)), ("BLKh", X("Z", o))])
        scan(X("SS", o), X("GM", o), ps("slot", o), 0.0, OP.add, OP.max)
        ts(X("sL", w(o)), ends("SS", o), c("corr"), OP.subtract)
        left, base = X("k1", slice(256 + o.start, 256 + o.stop)), X("k1", o)
        acc(left, [("Ih", X("xc", o)), ("Ib", X("Ap", o))])
        act(X("u", o), left, AF.Relu, scale=-1.0, bias=VO)
        act(X("An", o), left, AF.Relu, bias=-VO)
        acc(base, [("NIh", X("xc", o)), ("WBm", X("PG", o))])
        act(X("Xb", o), base, AF.Identity, scale=-1.0, bias=5 * 2.0 ** 19 - VO)
        tt(by(X("XW", slice(1024 * s, 1024 * s + XWIN)), X("sL", w(o))), X("Xb", o), X("u", o), OP.add)

    def writes(s, o):
        draw = [("Ib", X("Ap", o)), ("NIb", X("An", o)), ("B4a", X("OA", o))]
        if s == STEPS - 1:
            acc(X("k0", o), draw)
            act(X("tp", o), X("k0", o), AF.Relu)
            tt(by(X("V"), X("wU", w(o))), X("x", o), X("tp", o), OP.add)
            return
        acc(X("k0", o), [("Ih", X("xo", o))] + draw)
        tt(X("vn", o), X("k0", o), X("xo", o), OP.max)
        if o.start and "VT" in ONV:
            tc(by(X("VT"), X("wU", w(o))), X("vn", o))
        else:
            act(by(X("VT"), X("wU", w(o))), X("vn", o), AF.Silu)

    def used():
        ts(X("pWc", w(ALL, 16)), X("Wf"), c("corr"), OP.add)
        for table, plus in (("Q", 16), ("A", 0)):
            for o in shares if table in WRITE2 else [ALL]:
                if table == "A":
                    ts(X("pWc", w(o)), X("pL", w(o)), c("pco"), OP.add)
                tt(X("pa", w(o, plus)), ends("SS", o), X("pWc", w(o, plus)), OP.max)
                ts(X("pU", w(o, plus)), X("pa", w(o, plus)), c("pco"), OP.subtract)
                if table == "A":
                    tc(by(X("A"), X("pU", w(o))), X("An", o))
                else:
                    act(by(X("Q"), X("pU", w(o, 16))), X("qn", o), AF.Silu)

    for s in range(STEPS):
        stage[0] = None
        if s:
            for o in pieces[:2] + ([slice(pieces[2].start, pieces[3].stop)] if pieces[2].stop == pieces[3].start else pieces[2:]):
                head(s, o)
            amounts(s, pieces[0])
            amounts(s, pieces[1])
            positions(s)
            amounts(s, pieces[2])
            amounts(s, pieces[3])
        else:
            head(s, ALL)
            amounts(s, helped)
            amounts(s, HALF[0])
            positions(s)
            amounts(s, slice(helped.stop, 256))
        stage[0] = "banks"
        banks()
        if s == 0:
            for o in [slice(at, at + 256) for at in range(0, B, 256)]:
                ts(X("Q", o), X("Qin", o), float(LO), OP.add)
                act(X("VT", o), X("V", o), AF.Identity, bias=VO)
        if s == STEPS - 1:
            act(X("Vr"), X("VT", slice(0, B)), AF.Identity, bias=MAGIC)
            act(X("V", slice(0, B)), X("Vr"), AF.Identity, bias=-MAGIC - VO)
        for o in parts if s else [HALF[0], helped, slice(192, 256)][::1]:
            stage[0] = "lines%d" % o.start
            lines(s, o)
        for o in shares:
            stage[0] = "draws%d" % o.start
            draws(s, o)
        stage[0] = None
        exchange(s)
        if s < STEPS - 1:
            used()
        for o in shares:
            writes(s, o)
    dma("y", T.yv[:], X("V", slice(0, B)), 1 << 18)
    L = X("L%d" % STEPS)
    ts(X("k0", ALL), L, 512 * MAGIC, OP.add, 512 * MAGIC, OP.subtract)
    tt(X("cb"), X("k0", ALL), L, OP.subtract)
    dma("y", T.yc[:], X("cb"), 1 << 16)
    act(X("u"), L, AF.Identity, scale=-1 / 512, bias=MAGIC)
    act(X("yw32"), X("u"), AF.Identity, bias=-MAGIC - B)
    dma("s", T.yw[:], X("yw32", rows=slice(0, 128, 16)), 8192)

    semof = {"v": "sv", "s": "ss", "t": "st", "g": "sg"}
    count = {e: 0 for e in semof}
    know, seen, user, total, program = {e: {} for e in queue}, {}, {}, {}, []

    def wait(e, sem, val):
        if know[e].get(sem, 0) < val:
            program.append((e, None, sem, val))
            for s2, v2 in list(seen.get((sem, val), {}).items()) + [(sem, val)]:
                know[e][s2] = max(know[e].get(s2, 0), v2)

    for i in issue_order(calls, TRIES // (1 + 2 * (q < 2))):
        call = calls[i]
        e, need = call["queue"], {}
        marks = [calls[j]["sem"][0:2] if wrote else calls[j]["sem"][2:4] for j, wrote in call["needs"].items() if waits(calls[j], call, wrote)]
        for sem, val in marks + [m for bank in call["banks"] for u, m in user.get(bank, {}).items() if u != e]:
            need[sem] = max(need.get(sem, 0), val)
        for sem in sorted(need):
            wait(e, sem, need[sem])
        if call["sem"] is None:
            count[e] += 1
            call["sem"] = (semof[e], count[e]) * 2
            program.append((e, call["issue"], semof[e], count[e]))
        else:
            program.append((e, call["issue"], None, 0))
        for sem, val in (call["sem"][0:2], call["sem"][2:4]):
            seen[(sem, val)] = {} if sem[0] == "r" else dict(know[e])
            total[sem] = val
        for bank in call["banks"]:
            user.setdefault(bank, {})[e] = call["sem"][0:2]
    for sem in sorted(total):
        wait("g", sem, total[sem])
    waited = {(sem, val) for e, issue, sem, val in program if issue is None}
    raised = {sem: 0 for sem in semof.values()}
    for e, issue, sem, val in program:
        if issue is None:
            queue[e].wait_ge(T.sem[sem], val)
        elif (sem, val) in waited:
            issue().then_inc(T.sem[sem], val - raised[sem])
            raised[sem] = val
        else:
            issue()
